import numpy as np, ml_dtypes
CORES = [25,29,65,69,153,157,193,197]
N = 8
BF = ml_dtypes.bfloat16
H, W, V, K, F, S, R, CAP = 2624, 2816, 512, 256, 2, 2, 3, 64
def start(q, ans):
    s = np.add.reduce(np.arange(1, 17)[:, None] * q, axis=-2) + ans
    return F * np.arange(K) + (s & (F - 1))
def parts(rng):
    return (rng.integers(0, 256, (N, 8, 16, H)), rng.integers(0, 256, (N, 8, 16, K)), rng.integers(0, H, (N, 8, 16, V)),
            np.ascontiguousarray(np.argsort(rng.random((N, 8, V)), axis=-1)), rng.integers(800, 961, (N, 8)))
def pack(x, q, p, mo, th):
    return {"x": np.ascontiguousarray(x).reshape(N, 128, H).astype(np.float32).astype(BF), "qs": np.ascontiguousarray(q).reshape(N, 128, K).astype(np.float32).astype(BF),
            "towns": np.ascontiguousarray(p).reshape(N, 128, V).astype(np.int32), "mo": np.ascontiguousarray(mo).astype(np.int32),
            "th": np.repeat(th, 16, axis=1).reshape(N, 128, 1).astype(np.int32)}
def mothers(rng, src, dst):
    m = np.zeros(V, np.int64); i = np.arange(V)
    m[src] = dst; m[np.setdiff1d(i, src)] = rng.permutation(np.setdiff1d(i, dst))
    return m
def setup_inputs(rng):
    return pack(*parts(rng))
def setup_inputs_room(rng):
    x, q, p, mo, th = parts(rng)
    x = rng.integers(0, 112, x.shape); th = rng.integers(1, 17, (N, 8))
    for a in range(N):
        for g in range(8):
            n = int(rng.choice(np.array([0, 1, CAP - 1, CAP, CAP + 1, K])))
            if a == 0: n = (CAP, CAP + 1, CAP - 1, 0, 1, K, CAP, K - 1)[g]
            hard = np.zeros(K, bool); hard[rng.permutation(K)[:n]] = True
            rec = rng.integers(0, H - K, K)
            w = np.where(hard, rng.integers(128, 256, (16, K)), x[a, g][:, rec]); w[0, hard] = 128 + 16 * a
            q[a, g] = w; u = start(w, 0)
            e = np.flatnonzero(~hard); p[a, g][rng.integers(0, 8, len(e)), u[e]] = rec[e]
            v = u
            for s in range(S): v = mo[a, g][v]
            b = np.flatnonzero(hard); b = b[rng.random(len(b)) < 0.5]; o = (a + 1) % N
            x[o, g][:, H - K + b] = w[:, b]; p[o, g][rng.integers(8, 16, len(b)), v[b]] = H - K + b
    return pack(x, q, p, mo, th)
def setup_inputs_ties(rng):
    x, q, p, mo, th = parts(rng); o = rng.permutation(8); i, e = o[:4], o[4:]
    x[:, i] = 64 * rng.integers(0, 4, (N, 4, 16, H)); q[:, i] = 64 * rng.integers(0, 4, (N, 4, 16, K))
    y = p[:, i]; y[:, :, 8:, 1::3] = y[:, :, :8, 1::3]; p[:, i] = y
    th[:, i] = rng.choice(np.array([768, 769, 832, 833, 896]), (N, 4))
    k = rng.integers(0, 3, (N, 4, 1, H)); y = np.where(k == 0, 0, np.where(k == 1, 255, x[:, e])); y[..., 0] = 255; x[:, e] = y
    k = rng.integers(0, 3, (N, 4, 1, K)); q[:, e] = np.where(k == 0, 0, np.where(k == 1, 255, q[:, e]))
    y = p[:, e]; y[..., ::5] = 0; p[:, e] = y
    th[:, e] = np.concatenate([rng.permutation(np.array([0, 1, 800, 900, 2000, 4080, 4081, 4096])) for a in range((N + 1) // 2)])[:4 * N].reshape(N, 4)
    return pack(x, q, p, mo, th)
def setup_inputs_alike(rng):
    x, q, p, mo, th = parts(rng)
    pool = rng.integers(0, H, (N, 8, 40)); pool[..., 0] = 0; pool[..., 1] = H - 1
    p = np.take_along_axis(pool, rng.integers(0, 40, (N, 8, 16 * V)), 2).reshape(N, 8, 16, V)
    q[:, :, :, 1::2] = q[:, :, :, 0::2]
    o = rng.permutation(8); i = np.arange(V)
    mo[:, o[0]] = i; mo[:, o[1]] = (i + 1) % V; mo[:, o[2]] = V - 1 - i
    return pack(x, q, p, mo, rng.integers(850, 1001, (N, 8)))
def setup_inputs_crowd(rng):
    x, q, p, mo, th = parts(rng)
    x = rng.integers(0, 96, x.shape); p = rng.integers(0, H - 2 * K, p.shape); th = rng.integers(400, 513, (N, 8))
    for a in range(0, N, 2):
        o = a + 1
        for g in range(8):
            hard = np.zeros(K, bool); hard[rng.permutation(K)[:CAP]] = True
            rec = rng.integers(0, H - 2 * K, K)
            w = x[a, g][:, rec] + rng.integers(0, 8, (16, K)); w[:, hard] = rng.integers(240, 256, (16, CAP))
            q[a, g] = w; u = start(w, 0)
            e = np.flatnonzero(~hard); p[a, g][rng.integers(0, 16, len(e)), u[e]] = rec[e]
            b = np.flatnonzero(hard); c = K * int(rng.integers(0, F))
            free = rng.permutation(np.setdiff1d(np.arange(c, c + K), u[b]))
            way = np.concatenate([u[b], free[:S * CAP]]).reshape(S + 1, CAP)
            mo[a, g] = mothers(rng, way[:-1].reshape(-1), way[1:].reshape(-1))
            x[o, g][:, H - K:H - K + CAP] = 8 * rng.integers(30, 32, (16, CAP))
            p[o, g][rng.integers(8, 16, CAP), way[S]] = H - K + np.arange(CAP)
            x[o, g][:, H - 2 * K:H - K] = rng.integers(136, 200, (16, K))
            if g % 2 == 0: rec = np.full(K, H - 2 * K)
            else:
                rec = H - 2 * K + rng.permutation(K); rec[K - 1] = rec[0]
            w = x[o, g][:, rec] + rng.integers(-8, 9, (16, K))
            q[o, g] = w; u = start(w, 0)
            free = rng.permutation(np.setdiff1d(np.arange(V), u))
            if g // 2 % 2 == 0: free = free[np.argsort(free // K != int(rng.integers(0, F)), kind="stable")]
            v = rng.permutation(free[:K]); mo[o, g] = mothers(rng, u, v)
            p[o, g][rng.integers(0, 8, K), v] = rec
    z = rng.integers(0, H, (N, 8, 1, 1))
    return pack(np.take_along_axis(x, (np.arange(H) - z) % H, 3), q, (p + z) % H, mo, th)
def setup_inputs_spread(rng):
    x, q, p, mo, th = parts(rng)
    x = np.minimum((np.exp2(8.2 * rng.random((N, 8, 1, H))) * rng.random((N, 8, 16, H))).astype(np.int64), 255)
    q = np.minimum((np.exp2(8.2 * rng.random((N, 8, 1, K))) * rng.random((N, 8, 16, K))).astype(np.int64), 255)
    return pack(x, q, p, mo, np.exp2(5 + 6 * rng.random((N, 8))).astype(np.int64))
def check_inputs(d):
    bad = []
    for k in ("x", "qs"):
        v = np.asarray(d[k]).astype(np.float64)
        if not np.all((v >= 0) & (v <= 255) & (v == np.floor(v))): bad.append("whole numbers from 0 to 255 in " + k)
    if np.min(d["towns"]) < 0 or np.max(d["towns"]) > H - 1: bad.append("range of towns")
    m = np.sort(np.asarray(d["mo"]), axis=-1)
    if not np.array_equal(m, np.broadcast_to(np.arange(V), m.shape)): bad.append("the mothers of a group are all different")
    t = np.asarray(d["th"]).reshape(-1, 16)
    if np.min(t) < 0 or np.max(t) > 4096: bad.append("range of th")
    if not np.all(t == t[:, :1]): bad.append("one threshold a group")
    return bad
def tries(rec, lists, u, q, th):
    li = np.take_along_axis(lists, u[:, None, :], 2)
    col = np.take_along_axis(rec, li.reshape(8, 1, 16 * K), 2).reshape(8, 16, 16, K)
    dist = np.add.reduce(np.abs(col - q[:, :, None, :]), axis=1)
    best = np.argmin(dist, axis=1); worst = np.argmax(dist, axis=1)
    num = np.take_along_axis(li, best[:, None, :], 1)[:, 0]
    return np.min(dist, axis=1) < th[:, None], num, worst, li
def reference(x, qs, towns, mo, th):
    X = np.zeros((N, 8, 16, W), np.int32); X[..., :H] = x.astype(np.float32).astype(np.int32).reshape(N, 8, 16, H)
    q = qs.astype(np.float32).astype(np.int32).reshape(N, 8, 16, K)
    P = towns.astype(np.int64).reshape(N, 8, 16, V); M = mo.astype(np.int64); T = th.reshape(N, 8, 16)[:, :, 0].astype(np.int64)
    ans = np.zeros((N, K), np.int64)
    for t in range(R):
        X1, P1, M1, q1, ans1 = X.copy(), P.copy(), M.copy(), q.copy(), ans.copy()
        for a in range(N):
            u = start(q[a].astype(np.int64), ans[a][None, :]); home = np.zeros((8, K), bool); num = np.zeros((8, K), np.int64); path = []
            for s in range(S):
                ok, nm, worst, li = tries(X[a], P[a], u, q[a], T[a])
                hit = ok & ~home; fail = ~ok & ~home
                num = np.where(hit, nm, num); path.append((u, fail, worst, li)); home = home | hit
                u = np.where(fail, np.take_along_axis(M[a], u, 1), u)
            slot = np.add.accumulate((~home).astype(np.int64), axis=1) - 1; place = H + CAP * t + slot
            o = (a + 1 + t) % N
            ok, nm, worst, li = tries(X[o], P[o], u, q[a], T[o])
            came = ok & ~home & (slot < CAP); got = home | came
            old = np.where(home[:, None, :], np.take_along_axis(X[a], num[:, None, :], 2), np.take_along_axis(X[o], nm[:, None, :], 2))
            num = np.where(came, place, num)
            for g in range(8):
                for u_, fail, worst, li in path[::-1]:
                    j = np.flatnonzero(fail[g] & got[g]); new = li[g][:, j]; new[worst[g, j], np.arange(len(j))] = num[g, j]
                    P1[a, g][:, u_[g, j]] = new
                u0, f0 = path[0][0][g], path[0][1][g]
                k = np.flatnonzero(f0[0::2] & f0[1::2]); v, w = u0[2 * k], u0[2 * k + 1]
                M1[a, g, v] = M[a, g, w]; M1[a, g, w] = M[a, g, v]
                j = np.flatnonzero(home[g]); r, i = np.unique(num[g, j], return_index=True); j = j[i]
                X1[a, g][:, r] = (X[a, g][:, r] + q[a, g][:, j]) >> 1
                j = np.flatnonzero(came[g]); X1[a, g][:, place[g, j]] = old[g][:, j]
            q1[a] = np.where(got[:, None, :], (q[a] + old) & 255, q[a])
            ans1[a] = np.add.reduce(got.astype(np.int64), axis=0)
        X, P, M, q, ans = X1, P1, M1, q1, ans1
    return {"yx": X.reshape(N, 128, W).astype(np.float32).astype(BF), "yp": P.reshape(N, 128, V).astype(np.float32), "ym": M.astype(np.float32)}

@@ -1,0 +1,565 @@
+import numpy as np
+from concourse.mybir import AluOpType as A, ActivationFunctionType as AF
+
+R_, H, V, K, CAP, N = 3, 2624, 512, 256, 64, 8
+PAD, W = 16, 2816
+TRX, TRP = PAD + W, V
+BIG = float(2 ** 30)
+ENG = 8
+QA = 10
+
+BUF, AT = {}, {}
+SCRATCH = {}
+
+
+def _add(where, dtype, **kw):
+    for k, v in kw.items():
+        BUF[k] = (where, [128] + (v if isinstance(v, list) else [v]), dtype)
+        SCRATCH["z_" + k] = BUF[k]
+
+
+def _pack(dtype, **kw):
+    at = 0
+    for k, v in kw.items():
+        BUF[k] = ("sbuf", [128, v], dtype)
+        AT[k] = ("t_" + dtype, at, v)
+        at += (v + 15) // 16 * 16
+    SCRATCH["t_" + dtype] = ("sbuf", [128, at], dtype)
+
+
+_add("sbuf", "int32", pti=V, moi=V, thi=1, vv=256, pk0=256, pk1=256, pk2=256, pkr0=64, pkr1=64, pkr2=64, sh=256, rn=256,
+     s1=256, s2=256)
+_pack("int32", pc=1, pmi=1, pgi=1, podd=1, bi=16, bq=16, kc=32, ke=32, wi=32, we=32, u2i=64, qi=64, gkc=4, gpos=4)
+_add("sbuf", "uint16", li=512)
+_pack("uint16", uu=32, offu=16, numu=16, xoff=32, poff=32, u2u=4, posu=4, lig=64, expl=16)
+_add("sbuf", "bfloat16", x=TRX + 256, q=256, qrep=4096, d=8192, xg=1024, ad=[32, 16, 16], lm=[16, 128], wem=[16, 128], bm=[16, 128],
+     ci=256, resn=256, resx=256, nt=256, qg=1024, dg=1040, adg=[4, 16, 16], rs0=64, rs1=64, rs2=64, rr0=64, rr1=64, rr2=64)
+_pack("bfloat16", id=128, nid=128, bo=128, nbo=128, ntri=128, id14=128, sw=128, swd=128, sg=128, one=128, ef=256, it=256,
+      dm=256, trib=256, resa=256, e=256, fw=256, gw=256, c=256, jb=16, rj=16, zz=16, okt=32, h=16, f0=16, un=16, hj=16, cs=32,
+      ewa=32, ewb=32, xk=16, cap=64, qb=64, rz=64, got=16)
+_add("sbuf", "float16", moh=[16, 2], mo8=[16, 32], e8=128, pcg=64)
+_pack("float16", lic=512, ns=512, pl=16, u1h=16)
+_add("sbuf", "float32", pt=V + 256, m256=V, pf=1, sc=512, sw2=512, sg2=64, ym2=V, mt=256)
+_pack("float32", dv=512, numc=16, pm=1, pg=1, pidx=1, widx=1, evc=1, th32=1, th2k=1, dcol=16, idf=128, j2=16, trx=16, trp=32, ios=64,
+      dmo=16, uf=32, t16=16, dl=16, d1=16, d0=16, capf=64, wd=512, plf=16, numf=16, nrb=256, cnt=256, l0=16, lt=16, xo=16, nl=512,
+      um=64, us=64, du=32, pz=32, po=32, ms=256)
+_add("psum", "float32", b0=512, b1=512, b2=512, b3=512, b4=[16, 32], b5=512, b6=512, b7=512)
+SEMAPHORES = ["sv", "sa", "st", "sg", "loc"] + ["dma%d" % i for i in range(16)] + ["rq%d" % t for t in range(3)] + ["rp%d" % t for t in range(3)]
+
+
+def _emask(topo, src, dst, n):
+    m = 0
+    for e in topo.engines(src, dst)[:n]:
+        m |= 1 << e
+    return m
+
+
+def _relay(topo, src, dst):
+    if topo.may_write(src, dst):
+        return None
+    for c in topo.cores_of(src):
+        if topo.die(c) == topo.die(src) and topo.may_write(c, dst):
+            return c
+    return None
+
+
+def _send(g, T, topo, src, dst, name, sem, cols=None):
+    rid, pid = topo.addr(dst, src)
+    ap_out = T["z_" + name][:] if cols is None else T["z_" + cols[0]][:]
+    ap_in = T["z_" + name][:] if cols is None else T["z_" + name][:, 0:cols[1]]
+    g.remote_dma(ap_out, ap_in, T.sem[sem], T.sem.loc, pid, rid, _emask(topo, src, dst, ENG))
+    return len(topo.engines(src, dst)[:ENG])
+
+
+def _hand_on(g, core, T, topo):
+    n = 0
+    for t in range(R_):
+        for kind in ("rq", "rp"):
+            for r in range(N):
+                a, b = T.cores[r], T.cores[(r + 1 + t) % N]
+                src, dst = (a, b) if kind == "rq" else (b, a)
+                if _relay(topo, src, dst) == core:
+                    g.wait_ge(T.sem["%s%d" % (kind, t)], len(topo.engines(src, core)[:ENG]))
+                    n += _send(g, T, topo, core, dst, ("pkr%d" if kind == "rq" else "rr%d") % t, "%s%d" % (kind, t))
+    if n:
+        g.wait_ge(T.sem.loc, n)
+
+
+def rank_program(g, core, T, topo):
+    rank = T.rank_of(core)
+    if rank is None:
+        _hand_on(g, core, T, topo)
+        return
+
+    Q = {"v": g.vector, "s": g.scalar, "t": g.tensor, "g": g, "y": g.sync}
+    SEM = {"v": "sv", "s": "sa", "t": "st", "g": "sg"}
+    total, hist, clk, known, cache = {}, {}, {}, {k: {} for k in "vstgy"}, {}
+    ndma = [0]
+
+    def B(name, *idx):
+        key = (name, idx)
+        if key not in cache:
+            full = (slice(None),) + tuple(slice(*i) if isinstance(i, tuple) else i for i in idx)
+            m = np.zeros(BUF[name][1][1:], bool)
+            m[tuple(full[1:])] = True
+            if name in AT:
+                phys, at, w = AT[name]
+                lo, hi, st = (tuple(idx[0]) + (1,))[:3] if idx else (0, w, 1)
+                ap = T[phys][:, at + lo:at + hi:st] if st > 1 else T[phys][:, at + lo:at + hi]
+            else:
+                ap = T["z_" + name][full]
+            cache[key] = (ap, name, int.from_bytes(np.packbits(m.ravel(), bitorder="little").tobytes(), "little"))
+        return cache[key]
+
+    def deps(q, reads, writes):
+        need = {}
+
+        def want(rec):
+            need[rec[2]] = max(need.get(rec[2], 0), rec[3])
+        for wr, lst in ((False, reads), (True, writes)):
+            for ap, name, m in lst:
+                ps = BUF[name][0] == "psum"
+                for rec in hist.get(name, ()):
+                    same = rec[4] == q
+                    if ps and not same:
+                        want(rec)
+                    elif rec[0] & m:
+                        if rec[1] and not (ps and q == "t" and same):
+                            want(rec)
+                        elif wr and not rec[1] and not same:
+                            want(rec)
+        return need
+
+    def wait(q, need):
+        kn = known[q]
+        todo = {s: v for s, v in need.items() if kn.get(s, 0) < v}
+        for s, v in todo.items():
+            if any(o != s and clk[(o, w)].get(s, 0) >= v for o, w in todo.items()):
+                continue
+            if kn.get(s, 0) >= v:
+                continue
+            Q[q].wait_ge(T.sem[s], v)
+            for k2, v2 in clk[(s, v)].items():
+                kn[k2] = max(kn.get(k2, 0), v2)
+            kn[s] = max(kn.get(s, 0), v)
+
+    def record(q, reads, writes, sem, val):
+        clk[(sem, val)] = dict(known[q])
+        for ap, name, m in writes:
+            hist[name] = [r for r in hist.get(name, []) if r[0] & ~m] + [(m, True, sem, val, q)]
+        for ap, name, m in reads:
+            hist[name] = [r for r in hist.get(name, []) if r[1] or r[4] != q or r[0] & ~m] + [(m, False, sem, val, q)]
+
+    def op(q, fn, out, *ins):
+        wait(q, deps(q, ins, (out,)))
+        sem = SEM[q]
+        total[sem] = total.get(sem, 0) + 1
+        fn().then_inc(T.sem[sem], 1)
+        record(q, ins, (out,), sem, total[sem])
+
+    def dma(q, out, in_, reads, writes):
+        wait(q, deps(q, reads, writes))
+        sem = "dma%d" % ndma[0]
+        ndma[0] += 1
+        total[sem] = 16
+        Q[q].dma_start(out, in_).then_inc(T.sem[sem], 16)
+        record(q, reads, writes, sem, 16)
+
+    def arrived(name, sem, src, dst):
+        n = len(topo.engines(src, dst)[:ENG])
+        total[sem] = n
+        clk[(sem, n)] = {}
+        hist[name] = [((1 << 64) - 1, True, sem, n, "r")]
+
+    vec, act, pe = g.vector, g.scalar, g.tensor
+
+    def cp(out, in_):
+        op("v", lambda: vec.tensor_copy(out[0], in_[0]), out, in_)
+
+    def tt(out, a, b, o):
+        op("v", lambda: vec.tensor_tensor(out[0], a[0], b[0], o), out, a, b)
+
+    def ts(out, a, s1, o1, s2=None, o2=None):
+        cols = [s for s in (s1, s2) if isinstance(s, tuple)]
+        x1 = s1[0] if isinstance(s1, tuple) else s1
+        x2 = s2[0] if isinstance(s2, tuple) else s2
+        if o2 is None:
+            op("v", lambda: vec.tensor_scalar(out[0], a[0], x1, None, o1), out, a, *cols)
+        else:
+            op("v", lambda: vec.tensor_scalar(out[0], a[0], x1, x2, o1, o2), out, a, *cols)
+
+    def scan(out, d0, d1, o1, o2):
+        op("v", lambda: vec.tensor_tensor_scan(out[0], d0[0], d1[0], 0.0, o1, o2), out, d0, d1)
+
+    def gat(out, win, off):
+        op("v", lambda: vec.tensor_copy(out[0], win[0].indirect(off[0])), out, win, off)
+
+    def gat_tt(out, win, off, b, o):
+        op("v", lambda: vec.tensor_tensor(out[0], win[0].indirect(off[0]), b[0], o), out, win, off, b)
+
+    def scat(win, off, in_):
+        op("v", lambda: vec.tensor_copy(win[0].indirect(off[0]), in_[0]), win, off, in_)
+
+    def fill(out, c):
+        op("v", lambda: vec.memset(out[0], c), out)
+
+    def ac(out, in_, f, bias=0.0, scale=1.0):
+        if isinstance(scale, tuple):
+            op("s", lambda: act.activation(out[0], in_[0], f, bias=bias, scale=scale[0]), out, in_, scale)
+        else:
+            op("s", lambda: act.activation(out[0], in_[0], f, bias=bias, scale=scale), out, in_)
+
+    def agat(out, win, off, bias=0.0, scale=1.0):
+        op("s", lambda: act.activation(out[0], win[0].indirect(off[0]), AF.Identity, bias=bias, scale=scale), out, win, off)
+
+    def mm(out, l, r, start, stop):
+        op("t", lambda: pe.matmul(out[0], l[0], r[0], start, stop), out, l, r)
+
+    def iota(out, pattern, base=0, mult=0):
+        if BUF[out[1]][2] == "int32":
+            op("g", lambda: g.iota(out[0], pattern, base, mult), out)
+        else:
+            op("g", lambda: g.iota(out[0], pattern, base, mult, allow_small_or_imprecise_dtypes=True), out)
+
+    def send(dst, name, sem, cols=None):
+        hop = _relay(topo, core, dst)
+        src = B(name) if cols is None else B(name, (0, cols[1]))
+        wait("g", deps("g", (src,), ()))
+        n = _send(g, T, topo, core, dst if hop is None else hop, name, sem, cols)
+        total["loc"] = total.get("loc", 0) + n
+
+    dma("y", B("q")[0], T.qs[:], (), (B("q"),))
+    dma("s", B("x", (PAD, PAD + H))[0], T.x[:], (), (B("x", (PAD, PAD + H)),))
+    dma("y", B("pti")[0], T.towns[:], (), (B("pti"),))
+    dma("y", T.z_moi[0:8, :], T.mo[:], (), (B("moi"),))
+    dma("y", B("thi")[0], T.th[:], (), (B("thi"),))
+    AND, SHR = A.bitwise_and, A.arith_shift_right
+    iota(B("pc"), [[1, 1]], 0, 1)
+    iota(B("nt"), [[1, 16], [0, 16]])
+    iota(B("it"), [[0, 16], [1, 16]])
+    iota(B("ef"), [[1, 256]])
+    fill(B("lm"), 0.0)
+    fill(B("one"), 1.0)
+    op("g", lambda: g.affine_select(B("id")[0], B("one")[0], [[-1, 128]], A.is_equal, 0.0, 0, 1), B("id"), B("one"))
+    iota(B("ci"), [[0, 16], [1, 16]], 1)
+    iota(B("ios"), [[1, 64]])
+    ts(B("pmi"), B("pc"), 15, AND)
+    ts(B("pgi"), B("pc"), 4, SHR)
+    ts(B("podd"), B("pc"), 1, AND)
+    cp(B("pg"), B("pgi"))
+    ts(B("evc"), B("podd"), -1.0 / 32, A.mult, 1.0 / 32, A.add)
+    cp(B("pm"), B("pmi"))
+    cp(B("pf"), B("pc"))
+    e128, i128, n128 = B("ef", (0, 128)), B("it", (0, 128)), B("nt", (0, 128))
+    ts(B("bo"), n128, B("pg"), A.is_equal)
+    for m in range(16):
+        ac(B("lm", m, (m, 128, 16)), B("bo", (m, 128, 16)), AF.Copy, scale=32.0)
+    ts(B("resn"), B("it"), 0.5, A.is_lt, 2 * BIG, A.mult)
+    ts(B("resn"), B("resn"), -BIG, A.add)
+    ts(B("j2"), B("ef", (0, 16)), 16.0, A.mult, B("pm"), A.add)
+    cp(B("jb"), B("j2"))
+    ts(B("rj"), B("j2"), -1.0, A.mult, 255.0, A.add)
+    ts(B("trx"), B("j2"), float(TRX), A.add)
+    for s in range(2):
+        ts(B("trp", (16 * s, 16 * s + 16)), B("j2"), float(TRP), A.add)
+    ts(B("j2"), B("j2"), 2.0, A.mult)
+    ac(B("nid"), B("id"), AF.Copy, scale=-1.0)
+    ac(B("nbo"), B("bo"), AF.Copy, scale=-1.0)
+    op("g", lambda: g.affine_select(B("ntri")[0], B("nbo")[0], [[1, 128]], A.is_gt, 0.0, 0, -1), B("ntri"), B("nbo"))
+    ac(B("id14"), B("id"), AF.Copy, scale=1424.0)
+    ac(B("idf"), B("id"), AF.Copy)
+    ts(B("resx"), B("it"), 0.5, A.is_lt, -BIG - 2.0, A.mult)
+    ts(B("resx"), B("resx"), 2.0, A.add)
+    fill(B("x", (0, PAD)), 0.0)
+    fill(B("x", (PAD + H, TRX)), 0.0)
+
+    def qrep_v(lo, hi):
+        for i in range(lo, hi):
+            cp(B("qrep", (i, 4096, 16)), B("q"))
+
+    def qrep_s():
+        for i in range(16 - QA, 16):
+            ac(B("qrep", (i, 4096, 16)), B("q"), AF.Copy)
+
+    par = B("b1", (256, 272))
+
+    def parity(last):
+        for m in range(16):
+            mm(par, B("wem", m), B("q", (m, 256, 16)), m == 0, last and m == 15)
+
+    qrep_v(0, 5)
+    ts(B("wem"), B("lm"), B("evc"), A.mult)
+    parity(True)
+    op("v", lambda: vec.tensor_copy(T.z_mo8[0:8, :, :], T.z_moi[0:8, :]), B("mo8"), B("moi"))
+    op("v", lambda: vec.tensor_scalar(T.z_e8[0:8, :], T.z_nt[0:8, 0:128], T.z_pf[0:8, 0:1], None, A.is_equal), B("e8"), B("nt"), B("pf"))
+    op("t", lambda: pe.matmul(B("b4")[0], T.z_e8[0:8, :], T.z_mo8[0:8, :, :], True, True), B("b4"), B("e8"), B("mo8"))
+    qrep_s()
+    qrep_v(5, 16 - QA)
+    cp(B("pt", (0, V)), B("pti"))
+
+    def first_mothers():
+        ts(B("dm"), B("it"), B("pm"), A.is_equal)
+        ts(B("resa"), B("it"), 0.5, A.is_gt)
+        for s in range(2):
+            tt(B("mt"), B("b4", (0, 16), (s, 32, 2)), B("dm"), A.mult)
+            scan(B("ms"), B("resa"), B("mt"), A.mult, A.add)
+            cp(B("moh", (0, 16), s), B("ms", (15, 256, 16)))
+        tt(B("dmo"), B("moh", (0, 16), 1), B("moh", (0, 16), 0), A.subtract)
+
+    def late_constants():
+        ts(B("dcol"), B("ef", (0, 16)), B("pm"), A.is_equal)
+        ts(B("th32"), B("thi"), 32.0, A.mult)
+        ts(B("th2k"), B("thi"), 2048.0, A.mult)
+        ts(B("t16", (0, 1)), B("podd"), -2.0, A.mult, 1.0, A.add)
+        tt(B("t16", (0, 1)), B("t16", (0, 1)), B("pf"), A.add)
+        ts(B("sw"), e128, B("t16", (0, 1)), A.is_equal)
+        tt(B("swd"), B("sw"), B("id"), A.subtract)
+        ts(B("sg"), i128, B("pm"), A.is_equal)
+        fill(B("zz"), 0.0)
+        fill(B("cs"), 0.0)
+        ts(B("trib"), B("it"), B("pm"), A.is_ge, 1024.0, A.mult)
+        ts(B("pidx"), B("pm"), 1.0, A.add)
+        ts(B("widx"), B("pm"), -1.0, A.mult, 31.0, A.add)
+        cp(B("expl"), B("ios", (0, 16)))
+        ts(B("t16", (0, 1)), B("pm"), 16.0, A.mult, 16.0, A.add)
+        ts(B("um"), B("nt", (0, 64)), 256.0, A.mult, B("t16", (0, 1)), A.add)
+        tt(B("pcg"), B("um"), B("it", (0, 64)), A.add)
+        fill(B("dg", (0, 16)), -512.0)
+        fill(B("fw", (64, 256)), 0.0)
+        fill(B("gw", (64, 256)), 0.0)
+
+    xwin = B("x", (PAD, TRX))
+    u0, u1 = B("uf", (0, 16)), B("uf", (16, 32))
+    k0, k1 = B("b0", (0, 256)), B("b1", (0, 256))
+    best0, best1 = B("sc", (15, 256, 16)), B("sc", (271, 512, 16))
+
+    for t in range(R_):
+        end = t == R_ - 1
+        guest, host_of = T.cores[(rank - 1 - t) % N], T.cores[(rank + 1 + t) % N]
+        pk, pkr, rs, rr = "pk%d" % t, "pkr%d" % t, "rs%d" % t, "rr%d" % t
+
+        def came_from(src):
+            hop = _relay(topo, src, core)
+            return src if hop is None else hop
+
+        def diff(k, parts=(0, 1)):
+            lo, hi = 2 * k + parts[0], 2 * k + parts[-1] + 1
+            r = lo % 8
+            gat_tt(B("d", (512 * lo, 512 * hi)), xwin, B("li", (32 * lo, 32 * hi)), B("qrep", (512 * r, 512 * (r + hi - lo))), A.subtract)
+
+        def absd(k, parts=(0, 1)):
+            lo, hi = 2 * k + parts[0], 2 * k + parts[-1] + 1
+            ac(B("ad", (2 * lo, 2 * hi)), B("d", (512 * lo, 512 * hi)), AF.Abs)
+
+        def reduce(k):
+            s, c = k // 4, k % 4
+            out = B("b%d" % s, (64 * c, 64 * c + 64))
+            mm(out, B("id"), B("ci", (64 * c, 64 * c + 64)), True, False)
+            for m in range(16):
+                mm(out, B("lm", m), B("ad", (4 * k, 4 * k + 4), m), False, m == 15)
+
+        cp(B("bi"), par)
+        ts(B("bq"), B("bi"), 1, AND)
+        tt(u0, B("bq"), B("j2"), A.add)
+
+        def second_town():
+            tt(B("t16"), B("bq"), B("dmo"), A.mult)
+            tt(u1, B("t16"), B("moh", (0, 16), 0), A.add)
+
+        if t == 0:
+            cp(B("uu", (0, 16)), u0)
+            gat(B("li", (0, 256)), B("pt", (0, V)), B("uu", (0, 16)))
+        else:
+            second_town()
+            cp(B("uu"), B("uf"))
+            gat(B("li"), B("pt", (0, V)), B("uu"))
+        agat(B("xg"), xwin, B("li", (0, 64)))
+        for a in range(2):
+            mm(B("b%d" % (2 + a)), B("nid"), B("qrep", (512 * a, 512 * a + 512)), True, False)
+            mm(B("b%d" % (2 + a)), B("id"), B("xg", (512 * a, 512 * a + 512)), False, True)
+        diff(1)
+        absd(1)
+        if t == 0:
+            first_mothers()
+            second_town()
+            cp(B("uu", (16, 32)), u1)
+            gat(B("li", (256, 512)), B("pt", (0, V)), B("uu", (16, 32)))
+        for a in range(2):
+            ac(B("ad", (2 * a, 2 * a + 2)), B("b%d" % (2 + a)), AF.Abs)
+        reduce(1)
+        reduce(0)
+        diff(2)
+        if t == 0:
+            ac(B("m256"), B("b4"), AF.Copy, scale=256.0)
+        absd(2)
+        reduce(2)
+        diff(3)
+        absd(3)
+        reduce(3)
+        diff(4)
+        absd(4)
+        reduce(4)
+        if t == 0:
+            late_constants()
+        tt(B("du"), B("uf"), B("trp"), A.subtract)
+        ac(B("u1h"), u1, AF.Copy)
+        diff(5)
+        absd(5)
+        reduce(5)
+        scan(B("sc", (0, 256)), B("resn"), k0, A.max, A.min)
+        ts(B("okt", (0, 16)), best0, B("th32"), A.is_lt)
+        ts(B("f0"), B("okt", (0, 16)), -1.0, A.mult, 1.0, A.add)
+        diff(6)
+        absd(6)
+        mm(B("b6", (48, 64)), B("swd"), B("u1h"), True, True)
+        mm(B("b6", (64, 80)), B("sw"), B("f0"), True, True)
+        reduce(6)
+        for hf in range(2):
+            diff(7, (hf,))
+            absd(7, (hf,))
+        reduce(7)
+        tt(B("xk"), B("b6", (64, 80)), B("f0"), A.mult)
+        tt(B("du", (0, 16)), B("du", (0, 16)), B("f0"), A.mult)
+        tt(B("dl"), B("b6", (48, 64)), B("xk"), A.mult)
+        scan(B("sw2", (0, 256)), B("resx"), k0, A.add, A.max)
+        tt(B("d1"), B("dl"), B("bq"), A.mult)
+        tt(B("d0"), B("dl"), B("d1"), A.subtract)
+        tt(B("moh", (0, 16), 1), B("moh", (0, 16), 1), B("d1"), A.add)
+        tt(B("moh", (0, 16), 0), B("moh", (0, 16), 0), B("d0"), A.add)
+        ts(B("kc", (0, 16)), best0, B("th32"), A.min)
+        ts(B("ke", (0, 16)), B("kc", (0, 16)), 31, AND)
+        cp(B("ewa", (0, 16)), B("ke", (0, 16)))
+        tt(B("dmo"), B("moh", (0, 16), 1), B("moh", (0, 16), 0), A.subtract)
+        gat_tt(B("vv"), B("m256"), B("uu", (16, 32)), B("q"), A.add)
+        scan(B("sc", (256, 512)), B("resn"), k1, A.max, A.min)
+        ts(B("okt", (16, 32)), best1, B("th32"), A.is_lt)
+        tt(B("h"), B("okt", (0, 16)), B("okt", (16, 32)), A.max)
+        scan(B("cs", (1, 17)), B("h"), B("zz"), A.add, A.add)
+        tt(B("hj"), B("h"), B("rj"), A.mult)
+        off = B("b6", (16, 32))
+        mm(off, B("id"), B("jb"), True, False)
+        mm(off, B("ntri"), B("h"), False, False)
+        mm(off, B("nbo"), B("cs", (0, 16)), False, False)
+        mm(off, B("id"), B("hj"), False, True)
+        ts(B("kc", (16, 32)), best1, B("th32"), A.min)
+        ts(B("ke", (16, 32)), B("kc", (16, 32)), 31, AND)
+        tt(B("ewa", (16, 32)), B("ke", (16, 32)), B("f0"), A.mult)
+        ac(B("un"), B("h"), AF.Identity, bias=1.0, scale=-1.0)
+        mm(B("b6", (32, 33)), B("bo"), B("cs", (16, 17)), True, True)
+        cp(B("offu"), off)
+        scat(B(pk, (0, 256)), B("offu"), B("vv"))
+        send(host_of, pk, "rq%d" % t, (pkr, 64))
+        agat(B("lic"), B("pt", (0, V)), B("uu"), bias=-44.0, scale=1.0 / 32)
+        if t == 0:
+            for m in range(16):
+                ac(B("bm", m), B("bo"), AF.Copy, scale=B("dcol", (m, m + 1)))
+        for m in range(16):
+            mm(B("b2", (m, 512, 16)), B("bm", m), B("ewa"), True, True)
+        ac(B("plf"), off, AF.Identity, bias=(1216.0 + 64 * t) / 32, scale=1.0 / 32)
+        tt(B("pl"), B("plf"), B("un"), A.mult)
+        ts(B("capf"), B("ios"), B("b6", (32, 33)), A.add, 256.0, A.is_lt)
+        ac(B("cap"), B("capf"), AF.Identity, bias=-1.0, scale=256.0)
+        ts(B("b3"), B("b2"), B("pidx"), A.is_equal)
+        tt(B("ns"), B("b3"), B("lic"), A.mult)
+        scan(B("sw2", (256, 512)), B("resx"), k1, A.add, A.max)
+        ts(B("wi"), B("sw2", (15, 512, 16)), -64.0, A.max)
+        ts(B("we"), B("wi"), 31, AND)
+        cp(B("ewb"), B("we"))
+        num = B("b6", (80, 96))
+        for m in range(16):
+            for s in range(2):
+                mm(num, B("lm", m), B("ns", (256 * s + m, 256 * s + 256, 16)), m == 0 and s == 0, False)
+        mm(num, B("id14"), B("h"), False, True)
+        for m in range(16):
+            mm(B("b7", (m, 512, 16)), B("bm", m), B("ewb"), True, True)
+        vp = B("b5", (0, 256))
+        for s in range(2):
+            mm(vp, B("bo"), B("ns", (256 * s, 256 * s + 256)), s == 0, False)
+        for m in range(16):
+            mm(B("b5", (m, 256, 16)), B("bm", m), B("pl"), False, m == 15)
+        cp(B("numu"), num)
+        ac(B("numc"), num, AF.Identity, bias=-44.5, scale=1.0 / 32)
+        ac(B("numf"), num, AF.Copy)
+        gat_tt(B("sh"), B("x", (0, TRX)), B("numu"), B("q"), A.add)
+        ts(B("rn"), B("sh"), 1, SHR)
+        arrived(pkr, "rq%d" % t, came_from(guest), core)
+        ts(B("qi"), B(pkr), 255, AND)
+        cp(B("qb"), B("qi"))
+        for i in range(5, 16):
+            ac(B("qg", (i, 1024, 16)), B("qb"), AF.Copy)
+        ts(B("u2i"), B(pkr), 8, SHR)
+        tt(B("um"), B("u2i"), B("dm", (0, 64)), A.mult)
+        scan(B("us"), B("resa", (0, 64)), B("um"), A.mult, A.add)
+        cp(B("u2u"), B("us", (15, 64, 16)))
+        gat(B("lig"), B("pt", (0, V)), B("u2u"))
+        for i in range(5):
+            cp(B("qg", (i, 1024, 16)), B("qb"))
+        for hf in range(2):
+            gat_tt(B("dg", (16 + 512 * hf, 528 + 512 * hf)), xwin, B("lig", (32 * hf, 32 * hf + 32)), B("qg", (512 * hf, 512 * hf + 512)), A.subtract)
+            ac(B("adg", (2 * hf, 2 * hf + 2)), B("dg", (16 + 512 * hf, 528 + 512 * hf)), AF.Abs, scale=64.0)
+        gk = B("b1", (0, 64))
+        mm(gk, B("id"), B("pcg"), True, False)
+        for m in range(16):
+            mm(gk, B("lm", m), B("adg", (0, 4), m), False, m == 15)
+        ts(B("b3"), B("b7"), B("widx"), A.is_equal)
+        for s in range(2):
+            tt(B("dv", (256 * s, 256 * s + 256)), vp, B("lic", (256 * s, 256 * s + 256)), A.subtract)
+        tt(B("wd"), B("b3"), B("dv"), A.mult)
+        tt(B("nrb"), vp, B("trib"), A.add)
+        scan(B("sg2"), B("resn", (0, 64)), gk, A.max, A.min)
+        ts(B("gkc"), B("sg2", (15, 64, 16)), B("th2k"), A.min)
+        ts(B("gpos"), B("gkc"), 2047, AND)
+        cp(B("posu"), B("gpos"))
+        gat_tt(B(rs), B("dg"), B("posu"), B("qb"), A.add)
+        send(guest, rs, "rp%d" % t, (rr, 64))
+        for m in range(16):
+            mm(B("b4", (0, 16), (2 * m, 2 * m + 2)), B("bm", m), B("moh"), True, True)
+        mm(B("b7"), B("id"), B("lic"), True, False)
+        mm(B("b7"), B("idf"), B("wd"), False, True)
+        if not end:
+            ac(B("m256"), B("b4"), AF.Copy, scale=256.0)
+        else:
+            ac(B("ym2"), B("b4"), AF.Copy)
+            dma("y", T.ym[:], T.z_ym2[0:128:16, :], (B("ym2"),), ())
+        ac(B("nl"), B("b7"), AF.Identity, bias=1408.0, scale=32.0)
+        gat_tt(B("e"), B("numc"), B("expl"), B("nrb"), A.is_equal)
+        scan(B("cnt"), B("resa"), B("e"), A.mult, A.add)
+        ts(B("l0"), B("cnt", (15, 256, 16)), 0.5, A.is_ge)
+        tt(B("l0"), B("l0"), B("un"), A.max)
+        tt(B("lt"), B("l0"), B("trx"), A.mult)
+        tt(B("xo"), B("lt"), B("numf"), A.max)
+        cp(B("xoff", (0, 32, 2)), B("xo"))
+        for n in range(15, -1, -1):
+            scat(B("x"), B("xoff", (2 * n, 2 * n + 1)), B("rn", (16 * n, 16 * n + 16)))
+        if end:
+            dma("y", T.yx[:, 0:H + 2 * CAP], B("x", (PAD, PAD + H + 2 * CAP))[0], (B("x", (PAD, PAD + H + 2 * CAP)),), ())
+        arrived(rr, "rp%d" % t, came_from(host_of), core)
+        tt(B("rz"), B(rr), B("cap"), A.min)
+        ts(B("fw", (0, 64)), B("rz"), 0.0, A.is_ge, 1.0 / 512, A.mult)
+        agat(B("c"), B("fw"), B("offu"))
+        ts(B("gw", (0, 64)), B("rz"), 0.0, A.max)
+        gcol = B("x", (PAD + H + CAP * t, PAD + H + CAP * t + CAP))
+        came = B("b6", (96, 112))
+        for m in range(16):
+            mm(came, B("lm", m), B("c", (m, 256, 16)), m == 0, m == 15)
+        if not end:
+            gat_tt(B("s1"), B("gw"), B("offu"), B("sh"), A.add)
+            ts(B("s2"), B("s1"), 255, AND)
+            cp(B("q"), B("s2"))
+            parity(False)
+            qrep_s()
+            qrep_v(0, 16 - QA)
+        ac(gcol, B("gw", (0, 64)), AF.Copy)
+        tt(B("got"), B("h"), came, A.max)
+        if not end:
+            mm(par, B("sg"), B("got"), False, True)
+        tt(B("pz", (0, 16)), B("got"), B("du", (0, 16)), A.mult)
+        tt(B("pz", (16, 32)), came, B("du", (16, 32)), A.mult)
+        tt(B("po"), B("pz"), B("trp"), A.add)
+        cp(B("poff"), B("po"))
+        scat(B("pt"), B("poff", (16, 32)), B("nl", (256, 512)))
+        scat(B("pt"), B("poff", (0, 16)), B("nl", (0, 256)))
+    dma("y", T.yx[:, H + 2 * CAP:W], B("x", (PAD + H + 2 * CAP, TRX))[0], (B("x", (PAD + H + 2 * CAP, TRX)),), ())
+    dma("s", T.yp[:], B("pt", (0, V))[0], (B("pt", (0, V)),), ())
+    for s, v in total.items():
+        g.wait_ge(T.sem[s], v)

@@ -1,12 +1,16 @@
 import numpy as np
+from concourse.bass import DstId, RemoteDMATransfer
 from concourse.mybir import AluOpType as A, ActivationFunctionType as AF
 
 R_, H, V, K, CAP, N = 3, 2624, 512, 256, 64, 8
 PAD, W = 16, 2816
 TRX, TRP = PAD + W, V
+LP = 8
 BIG = float(2 ** 30)
-ENG = 8
-QA = 10
+MID = float(2 ** 20)
+QV = 0
+QV0 = 8
+GV = 5
 
 BUF, AT = {}, {}
 SCRATCH = {}
@@ -27,62 +31,74 @@ def _pack(dtype, **kw):
     SCRATCH["t_" + dtype] = ("sbuf", [128, at], dtype)
 
 
-_add("sbuf", "int32", pti=V, moi=V, thi=1, vv=256, pk0=256, pk1=256, pk2=256, pkr0=64, pkr1=64, pkr2=64, sh=256, rn=256,
-     s1=256, s2=256)
-_pack("int32", pc=1, pmi=1, pgi=1, podd=1, bi=16, bq=16, kc=32, ke=32, wi=32, we=32, u2i=64, qi=64, gkc=4, gpos=4)
+_add("sbuf", "int32", pti=LP + V, moi=V, vv=256, pk=512, s1=256, s2=256)
+_pack("int32", pc=1, pmi=1, pgi=1, podd=1, bi=16, bq=16, kc=64, ke=64, u2i=64, qi=64, gkc=4, gpos=4)
 _add("sbuf", "uint16", li=512)
-_pack("uint16", uu=32, offu=16, numu=16, xoff=32, poff=32, u2u=4, posu=4, lig=64, expl=16)
-_add("sbuf", "bfloat16", x=TRX + 256, q=256, qrep=4096, d=8192, xg=1024, ad=[32, 16, 16], lm=[16, 128], wem=[16, 128], bm=[16, 128],
-     ci=256, resn=256, resx=256, nt=256, qg=1024, dg=1040, adg=[4, 16, 16], rs0=64, rs1=64, rs2=64, rr0=64, rr1=64, rr2=64)
-_pack("bfloat16", id=128, nid=128, bo=128, nbo=128, ntri=128, id14=128, sw=128, swd=128, sg=128, one=128, ef=256, it=256,
-      dm=256, trib=256, resa=256, e=256, fw=256, gw=256, c=256, jb=16, rj=16, zz=16, okt=32, h=16, f0=16, un=16, hj=16, cs=32,
-      ewa=32, ewb=32, xk=16, cap=64, qb=64, rz=64, got=16)
-_add("sbuf", "float16", moh=[16, 2], mo8=[16, 32], e8=128, pcg=64)
-_pack("float16", lic=512, ns=512, pl=16, u1h=16)
-_add("sbuf", "float32", pt=V + 256, m256=V, pf=1, sc=512, sw2=512, sg2=64, ym2=V, mt=256)
-_pack("float32", dv=512, numc=16, pm=1, pg=1, pidx=1, widx=1, evc=1, th32=1, th2k=1, dcol=16, idf=128, j2=16, trx=16, trp=32, ios=64,
-      dmo=16, uf=32, t16=16, dl=16, d1=16, d0=16, capf=64, wd=512, plf=16, numf=16, nrb=256, cnt=256, l0=16, lt=16, xo=16, nl=512,
-      um=64, us=64, du=32, pz=32, po=32, ms=256)
+_pack("uint16", uu=32, offu=16, numu=16, xoff=32, poff=32, u2u=4, posu=4, lig=64, eu=64)
+_add("sbuf", "bfloat16", x=TRX + 256, q=256, qrep=4096, d=8192, ad=[32, 16, 16], bm=[16, 128], zl=144, zw=144, ci=256, resn=256,
+     resx=256, nt=256, qg=1024, dg=CAP + 1024, flw=CAP + 1024, adg=[4, 16, 16], xr0=H, xr1=H + CAP, xr2=H + 2 * CAP, fw=512, gw=512,
+     rn=256)
+_pack("bfloat16", id=128, nid=128, bo=128, nbo=128, ntri=128, id14=128, idk=128, sw=128, swd=128, sg=128, one=144, ef=256, it=256,
+      dm=64, trib=256, resa=64, c=256, da=256, am=256, jb=16, zz=16, ok=32, f0=16, un=16, cs=32, xk=16, qb=64, got=16, oh=32)
+_add("sbuf", "float16", moh=[16, 2], mo8=[16, 32], e8=128, z8=144, pcg=64)
+_pack("float16", lic=512, ns=512, plg=256, rnh=256, u1h=16, rj=16, hj=16, numc=16, trph=16)
+_add("sbuf", "float32", pt=LP + V + 256, pr0=LP + V, pr1=LP + V, pr2=LP + V, mw=V, pf=1, sc=1024, sg2=64, ym2=V, plw=512, lif=512,
+     dvs=512, wd=512, sh=256)
+_pack("float32", pm=1, pg=1, pz=1, pidx=1, widx=1, evc=1, th32=1, thb=1, th2k=1, dcol=16, j2=16, trx=16, trp=32, dmo=16, uf=32, t16=16,
+      dl=16, d1=16, d0=16, thl=16, thq=64, thp=4, a2=16, xt=16, xo=16, um=64, us=64, zu=32, ub=32, po=32)
 _add("psum", "float32", b0=512, b1=512, b2=512, b3=512, b4=[16, 32], b5=512, b6=512, b7=512)
-SEMAPHORES = ["sv", "sa", "st", "sg", "loc"] + ["dma%d" % i for i in range(16)] + ["rq%d" % t for t in range(3)] + ["rp%d" % t for t in range(3)]
+KINDS = "xcp"
+SEMAPHORES = (["sv", "sa", "st", "sg"] + ["dma%d" % i for i in range(16)]
+              + [a + k + str(t) for a in ("in", "lo") for k in KINDS for t in range(R_)])
 
 
-def _emask(topo, src, dst, n):
+def _mask(es):
     m = 0
-    for e in topo.engines(src, dst)[:n]:
+    for e in es:
         m |= 1 << e
     return m
 
 
-def _relay(topo, src, dst):
-    if topo.may_write(src, dst):
-        return None
-    for c in topo.cores_of(src):
-        if topo.die(c) == topo.die(src) and topo.may_write(c, dst):
-            return c
-    return None
+def _relays(T, topo, r, t):
+    def far(a):
+        return not topo.may_write(T.cores[a], T.cores[(a - 1 - t) % N])
+    src, dst = T.cores[r], T.cores[(r - 1 - t) % N]
+    if not far(r):
+        return []
+    busy = {topo.die(T.cores[a]) for a in range(N) if a != r and T.cores[a] in topo.cores_of(src) and far(a)}
+    return [c for c in topo.cores_of(src) if topo.may_write(c, dst) and topo.die(c) not in busy]
 
 
-def _send(g, T, topo, src, dst, name, sem, cols=None):
-    rid, pid = topo.addr(dst, src)
-    ap_out = T["z_" + name][:] if cols is None else T["z_" + cols[0]][:]
-    ap_in = T["z_" + name][:] if cols is None else T["z_" + name][:, 0:cols[1]]
-    g.remote_dma(ap_out, ap_in, T.sem[sem], T.sem.loc, pid, rid, _emask(topo, src, dst, ENG))
-    return len(topo.engines(src, dst)[:ENG])
+def _pieces(T, topo, r, t, kind):
+    hops = _relays(T, topo, r, t) or [None]
+    old = H + CAP * max(t - 1, 0)
+    if kind == "c":
+        return [(hops[0], old, old + CAP)] if t else []
+    lo, hi = (0, old) if kind == "x" else (LP - 4, LP + V)
+    n = (hi - lo) // len(hops)
+    return [(c, lo + n * k, lo + n * k + n) for k, c in enumerate(hops)]
+
+
+def _copy(kind, t):
+    return "%s%d" % ("pr" if kind == "p" else "xr", t)
 
 
 def _hand_on(g, core, T, topo):
-    n = 0
+    sent = []
     for t in range(R_):
-        for kind in ("rq", "rp"):
+        for kind in ("px" if t == 0 else KINDS):
             for r in range(N):
-                a, b = T.cores[r], T.cores[(r + 1 + t) % N]
-                src, dst = (a, b) if kind == "rq" else (b, a)
-                if _relay(topo, src, dst) == core:
-                    g.wait_ge(T.sem["%s%d" % (kind, t)], len(topo.engines(src, core)[:ENG]))
-                    n += _send(g, T, topo, core, dst, ("pkr%d" if kind == "rq" else "rr%d") % t, "%s%d" % (kind, t))
-    if n:
-        g.wait_ge(T.sem.loc, n)
+                ps = _pieces(T, topo, r, t, kind)
+                for c, lo, hi in ps:
+                    if c == core:
+                        dst = T.cores[(r - 1 - t) % N]
+                        g.wait_ge(T.sem["in%s%d" % (kind, t)], len(topo.engines(T.cores[r], core)) // len(ps))
+                        rid, pid = topo.addr(dst, core)
+                        ap = T["z_" + _copy(kind, t)][:, lo:hi]
+                        g.remote_dma(ap, ap, T.sem["in%s%d" % (kind, t)], T.sem["lo%s%d" % (kind, t)], pid, rid, topo.mask(core, dst))
+                        sent.append(("lo%s%d" % (kind, t), len(topo.engines(core, dst))))
+    for sem, n in sent:
+        g.wait_ge(T.sem[sem], n)
 
 
 def rank_program(g, core, T, topo):
@@ -143,12 +159,13 @@ def rank_program(g, core, T, topo):
                 kn[k2] = max(kn.get(k2, 0), v2)
             kn[s] = max(kn.get(s, 0), v)
 
-    def record(q, reads, writes, sem, val):
+    def record(q, reads, writes, sem, val, who=None):
         clk[(sem, val)] = dict(known[q])
+        who = who or q
         for ap, name, m in writes:
-            hist[name] = [r for r in hist.get(name, []) if r[0] & ~m] + [(m, True, sem, val, q)]
+            hist[name] = [r for r in hist.get(name, []) if r[0] & ~m] + [(m, True, sem, val, who)]
         for ap, name, m in reads:
-            hist[name] = [r for r in hist.get(name, []) if r[1] or r[4] != q or r[0] & ~m] + [(m, False, sem, val, q)]
+            hist[name] = [r for r in hist.get(name, []) if r[1] or r[4] != who or r[0] & ~m] + [(m, False, sem, val, who)]
 
     def op(q, fn, out, *ins):
         wait(q, deps(q, ins, (out,)))
@@ -163,13 +180,37 @@ def rank_program(g, core, T, topo):
         ndma[0] += 1
         total[sem] = 16
         Q[q].dma_start(out, in_).then_inc(T.sem[sem], 16)
-        record(q, reads, writes, sem, 16)
+        record(q, reads, writes, sem, 16, sem)
 
-    def arrived(name, sem, src, dst):
-        n = len(topo.engines(src, dst)[:ENG])
+    def arrived(kind, t):
+        r = (rank + 1 + t) % N
+        sem, name = "in%s%d" % (kind, t), _copy(kind, t)
+        ps = _pieces(T, topo, r, t, kind)
+        n = sum(len(topo.engines(T.cores[r] if c is None else c, core)) for c, lo, hi in ps)
+        if n:
+            total[sem] = n
+            clk[(sem, n)] = {}
+            hist.setdefault(name, []).append((B(name, (ps[0][1], ps[-1][2]))[2], True, sem, n, sem))
+
+    def send(kind, t):
+        ps = _pieces(T, topo, rank, t, kind)
+        name, at = ("pt", 0) if kind == "p" else ("x", PAD)
+        src = B(name, (at + ps[0][1], at + ps[-1][2]))
+        wait("g", deps("g", (src,), ()))
+        trs, n = [], 0
+        for k, (c, lo, hi) in enumerate(ps):
+            dst = T.cores[(rank - 1 - t) % N] if c is None else c
+            es = topo.engines(core, dst)
+            es = es[k * len(es) // len(ps):(k + 1) * len(es) // len(ps)]
+            rid, pid = topo.addr(dst, core)
+            trs.append(RemoteDMATransfer(dst_ids=[DstId(rid=rid, pnc=pid)], dma_engine_mask=_mask(es),
+                                         remote_sem=T.sem["in%s%d" % (kind, t)],
+                                         src=B(name, (at + lo, at + hi))[0], dst=T["z_" + _copy(kind, t)][:, lo:hi]))
+            n += len(es)
+        sem = "lo%s%d" % (kind, t)
+        g.remote_dma_fused(trs, local_sem=T.sem[sem])
         total[sem] = n
-        clk[(sem, n)] = {}
-        hist[name] = [((1 << 64) - 1, True, sem, n, "r")]
+        record("g", (src,), (), sem, n, sem)
 
     vec, act, pe = g.vector, g.scalar, g.tensor
 
@@ -200,17 +241,20 @@ def rank_program(g, core, T, topo):
     def scat(win, off, in_):
         op("v", lambda: vec.tensor_copy(win[0].indirect(off[0]), in_[0]), win, off, in_)
 
+    def scat_add(win, off, a, b):
+        op("v", lambda: vec.tensor_tensor(win[0].indirect(off[0]), a[0], b[0], A.add), win, off, a, b)
+
     def fill(out, c):
         op("v", lambda: vec.memset(out[0], c), out)
 
     def ac(out, in_, f, bias=0.0, scale=1.0):
-        if isinstance(scale, tuple):
-            op("s", lambda: act.activation(out[0], in_[0], f, bias=bias, scale=scale[0]), out, in_, scale)
-        else:
-            op("s", lambda: act.activation(out[0], in_[0], f, bias=bias, scale=scale), out, in_)
+        cols = [s for s in (bias, scale) if isinstance(s, tuple)]
+        b = bias[0] if isinstance(bias, tuple) else bias
+        s = scale[0] if isinstance(scale, tuple) else scale
+        op("s", lambda: act.activation(out[0], in_[0], f, bias=b, scale=s), out, in_, *cols)
 
-    def agat(out, win, off, bias=0.0, scale=1.0):
-        op("s", lambda: act.activation(out[0], win[0].indirect(off[0]), AF.Identity, bias=bias, scale=scale), out, win, off)
+    def agat(out, win, off):
+        op("s", lambda: act.activation(out[0], win[0].indirect(off[0]), AF.Copy), out, win, off)
 
     def mm(out, l, r, start, stop):
         op("t", lambda: pe.matmul(out[0], l[0], r[0], start, stop), out, l, r)
@@ -221,126 +265,146 @@ def rank_program(g, core, T, topo):
         else:
             op("g", lambda: g.iota(out[0], pattern, base, mult, allow_small_or_imprecise_dtypes=True), out)
 
-    def send(dst, name, sem, cols=None):
-        hop = _relay(topo, core, dst)
-        src = B(name) if cols is None else B(name, (0, cols[1]))
-        wait("g", deps("g", (src,), ()))
-        n = _send(g, T, topo, core, dst if hop is None else hop, name, sem, cols)
-        total["loc"] = total.get("loc", 0) + n
+    def rows8(b, *idx):
+        full = (slice(0, 8),) + tuple(slice(*i) for i in idx)
+        return (T["z_" + b][full], b, B(b, *idx)[2])
+
+    def lm(m, name="zl"):
+        return B(name, (15 - m, 143 - m))
+
+    lists = B("pt", (LP, LP + V))
 
     dma("y", B("q")[0], T.qs[:], (), (B("q"),))
-    dma("s", B("x", (PAD, PAD + H))[0], T.x[:], (), (B("x", (PAD, PAD + H)),))
-    dma("y", B("pti")[0], T.towns[:], (), (B("pti"),))
-    dma("y", T.z_moi[0:8, :], T.mo[:], (), (B("moi"),))
-    dma("y", B("thi")[0], T.th[:], (), (B("thi"),))
+    dma("s", B("pti", (LP, LP + V))[0], T.towns[:], (), (B("pti", (LP, LP + V)),))
+    dma("y", B("x", (PAD, PAD + H))[0], T.x[:], (), (B("x", (PAD, PAD + H)),))
+    dma("s", T.z_moi[0:8, :], T.mo[:], (), (B("moi"),))
+    fill(B("pti", (0, LP)), 0)
+    dma("y", B("pti", (LP - 1, LP))[0], T.th[:], (), (B("pti", (0, LP)),))
     AND, SHR = A.bitwise_and, A.arith_shift_right
     iota(B("pc"), [[1, 1]], 0, 1)
-    iota(B("nt"), [[1, 16], [0, 16]])
-    iota(B("it"), [[0, 16], [1, 16]])
     iota(B("ef"), [[1, 256]])
-    fill(B("lm"), 0.0)
     fill(B("one"), 1.0)
-    op("g", lambda: g.affine_select(B("id")[0], B("one")[0], [[-1, 128]], A.is_equal, 0.0, 0, 1), B("id"), B("one"))
-    iota(B("ci"), [[0, 16], [1, 16]], 1)
-    iota(B("ios"), [[1, 64]])
+    iota(B("nt"), [[1, 16], [0, 16]])
+    op("g", lambda: g.affine_select(B("id")[0], B("one", (0, 128))[0], [[-1, 128]], A.is_equal, 0.0, 0, 1), B("id"), B("one"))
+    iota(B("it"), [[0, 16], [1, 16]])
     ts(B("pmi"), B("pc"), 15, AND)
     ts(B("pgi"), B("pc"), 4, SHR)
     ts(B("podd"), B("pc"), 1, AND)
     cp(B("pg"), B("pgi"))
+    ts(B("pz"), B("pgi"), 16.0, A.mult, 15.0, A.add)
     ts(B("evc"), B("podd"), -1.0 / 32, A.mult, 1.0 / 32, A.add)
     cp(B("pm"), B("pmi"))
     cp(B("pf"), B("pc"))
+    ts(B("t16", (0, 1)), B("pc"), 16.0, A.mult, 15.0, A.add)
+    fill(B("x", (0, PAD)), 0.0)
+    fill(B("x", (PAD + H, TRX)), 0.0)
     e128, i128, n128 = B("ef", (0, 128)), B("it", (0, 128)), B("nt", (0, 128))
-    ts(B("bo"), n128, B("pg"), A.is_equal)
-    for m in range(16):
-        ac(B("lm", m, (m, 128, 16)), B("bo", (m, 128, 16)), AF.Copy, scale=32.0)
-    ts(B("resn"), B("it"), 0.5, A.is_lt, 2 * BIG, A.mult)
-    ts(B("resn"), B("resn"), -BIG, A.add)
+    ts(B("zl"), B("ef", (0, 144)), B("pz"), A.is_equal, 32.0, A.mult)
+    ts(B("zw"), B("zl"), B("evc"), A.mult)
     ts(B("j2"), B("ef", (0, 16)), 16.0, A.mult, B("pm"), A.add)
+    ts(B("z8"), B("ef", (0, 144)), B("t16", (0, 1)), A.is_equal)
     cp(B("jb"), B("j2"))
-    ts(B("rj"), B("j2"), -1.0, A.mult, 255.0, A.add)
+    ts(B("rj"), B("j2"), -1.0, A.mult, 511.0, A.add)
     ts(B("trx"), B("j2"), float(TRX), A.add)
     for s in range(2):
         ts(B("trp", (16 * s, 16 * s + 16)), B("j2"), float(TRP), A.add)
     ts(B("j2"), B("j2"), 2.0, A.mult)
+    ts(B("bo"), n128, B("pg"), A.is_equal)
+    ts(B("e8"), n128, B("pf"), A.is_equal)
     ac(B("nid"), B("id"), AF.Copy, scale=-1.0)
-    ac(B("nbo"), B("bo"), AF.Copy, scale=-1.0)
-    op("g", lambda: g.affine_select(B("ntri")[0], B("nbo")[0], [[1, 128]], A.is_gt, 0.0, 0, -1), B("ntri"), B("nbo"))
-    ac(B("id14"), B("id"), AF.Copy, scale=1424.0)
-    ac(B("idf"), B("id"), AF.Copy)
-    ts(B("resx"), B("it"), 0.5, A.is_lt, -BIG - 2.0, A.mult)
-    ts(B("resx"), B("resx"), 2.0, A.add)
-    fill(B("x", (0, PAD)), 0.0)
-    fill(B("x", (PAD + H, TRX)), 0.0)
 
-    def qrep_v(lo, hi):
-        for i in range(lo, hi):
-            cp(B("qrep", (i, 4096, 16)), B("q"))
-
-    def qrep_s():
-        for i in range(16 - QA, 16):
+    def qrep(nv):
+        for i in range(nv, 16):
             ac(B("qrep", (i, 4096, 16)), B("q"), AF.Copy)
+        for i in range(nv):
+            cp(B("qrep", (i, 4096, 16)), B("q"))
 
     par = B("b1", (256, 272))
 
     def parity(last):
         for m in range(16):
-            mm(par, B("wem", m), B("q", (m, 256, 16)), m == 0, last and m == 15)
+            mm(par, lm(m, "zw"), B("q", (m, 256, 16)), m == 0, last and m == 15)
 
-    qrep_v(0, 5)
-    ts(B("wem"), B("lm"), B("evc"), A.mult)
     parity(True)
-    op("v", lambda: vec.tensor_copy(T.z_mo8[0:8, :, :], T.z_moi[0:8, :]), B("mo8"), B("moi"))
-    op("v", lambda: vec.tensor_scalar(T.z_e8[0:8, :], T.z_nt[0:8, 0:128], T.z_pf[0:8, 0:1], None, A.is_equal), B("e8"), B("nt"), B("pf"))
-    op("t", lambda: pe.matmul(B("b4")[0], T.z_e8[0:8, :], T.z_mo8[0:8, :, :], True, True), B("b4"), B("e8"), B("mo8"))
-    qrep_s()
-    qrep_v(5, 16 - QA)
-    cp(B("pt", (0, V)), B("pti"))
-
-    def first_mothers():
-        ts(B("dm"), B("it"), B("pm"), A.is_equal)
-        ts(B("resa"), B("it"), 0.5, A.is_gt)
-        for s in range(2):
-            tt(B("mt"), B("b4", (0, 16), (s, 32, 2)), B("dm"), A.mult)
-            scan(B("ms"), B("resa"), B("mt"), A.mult, A.add)
-            cp(B("moh", (0, 16), s), B("ms", (15, 256, 16)))
-        tt(B("dmo"), B("moh", (0, 16), 1), B("moh", (0, 16), 0), A.subtract)
+    qrep(QV0)
+    cp(rows8("mo8"), rows8("moi"))
+    for m in range(16):
+        mm(B("b7", (0, 32)), rows8("z8", (15 - m, 143 - m)), rows8("mo8", (0, 16), (2 * m, 2 * m + 2)), m == 0, m == 15)
+    mm(B("b4"), rows8("e8"), rows8("mo8"), True, True)
+    ac(B("moh"), B("b7", (0, 32)), AF.Copy)
+    cp(B("pt", (0, LP + V)), B("pti"))
+    send("p", 0)
+    send("x", 0)
+    ts(B("ci"), B("it"), 1.0, A.add)
+    tt(B("dmo"), B("moh", (0, 16), 1), B("moh", (0, 16), 0), A.subtract)
 
     def late_constants():
-        ts(B("dcol"), B("ef", (0, 16)), B("pm"), A.is_equal)
-        ts(B("th32"), B("thi"), 32.0, A.mult)
-        ts(B("th2k"), B("thi"), 2048.0, A.mult)
+        ts(B("resn"), B("it"), 0.5, A.is_lt, 2 * BIG, A.mult)
+        ts(B("resx"), B("it"), 0.5, A.is_lt, -BIG - 2.0, A.mult)
+        ts(B("th32"), B("pt", (LP - 1, LP)), 32.0, A.mult)
         ts(B("t16", (0, 1)), B("podd"), -2.0, A.mult, 1.0, A.add)
+        ts(B("resn"), B("resn"), -BIG, A.add)
+        ts(B("resx"), B("resx"), 2.0, A.add)
         tt(B("t16", (0, 1)), B("t16", (0, 1)), B("pf"), A.add)
+        ts(B("thb"), B("th32"), MID, A.add)
+        fill(B("thq"), MID)
         ts(B("sw"), e128, B("t16", (0, 1)), A.is_equal)
+        ts(B("thq", (0, 16)), B("jb"), 0.0, A.mult, B("th32"), A.add)
         tt(B("swd"), B("sw"), B("id"), A.subtract)
-        ts(B("sg"), i128, B("pm"), A.is_equal)
-        fill(B("zz"), 0.0)
-        fill(B("cs"), 0.0)
-        ts(B("trib"), B("it"), B("pm"), A.is_ge, 1024.0, A.mult)
         ts(B("pidx"), B("pm"), 1.0, A.add)
         ts(B("widx"), B("pm"), -1.0, A.mult, 31.0, A.add)
-        cp(B("expl"), B("ios", (0, 16)))
-        ts(B("t16", (0, 1)), B("pm"), 16.0, A.mult, 16.0, A.add)
+        ts(B("nbo"), B("bo"), -1.0, A.mult)
+        fill(B("zz"), 0.0)
+        fill(B("cs"), 0.0)
+        op("g", lambda: g.affine_select(B("ntri")[0], B("nbo")[0], [[1, 128]], A.is_gt, 0.0, 0, -1), B("ntri"), B("nbo"))
+        iota(B("plw", (256, 512)), [[0, 256]])
+        iota(B("fw", (CAP, 512)), [[0, 512 - CAP]])
+        iota(B("gw", (CAP, 512)), [[0, 512 - CAP]])
+        iota(B("flw", (0, CAP)), [[0, CAP]])
+        iota(B("flw", (CAP, CAP + 1024)), [[0, 1024]], -2)
+
+    def later_constants():
+        ts(B("oh", (0, 16)), B("ef", (0, 16)), B("pidx"), A.is_equal)
+        ts(B("oh", (16, 32)), B("ef", (16, 32)), B("widx"), A.is_equal)
+        ts(B("dm"), B("it", (0, 64)), B("pm"), A.is_equal)
+        ts(B("resa"), B("it", (0, 64)), 0.5, A.is_gt)
+        ts(B("dcol"), B("ef", (0, 16)), B("pm"), A.is_equal)
+        ts(B("sg"), i128, B("pm"), A.is_equal)
+        ts(B("trib"), B("it"), B("pm"), A.is_ge, 1024.0, A.mult)
+        ts(B("t16", (0, 1)), B("pm"), 16.0, A.mult, float(CAP), A.add)
+        ts(B("id14"), B("id"), 1424.0, A.mult)
         ts(B("um"), B("nt", (0, 64)), 256.0, A.mult, B("t16", (0, 1)), A.add)
+        ts(B("idk"), B("id"), -1024.0, A.mult)
         tt(B("pcg"), B("um"), B("it", (0, 64)), A.add)
-        fill(B("dg", (0, 16)), -512.0)
-        fill(B("fw", (64, 256)), 0.0)
-        fill(B("gw", (64, 256)), 0.0)
+        cp(B("trph"), B("trp", (0, 16)))
 
     xwin = B("x", (PAD, TRX))
     u0, u1 = B("uf", (0, 16)), B("uf", (16, 32))
-    k0, k1 = B("b0", (0, 256)), B("b1", (0, 256))
-    best0, best1 = B("sc", (15, 256, 16)), B("sc", (271, 512, 16))
+    k0, k1, k2 = B("b0", (0, 256)), B("b1", (0, 192)), B("b0", (256, 320))
+    best0, best1 = B("sc", (15, 256, 16)), B("sc", (527, 768, 16))
+    ok0, h = B("ok", (0, 16)), B("ok", (16, 32))
 
+    def towns_a():
+        cp(B("bi"), par)
+
+    def towns_b():
+        ts(B("bq"), B("bi"), 1, AND)
+
+    def towns_c():
+        tt(B("t16"), B("bq"), B("dmo"), A.mult)
+        tt(u0, B("bq"), B("j2"), A.add)
+
+    def towns_d():
+        tt(u1, B("t16"), B("moh", (0, 16), 0), A.add)
+        cp(B("uu"), B("uf"))
+
+    towns_a()
+    towns_b()
+    towns_c()
+    towns_d()
     for t in range(R_):
         end = t == R_ - 1
-        guest, host_of = T.cores[(rank - 1 - t) % N], T.cores[(rank + 1 + t) % N]
-        pk, pkr, rs, rr = "pk%d" % t, "pkr%d" % t, "rs%d" % t, "rr%d" % t
-
-        def came_from(src):
-            hop = _relay(topo, src, core)
-            return src if hop is None else hop
+        xr, pr = "xr%d" % t, "pr%d" % t
 
         def diff(k, parts=(0, 1)):
             lo, hi = 2 * k + parts[0], 2 * k + parts[-1] + 1
@@ -351,215 +415,217 @@ def rank_program(g, core, T, topo):
             lo, hi = 2 * k + parts[0], 2 * k + parts[-1] + 1
             ac(B("ad", (2 * lo, 2 * hi)), B("d", (512 * lo, 512 * hi)), AF.Abs)
 
+        def raw(k):
+            agat(B("d", (1024 * k, 1024 * k + 1024)), xwin, B("li", (64 * k, 64 * k + 64)))
+            for a in range(2):
+                r = (2 * k + a) % 8
+                mm(B("b%d" % (2 + a)), B("nid"), B("qrep", (512 * r, 512 * r + 512)), True, False)
+                mm(B("b%d" % (2 + a)), B("id"), B("d", (512 * (2 * k + a), 512 * (2 * k + a + 1))), False, True)
+
+        def raw_abs(k):
+            for a in range(2):
+                ac(B("ad", (4 * k + 2 * a, 4 * k + 2 * a + 2)), B("b%d" % (2 + a)), AF.Abs)
+
         def reduce(k):
             s, c = k // 4, k % 4
-            out = B("b%d" % s, (64 * c, 64 * c + 64))
-            mm(out, B("id"), B("ci", (64 * c, 64 * c + 64)), True, False)
+            out = k2 if k == 7 else B("b%d" % s, (64 * c, 64 * c + 64))
+            mm(out, B("id"), B("ci", (0, 64)), True, False)
             for m in range(16):
-                mm(out, B("lm", m), B("ad", (4 * k, 4 * k + 4), m), False, m == 15)
+                mm(out, lm(m), B("ad", (4 * k, 4 * k + 4), m), False, m == 15)
 
-        cp(B("bi"), par)
-        ts(B("bq"), B("bi"), 1, AND)
-        tt(u0, B("bq"), B("j2"), A.add)
+        def entries(s):
+            r = (32 * s, 32 * s + 32)
+            tt(B("kc", r), B("sc", (512 * s + 15, 512 * s + 512, 16)), B("thq", r), A.min)
+            ts(B("ke", r), B("kc", r), 31, AND)
+            cp(B("eu", r), B("ke", r))
 
-        def second_town():
-            tt(B("t16"), B("bq"), B("dmo"), A.mult)
-            tt(u1, B("t16"), B("moh", (0, 16), 0), A.add)
-
-        if t == 0:
-            cp(B("uu", (0, 16)), u0)
-            gat(B("li", (0, 256)), B("pt", (0, V)), B("uu", (0, 16)))
-        else:
-            second_town()
-            cp(B("uu"), B("uf"))
-            gat(B("li"), B("pt", (0, V)), B("uu"))
-        agat(B("xg"), xwin, B("li", (0, 64)))
-        for a in range(2):
-            mm(B("b%d" % (2 + a)), B("nid"), B("qrep", (512 * a, 512 * a + 512)), True, False)
-            mm(B("b%d" % (2 + a)), B("id"), B("xg", (512 * a, 512 * a + 512)), False, True)
+        gat(B("li"), lists, B("uu"))
+        iota(B("pk", (0, CAP)), [[0, CAP]], 512)
+        iota(B("plw", (0, 256)), [[1, 256]], 1216 + CAP * t)
+        raw(0)
         diff(1)
         absd(1)
-        if t == 0:
-            first_mothers()
-            second_town()
-            cp(B("uu", (16, 32)), u1)
-            gat(B("li", (256, 512)), B("pt", (0, V)), B("uu", (16, 32)))
-        for a in range(2):
-            ac(B("ad", (2 * a, 2 * a + 2)), B("b%d" % (2 + a)), AF.Abs)
+        raw_abs(0)
         reduce(1)
         reduce(0)
         diff(2)
-        if t == 0:
-            ac(B("m256"), B("b4"), AF.Copy, scale=256.0)
         absd(2)
+        raw(4)
         reduce(2)
         diff(3)
         absd(3)
         reduce(3)
-        diff(4)
-        absd(4)
-        reduce(4)
         if t == 0:
             late_constants()
-        tt(B("du"), B("uf"), B("trp"), A.subtract)
-        ac(B("u1h"), u1, AF.Copy)
         diff(5)
+        raw_abs(4)
+        reduce(4)
         absd(5)
+        ac(B("u1h"), u1, AF.Copy)
         reduce(5)
-        scan(B("sc", (0, 256)), B("resn"), k0, A.max, A.min)
-        ts(B("okt", (0, 16)), best0, B("th32"), A.is_lt)
-        ts(B("f0"), B("okt", (0, 16)), -1.0, A.mult, 1.0, A.add)
+        if t == 0:
+            later_constants()
         diff(6)
         absd(6)
+        reduce(6)
+        scan(B("sc", (0, 256)), B("resn"), k0, A.max, A.min)
+        scan(B("sc", (256, 512)), B("resx"), k0, A.add, A.max)
+        ts(B("f0"), best0, B("th32"), A.is_ge)
         mm(B("b6", (48, 64)), B("swd"), B("u1h"), True, True)
         mm(B("b6", (64, 80)), B("sw"), B("f0"), True, True)
-        reduce(6)
         for hf in range(2):
             diff(7, (hf,))
             absd(7, (hf,))
         reduce(7)
-        tt(B("xk"), B("b6", (64, 80)), B("f0"), A.mult)
-        tt(B("du", (0, 16)), B("du", (0, 16)), B("f0"), A.mult)
-        tt(B("dl"), B("b6", (48, 64)), B("xk"), A.mult)
-        scan(B("sw2", (0, 256)), B("resx"), k0, A.add, A.max)
-        tt(B("d1"), B("dl"), B("bq"), A.mult)
-        tt(B("d0"), B("dl"), B("d1"), A.subtract)
-        tt(B("moh", (0, 16), 1), B("moh", (0, 16), 1), B("d1"), A.add)
-        tt(B("moh", (0, 16), 0), B("moh", (0, 16), 0), B("d0"), A.add)
-        ts(B("kc", (0, 16)), best0, B("th32"), A.min)
-        ts(B("ke", (0, 16)), B("kc", (0, 16)), 31, AND)
-        cp(B("ewa", (0, 16)), B("ke", (0, 16)))
-        tt(B("dmo"), B("moh", (0, 16), 1), B("moh", (0, 16), 0), A.subtract)
-        gat_tt(B("vv"), B("m256"), B("uu", (16, 32)), B("q"), A.add)
-        scan(B("sc", (256, 512)), B("resn"), k1, A.max, A.min)
-        ts(B("okt", (16, 32)), best1, B("th32"), A.is_lt)
-        tt(B("h"), B("okt", (0, 16)), B("okt", (16, 32)), A.max)
-        scan(B("cs", (1, 17)), B("h"), B("zz"), A.add, A.add)
-        tt(B("hj"), B("h"), B("rj"), A.mult)
+        if t == 0:
+            ac(B("mw"), B("b4"), AF.Copy, scale=1024.0)
+        agat(B("lif"), lists, B("uu"))
+        ac(B("lic"), B("lif"), AF.Identity, bias=-44.0, scale=1.0 / 32)
+        ts(B("thl"), B("f0"), -MID, A.mult, B("thb"), A.add)
+        ts(B("thq", (32, 48)), B("f0"), B("th32"), A.mult)
+        scan(B("sc", (512, 704)), B("resn", (0, 192)), k1, A.max, A.min)
+        scan(B("sc", (768, 960)), B("resx", (0, 192)), k1, A.add, A.max)
+        gat_tt(B("vv"), B("mw"), B("uu", (16, 32)), B("q"), A.add)
+        scan(B("sc", (704, 768)), B("resn", (0, 64)), k2, A.max, A.min)
+        tt(h, best1, B("thl"), A.is_lt)
+        scan(B("sc", (960, 1024)), B("resx", (0, 64)), k2, A.add, A.max)
+        scan(B("cs", (1, 17)), h, B("zz"), A.add, A.add)
+        tt(B("hj"), h, B("rj"), A.mult)
         off = B("b6", (16, 32))
         mm(off, B("id"), B("jb"), True, False)
-        mm(off, B("ntri"), B("h"), False, False)
+        mm(off, B("ntri"), h, False, False)
         mm(off, B("nbo"), B("cs", (0, 16)), False, False)
         mm(off, B("id"), B("hj"), False, True)
-        ts(B("kc", (16, 32)), best1, B("th32"), A.min)
-        ts(B("ke", (16, 32)), B("kc", (16, 32)), 31, AND)
-        tt(B("ewa", (16, 32)), B("ke", (16, 32)), B("f0"), A.mult)
-        ac(B("un"), B("h"), AF.Identity, bias=1.0, scale=-1.0)
-        mm(B("b6", (32, 33)), B("bo"), B("cs", (16, 17)), True, True)
+        tt(B("kc"), B("sc", (15, 1024, 16)), B("thq"), A.min)
+        ts(B("ke"), B("kc"), 31, AND)
         cp(B("offu"), off)
-        scat(B(pk, (0, 256)), B("offu"), B("vv"))
-        send(host_of, pk, "rq%d" % t, (pkr, 64))
-        agat(B("lic"), B("pt", (0, V)), B("uu"), bias=-44.0, scale=1.0 / 32)
-        if t == 0:
-            for m in range(16):
-                ac(B("bm", m), B("bo"), AF.Copy, scale=B("dcol", (m, m + 1)))
-        for m in range(16):
-            mm(B("b2", (m, 512, 16)), B("bm", m), B("ewa"), True, True)
-        ac(B("plf"), off, AF.Identity, bias=(1216.0 + 64 * t) / 32, scale=1.0 / 32)
-        tt(B("pl"), B("plf"), B("un"), A.mult)
-        ts(B("capf"), B("ios"), B("b6", (32, 33)), A.add, 256.0, A.is_lt)
-        ac(B("cap"), B("capf"), AF.Identity, bias=-1.0, scale=256.0)
-        ts(B("b3"), B("b2"), B("pidx"), A.is_equal)
-        tt(B("ns"), B("b3"), B("lic"), A.mult)
-        scan(B("sw2", (256, 512)), B("resx"), k1, A.add, A.max)
-        ts(B("wi"), B("sw2", (15, 512, 16)), -64.0, A.max)
-        ts(B("we"), B("wi"), 31, AND)
-        cp(B("ewb"), B("we"))
-        num = B("b6", (80, 96))
-        for m in range(16):
-            for s in range(2):
-                mm(num, B("lm", m), B("ns", (256 * s + m, 256 * s + 256, 16)), m == 0 and s == 0, False)
-        mm(num, B("id14"), B("h"), False, True)
-        for m in range(16):
-            mm(B("b7", (m, 512, 16)), B("bm", m), B("ewb"), True, True)
-        vp = B("b5", (0, 256))
-        for s in range(2):
-            mm(vp, B("bo"), B("ns", (256 * s, 256 * s + 256)), s == 0, False)
-        for m in range(16):
-            mm(B("b5", (m, 256, 16)), B("bm", m), B("pl"), False, m == 15)
-        cp(B("numu"), num)
-        ac(B("numc"), num, AF.Identity, bias=-44.5, scale=1.0 / 32)
-        ac(B("numf"), num, AF.Copy)
-        gat_tt(B("sh"), B("x", (0, TRX)), B("numu"), B("q"), A.add)
-        ts(B("rn"), B("sh"), 1, SHR)
-        arrived(pkr, "rq%d" % t, came_from(guest), core)
-        ts(B("qi"), B(pkr), 255, AND)
+        cp(B("eu"), B("ke"))
+        scat(B("pk"), B("offu"), B("vv"))
+        ac(B("un"), h, AF.Identity, bias=1.0, scale=-1.0)
+        ac(ok0, B("f0"), AF.Identity, bias=1.0, scale=-1.0)
+        op("s", lambda: act.activation(B("plg")[0], B("plw")[0].indirect(B("offu")[0]), AF.Copy, scale=1.0 / 32), B("plg"), B("plw"), B("offu"))
+        ts(B("qi"), B("pk", (0, CAP)), 1023, AND)
+        ts(B("u2i"), B("pk", (0, CAP)), 10, SHR)
         cp(B("qb"), B("qi"))
-        for i in range(5, 16):
+        tt(B("um"), B("u2i"), B("dm"), A.mult)
+        for i in range(GV, 16):
             ac(B("qg", (i, 1024, 16)), B("qb"), AF.Copy)
-        ts(B("u2i"), B(pkr), 8, SHR)
-        tt(B("um"), B("u2i"), B("dm", (0, 64)), A.mult)
-        scan(B("us"), B("resa", (0, 64)), B("um"), A.mult, A.add)
+        gat_tt(B("ns", (0, 256)), B("oh"), B("eu", (0, 16)), B("lic", (0, 256)), A.mult)
+        scan(B("us"), B("resa"), B("um"), A.mult, A.add)
+        gat_tt(B("ns", (256, 512)), B("oh"), B("eu", (32, 48)), B("lic", (256, 512)), A.mult)
         cp(B("u2u"), B("us", (15, 64, 16)))
-        gat(B("lig"), B("pt", (0, V)), B("u2u"))
-        for i in range(5):
+        num = B("b7", (0, 16))
+        mm(num, B("id14"), h, True, False)
+        for s in range(2):
+            for m in range(16):
+                mm(num, lm(m), B("ns", (256 * s + m, 256 * s + 256, 16)), False, s == 1 and m == 15)
+        for i in range(GV):
             cp(B("qg", (i, 1024, 16)), B("qb"))
+        for kind in KINDS:
+            arrived(kind, t)
+        gat(B("lig"), B(pr, (LP, LP + V)), B("u2u"))
+        ac(B("dg", (0, CAP)), B("qb"), AF.Copy, scale=-1.0)
+        ac(B("numc"), num, AF.Identity, bias=-44.5, scale=1.0 / 32)
+        dd = B("b5", (0, 256))
+        mm(dd, B("nid"), B("trib"), True, False)
+        mm(dd, B("nid"), B("plg"), False, False)
+        for s in range(2):
+            mm(dd, B("nbo"), B("ns", (256 * s, 256 * s + 256)), False, False)
+        for m in range(16):
+            mm(B("b5", (m, 256, 16)), B("id"), B("numc"), False, m == 15)
+        cp(B("numu"), num)
         for hf in range(2):
-            gat_tt(B("dg", (16 + 512 * hf, 528 + 512 * hf)), xwin, B("lig", (32 * hf, 32 * hf + 32)), B("qg", (512 * hf, 512 * hf + 512)), A.subtract)
-            ac(B("adg", (2 * hf, 2 * hf + 2)), B("dg", (16 + 512 * hf, 528 + 512 * hf)), AF.Abs, scale=64.0)
-        gk = B("b1", (0, 64))
+            r = (CAP + 512 * hf, CAP + 512 * hf + 512)
+            gat_tt(B("dg", r), B(xr, (0, H + CAP * t)), B("lig", (32 * hf, 32 * hf + 32)), B("qg", (512 * hf, 512 * hf + 512)), A.subtract)
+            ac(B("adg", (2 * hf, 2 * hf + 2)), B("dg", r), AF.Abs, scale=64.0)
+            if hf == 0:
+                ac(B("da"), dd, AF.Abs, scale=float(2 ** 17))
+        gk = B("b0", (320, 384))
         mm(gk, B("id"), B("pcg"), True, False)
         for m in range(16):
-            mm(gk, B("lm", m), B("adg", (0, 4), m), False, m == 15)
-        ts(B("b3"), B("b7"), B("widx"), A.is_equal)
+            mm(gk, lm(m), B("adg", (0, 4), m), False, m == 15)
         for s in range(2):
-            tt(B("dv", (256 * s, 256 * s + 256)), vp, B("lic", (256 * s, 256 * s + 256)), A.subtract)
-        tt(B("wd"), B("b3"), B("dv"), A.mult)
-        tt(B("nrb"), vp, B("trib"), A.add)
-        scan(B("sg2"), B("resn", (0, 64)), gk, A.max, A.min)
-        ts(B("gkc"), B("sg2", (15, 64, 16)), B("th2k"), A.min)
-        ts(B("gpos"), B("gkc"), 2047, AND)
-        cp(B("posu"), B("gpos"))
-        gat_tt(B(rs), B("dg"), B("posu"), B("qb"), A.add)
-        send(guest, rs, "rp%d" % t, (rr, 64))
-        for m in range(16):
-            mm(B("b4", (0, 16), (2 * m, 2 * m + 2)), B("bm", m), B("moh"), True, True)
-        mm(B("b7"), B("id"), B("lic"), True, False)
-        mm(B("b7"), B("idf"), B("wd"), False, True)
-        if not end:
-            ac(B("m256"), B("b4"), AF.Copy, scale=256.0)
-        else:
-            ac(B("ym2"), B("b4"), AF.Copy)
-            dma("y", T.ym[:], T.z_ym2[0:128:16, :], (B("ym2"),), ())
-        ac(B("nl"), B("b7"), AF.Identity, bias=1408.0, scale=32.0)
-        gat_tt(B("e"), B("numc"), B("expl"), B("nrb"), A.is_equal)
-        scan(B("cnt"), B("resa"), B("e"), A.mult, A.add)
-        ts(B("l0"), B("cnt", (15, 256, 16)), 0.5, A.is_ge)
-        tt(B("l0"), B("l0"), B("un"), A.max)
-        tt(B("lt"), B("l0"), B("trx"), A.mult)
-        tt(B("xo"), B("lt"), B("numf"), A.max)
+            dv = B("b2", (256 * s, 256 * s + 256))
+            mm(dv, B("nid"), B("lic", (256 * s, 256 * s + 256)), True, False)
+            mm(dv, B("id"), B("plg"), False, False)
+            for a in range(2):
+                mm(dv, B("bo"), B("ns", (256 * a, 256 * a + 256)), False, a == 1)
+        gat_tt(B("sh"), B("x", (0, TRX)), B("numu"), B("q"), A.add)
+        ac(B("th2k"), B(pr, (LP - 1, LP)), AF.Copy, scale=2048.0)
+        ac(B("rnh"), B("sh"), AF.Identity, bias=1279.75, scale=0.5)
+        ac(B("thp"), B("jb", (0, 4)), AF.Identity, bias=B("th2k"))
+        ac(B("rn"), B("rnh"), AF.Identity, bias=-1280.0)
+        scan(B("am"), B("resn"), B("da"), A.max, A.min)
+        tt(B("xk"), B("b6", (64, 80)), B("f0"), A.mult)
+        tt(B("a2"), B("am", (15, 256, 16)), h, A.mult)
+        tt(B("dl"), B("b6", (48, 64)), B("xk"), A.mult)
+        tt(B("xt"), B("trx"), B("a2"), A.subtract)
+        tt(B("d1"), B("dl"), B("bq"), A.mult)
+        tt(B("xo"), B("xt"), num, A.max)
+        tt(B("d0"), B("dl"), B("d1"), A.subtract)
         cp(B("xoff", (0, 32, 2)), B("xo"))
-        for n in range(15, -1, -1):
-            scat(B("x"), B("xoff", (2 * n, 2 * n + 1)), B("rn", (16 * n, 16 * n + 16)))
-        if end:
-            dma("y", T.yx[:, 0:H + 2 * CAP], B("x", (PAD, PAD + H + 2 * CAP))[0], (B("x", (PAD, PAD + H + 2 * CAP)),), ())
-        arrived(rr, "rp%d" % t, came_from(host_of), core)
-        tt(B("rz"), B(rr), B("cap"), A.min)
-        ts(B("fw", (0, 64)), B("rz"), 0.0, A.is_ge, 1.0 / 512, A.mult)
+        tt(B("moh", (0, 16), 1), B("moh", (0, 16), 1), B("d1"), A.add)
+        scan(B("sg2"), B("resn", (0, 64)), gk, A.max, A.min)
+        tt(B("moh", (0, 16), 0), B("moh", (0, 16), 0), B("d0"), A.add)
+        tt(B("gkc"), B("sg2", (15, 64, 16)), B("thp"), A.min)
+        tt(B("zu"), B("trp"), B("ok"), A.mult)
+        ts(B("gpos"), B("gkc"), 2047, AND)
+        tt(B("dmo"), B("moh", (0, 16), 1), B("moh", (0, 16), 0), A.subtract)
+        cp(B("posu"), B("gpos"))
+        tt(B("ub"), B("zu"), B("uf"), A.max)
+        gat_tt(B("gw", (0, CAP)), B("dg"), B("posu"), B("qb"), A.add)
+        agat(B("fw", (0, CAP)), B("flw"), B("posu"))
         agat(B("c"), B("fw"), B("offu"))
-        ts(B("gw", (0, 64)), B("rz"), 0.0, A.max)
-        gcol = B("x", (PAD + H + CAP * t, PAD + H + CAP * t + CAP))
-        came = B("b6", (96, 112))
+        tr = B("b6", (96, 112))
+        mm(tr, B("id"), B("trph"), True, False)
+        mm(tr, B("idk"), h, False, False)
         for m in range(16):
-            mm(came, B("lm", m), B("c", (m, 256, 16)), m == 0, m == 15)
+            mm(tr, lm(m), B("c", (m, 256, 16)), False, m == 15)
+        gcol = B("x", (PAD + H + CAP * t, PAD + H + CAP * t + CAP))
+        ac(B("dvs"), B("b2"), AF.Copy, scale=32.0)
         if not end:
             gat_tt(B("s1"), B("gw"), B("offu"), B("sh"), A.add)
             ts(B("s2"), B("s1"), 255, AND)
             cp(B("q"), B("s2"))
             parity(False)
-            qrep_s()
-            qrep_v(0, 16 - QA)
-        ac(gcol, B("gw", (0, 64)), AF.Copy)
-        tt(B("got"), B("h"), came, A.max)
+        for n in range(15, -1, -1):
+            scat(B("x"), B("xoff", (2 * n, 2 * n + 1)), B("rn", (16 * n, 16 * n + 16)))
         if not end:
+            send("x", t + 1)
+            qrep(QV)
+        ac(gcol, B("gw", (0, CAP)), AF.Copy)
+        if not end:
+            send("c", t + 1)
+            ts(B("got"), tr, 0.0, A.is_lt)
             mm(par, B("sg"), B("got"), False, True)
-        tt(B("pz", (0, 16)), B("got"), B("du", (0, 16)), A.mult)
-        tt(B("pz", (16, 32)), came, B("du", (16, 32)), A.mult)
-        tt(B("po"), B("pz"), B("trp"), A.add)
-        cp(B("poff"), B("po"))
-        scat(B("pt"), B("poff", (16, 32)), B("nl", (256, 512)))
-        scat(B("pt"), B("poff", (0, 16)), B("nl", (0, 256)))
-    dma("y", T.yx[:, H + 2 * CAP:W], B("x", (PAD + H + 2 * CAP, TRX))[0], (B("x", (PAD + H + 2 * CAP, TRX)),), ())
-    dma("s", T.yp[:], B("pt", (0, V))[0], (B("pt", (0, V)),), ())
+        else:
+            dma("y", T.yx[:], B("x", (PAD, TRX))[0], (B("x", (PAD, TRX)),), ())
+        if t == 0:
+            for m in range(16):
+                ac(B("bm", m), B("bo"), AF.Copy, scale=B("dcol", (m, m + 1)))
+        for m in range(16):
+            mm(B("b4", (0, 16), (2 * m, 2 * m + 2)), B("bm", m), B("moh"), True, True)
+        if not end:
+            ac(B("mw"), B("b4"), AF.Copy, scale=1024.0)
+        else:
+            ac(B("ym2"), B("b4"), AF.Copy)
+            dma("y", T.ym[:], T.z_ym2[0:128:16, :], (B("ym2"),), ())
+        for s in range(2):
+            tt(B("po", (16 * s, 16 * s + 16)), B("ub", (16 * s, 16 * s + 16)), tr, A.max)
+        for s in (1, 0):
+            gat_tt(B("wd", (256 * s, 256 * s + 256)), B("oh"), B("eu", (32 * s + 16, 32 * s + 32)), B("dvs", (256 * s, 256 * s + 256)), A.mult)
+            if s:
+                cp(B("poff"), B("po"))
+        if not end:
+            towns_a()
+        scat_add(B("pt", (LP, LP + V + 256)), B("poff", (16, 32)), B("lif", (256, 512)), B("wd", (256, 512)))
+        if not end:
+            towns_b()
+            towns_c()
+        scat_add(B("pt", (LP, LP + V + 256)), B("poff", (0, 16)), B("lif", (0, 256)), B("wd", (0, 256)))
+        if not end:
+            send("p", t + 1)
+            towns_d()
+    dma("s", T.yp[:], lists[0], (lists,), ())
     for s, v in total.items():
         g.wait_ge(T.sem[s], v)

@@ -8,7 +8,9 @@ TRX, TRP = PAD + W, V
 LP = 8
 BIG = float(2 ** 30)
 MID = float(2 ** 20)
-QV = 0
+Z = 1408
+RAW = {0: ("b2", "b3"), 4: ("b5", "b7")}
+QV, QG = 2, 0
 QV0 = 8
 GV = 5
 
@@ -31,21 +33,21 @@ def _pack(dtype, **kw):
     SCRATCH["t_" + dtype] = ("sbuf", [128, at], dtype)
 
 
-_add("sbuf", "int32", pti=LP + V, moi=V, vv=256, pk=512, s1=256, s2=256)
-_pack("int32", pc=1, pmi=1, pgi=1, podd=1, bi=16, bq=16, kc=64, ke=64, u2i=64, qi=64, gkc=4, gpos=4)
+_add("sbuf", "int32", pti=LP + V, pr0=LP + V, moi=V, s1=256, s2=256)
+_pack("int32", pc=1, pmi=1, pgi=1, podd=1, bi=16, bq=16, kc=64, ke=64, u2i=64, gkc=4, gpos=4)
 _add("sbuf", "uint16", li=512)
 _pack("uint16", uu=32, offu=16, numu=16, xoff=32, poff=32, u2u=4, posu=4, lig=64, eu=64)
-_add("sbuf", "bfloat16", x=TRX + 256, q=256, qrep=4096, d=8192, ad=[32, 16, 16], bm=[16, 128], zl=144, zw=144, ci=256, resn=256,
+_add("sbuf", "bfloat16", x=TRX + 256, q=256, qrep=4096, d=8192, ad=[32, 16, 16], bm=[16, 128], zl=144, zw=144, ci=64, resn=256,
      resx=256, nt=256, qg=1024, dg=CAP + 1024, flw=CAP + 1024, adg=[4, 16, 16], xr0=H, xr1=H + CAP, xr2=H + 2 * CAP, fw=512, gw=512,
-     rn=256)
-_pack("bfloat16", id=128, nid=128, bo=128, nbo=128, ntri=128, id14=128, idk=128, sw=128, swd=128, sg=128, one=144, ef=256, it=256,
-      dm=64, trib=256, resa=64, c=256, da=256, am=256, jb=16, zz=16, ok=32, f0=16, un=16, cs=32, xk=16, qb=64, got=16, oh=32)
+     rn=256, ohw=512)
+_pack("bfloat16", id=128, nid=128, bo=128, nbo=128, ntri=128, idk=128, kp=128, kn=128, sw=128, swd=128, sg=128, one=144, ef=256,
+      it=256, dm=64, trib=256, resa=64, c=256, da=256, am=256, jb=16, zz=16, ok=32, f0=16, cs=32, xk=16, qs=64, qz=64, got=16, oh=32)
 _add("sbuf", "float16", moh=[16, 2], mo8=[16, 32], e8=128, z8=144, pcg=64)
-_pack("float16", lic=512, ns=512, plg=256, rnh=256, u1h=16, rj=16, hj=16, numc=16, trph=16)
-_add("sbuf", "float32", pt=LP + V + 256, pr0=LP + V, pr1=LP + V, pr2=LP + V, mw=V, pf=1, sc=1024, sg2=64, ym2=V, plw=512, lif=512,
-     dvs=512, wd=512, sh=256)
-_pack("float32", pm=1, pg=1, pz=1, pidx=1, widx=1, evc=1, th32=1, thb=1, th2k=1, dcol=16, j2=16, trx=16, trp=32, dmo=16, uf=32, t16=16,
-      dl=16, d1=16, d0=16, thl=16, thq=64, thp=4, a2=16, xt=16, xo=16, um=64, us=64, zu=32, ub=32, po=32)
+_pack("float16", lic=512, ns=512, plg=256, vps=256, rnh=256, u1h=16, rj=16, hj=16, numc=16, trph=16)
+_add("sbuf", "float32", pt=LP + V + 256, pr1=LP + V, pr2=LP + V, mw=V, pf=1, sc=1024, sg2=64, ym2=V, plw=512, t1=512,
+     t2=512, sh=256, pk=512, u2f=256, qf=256)
+_pack("float32", pm=1, pg=1, pz=1, pidx=1, widx=1, evc=1, th32=1, thb=1, th2k=1, c1=1, c2=1, c3=1, dcol=16, j2=16, trx=16, trp=32,
+      dmo=16, uf=32, t16=16, dl=16, d1=16, d0=16, thl=16, thq=64, thp=4, a2=16, xt=16, xo=16, um=64, us=64, zu=32, ub=32, po=32)
 _add("psum", "float32", b0=512, b1=512, b2=512, b3=512, b4=[16, 32], b5=512, b6=512, b7=512)
 KINDS = "xcp"
 SEMAPHORES = (["sv", "sa", "st", "sg"] + ["dma%d" % i for i in range(16)]
@@ -86,7 +88,7 @@ def _copy(kind, t):
 def _hand_on(g, core, T, topo):
     sent = []
     for t in range(R_):
-        for kind in ("px" if t == 0 else KINDS):
+        for kind in (KINDS if t else "px"):
             for r in range(N):
                 ps = _pieces(T, topo, r, t, kind)
                 for c, lo, hi in ps:
@@ -194,7 +196,7 @@ def rank_program(g, core, T, topo):
 
     def send(kind, t):
         ps = _pieces(T, topo, rank, t, kind)
-        name, at = ("pt", 0) if kind == "p" else ("x", PAD)
+        name, at = ("pt" if t else "pti", 0) if kind == "p" else ("x", PAD)
         src = B(name, (at + ps[0][1], at + ps[-1][2]))
         wait("g", deps("g", (src,), ()))
         trs, n = [], 0
@@ -253,8 +255,8 @@ def rank_program(g, core, T, topo):
         s = scale[0] if isinstance(scale, tuple) else scale
         op("s", lambda: act.activation(out[0], in_[0], f, bias=b, scale=s), out, in_, *cols)
 
-    def agat(out, win, off):
-        op("s", lambda: act.activation(out[0], win[0].indirect(off[0]), AF.Copy), out, win, off)
+    def agat(out, win, off, bias=0.0, scale=1.0):
+        op("s", lambda: act.activation(out[0], win[0].indirect(off[0]), AF.Identity, bias=bias, scale=scale), out, win, off)
 
     def mm(out, l, r, start, stop):
         op("t", lambda: pe.matmul(out[0], l[0], r[0], start, stop), out, l, r)
@@ -265,6 +267,9 @@ def rank_program(g, core, T, topo):
         else:
             op("g", lambda: g.iota(out[0], pattern, base, mult, allow_small_or_imprecise_dtypes=True), out)
 
+    def pick(out, in_, pattern, cmp, fill_, base, mult):
+        op("g", lambda: g.affine_select(out[0], in_[0], pattern, cmp, fill_, base, mult), out, in_)
+
     def rows8(b, *idx):
         full = (slice(0, 8),) + tuple(slice(*i) for i in idx)
         return (T["z_" + b][full], b, B(b, *idx)[2])
@@ -273,135 +278,140 @@ def rank_program(g, core, T, topo):
         return B(name, (15 - m, 143 - m))
 
     lists = B("pt", (LP, LP + V))
-
-    dma("y", B("q")[0], T.qs[:], (), (B("q"),))
-    dma("s", B("pti", (LP, LP + V))[0], T.towns[:], (), (B("pti", (LP, LP + V)),))
-    dma("y", B("x", (PAD, PAD + H))[0], T.x[:], (), (B("x", (PAD, PAD + H)),))
-    dma("s", T.z_moi[0:8, :], T.mo[:], (), (B("moi"),))
-    fill(B("pti", (0, LP)), 0)
-    dma("y", B("pti", (LP - 1, LP))[0], T.th[:], (), (B("pti", (0, LP)),))
     AND, SHR = A.bitwise_and, A.arith_shift_right
-    iota(B("pc"), [[1, 1]], 0, 1)
-    iota(B("ef"), [[1, 256]])
-    fill(B("one"), 1.0)
-    iota(B("nt"), [[1, 16], [0, 16]])
-    op("g", lambda: g.affine_select(B("id")[0], B("one", (0, 128))[0], [[-1, 128]], A.is_equal, 0.0, 0, 1), B("id"), B("one"))
-    iota(B("it"), [[0, 16], [1, 16]])
-    ts(B("pmi"), B("pc"), 15, AND)
-    ts(B("pgi"), B("pc"), 4, SHR)
-    ts(B("podd"), B("pc"), 1, AND)
-    cp(B("pg"), B("pgi"))
-    ts(B("pz"), B("pgi"), 16.0, A.mult, 15.0, A.add)
-    ts(B("evc"), B("podd"), -1.0 / 32, A.mult, 1.0 / 32, A.add)
-    cp(B("pm"), B("pmi"))
-    cp(B("pf"), B("pc"))
-    ts(B("t16", (0, 1)), B("pc"), 16.0, A.mult, 15.0, A.add)
-    fill(B("x", (0, PAD)), 0.0)
-    fill(B("x", (PAD + H, TRX)), 0.0)
     e128, i128, n128 = B("ef", (0, 128)), B("it", (0, 128)), B("nt", (0, 128))
-    ts(B("zl"), B("ef", (0, 144)), B("pz"), A.is_equal, 32.0, A.mult)
-    ts(B("zw"), B("zl"), B("evc"), A.mult)
-    ts(B("j2"), B("ef", (0, 16)), 16.0, A.mult, B("pm"), A.add)
-    ts(B("z8"), B("ef", (0, 144)), B("t16", (0, 1)), A.is_equal)
-    cp(B("jb"), B("j2"))
-    ts(B("rj"), B("j2"), -1.0, A.mult, 511.0, A.add)
-    ts(B("trx"), B("j2"), float(TRX), A.add)
-    for s in range(2):
-        ts(B("trp", (16 * s, 16 * s + 16)), B("j2"), float(TRP), A.add)
-    ts(B("j2"), B("j2"), 2.0, A.mult)
-    ts(B("bo"), n128, B("pg"), A.is_equal)
-    ts(B("e8"), n128, B("pf"), A.is_equal)
-    ac(B("nid"), B("id"), AF.Copy, scale=-1.0)
-
-    def qrep(nv):
-        for i in range(nv, 16):
-            ac(B("qrep", (i, 4096, 16)), B("q"), AF.Copy)
-        for i in range(nv):
-            cp(B("qrep", (i, 4096, 16)), B("q"))
-
     par = B("b1", (256, 272))
+    xwin = B("x", (PAD, TRX))
+    u0, u1 = B("uf", (0, 16)), B("uf", (16, 32))
+    k0, k1, k2 = B("b0", (0, 256)), B("b1", (0, 192)), B("b0", (256, 320))
+    best0, best1 = B("sc", (15, 256, 16)), B("sc", (271, 512, 16))
+    ok0, h = B("ok", (0, 16)), B("ok", (16, 32))
+
+    def qrep(q, lo, hi):
+        for i in range(lo, hi):
+            out = B("qrep", (i, 4096, 16))
+            if q == "v":
+                cp(out, B("q"))
+            elif q == "s":
+                ac(out, B("q"), AF.Copy)
+            else:
+                pick(out, B("q"), [[0, 256]], A.is_ge, 0.0, 0, 0)
 
     def parity(last):
         for m in range(16):
             mm(par, lm(m, "zw"), B("q", (m, 256, 16)), m == 0, last and m == 15)
 
+    def towns(step):
+        if step == 0:
+            cp(B("bi"), par)
+        elif step == 1:
+            ts(B("bq"), B("bi"), 1, AND)
+        elif step == 2:
+            tt(B("t16"), B("bq"), B("dmo"), A.mult)
+            tt(u0, B("bq"), B("j2"), A.add)
+        else:
+            tt(u1, B("t16"), B("moh", (0, 16), 0), A.add)
+            cp(B("uu"), B("uf"))
+
+    dma("y", B("q")[0], T.qs[:], (), (B("q"),))
+    dma("s", T.z_moi[0:8, :], T.mo[:], (), (B("moi"),))
+    dma("y", B("pti", (LP, LP + V))[0], T.towns[:], (), (B("pti", (LP, LP + V)),))
+    fill(B("pti", (0, LP)), 0)
+    dma("s", B("pti", (LP - 1, LP))[0], T.th[:], (), (B("pti", (0, LP)),))
+    dma("y", B("x", (PAD, PAD + H))[0], T.x[:], (), (B("x", (PAD, PAD + H)),))
+    iota(B("pc"), [[1, 1]], 0, 1)
+    iota(B("ef"), [[1, 256]])
+    fill(B("one"), 1.0)
+    iota(B("nt", (0, 128)), [[1, 8], [0, 16]])
+    pick(B("id"), B("one", (0, 128)), [[-1, 128]], A.is_equal, 0.0, 0, 1)
+    iota(B("it"), [[0, 16], [1, 16]])
+    iota(B("ci"), [[0, 4], [1, 16]], 1)
+    ts(B("pmi"), B("pc"), 15, AND)
+    ts(B("pgi"), B("pc"), 4, SHR)
+    ts(B("podd"), B("pc"), 1, AND)
+    cp(B("pm"), B("pmi"))
+    cp(B("pg"), B("pgi"))
+    ts(B("pz"), B("pgi"), 16.0, A.mult, 15.0, A.add)
+    ts(B("evc"), B("podd"), -1.0 / 32, A.mult, 1.0 / 32, A.add)
+    cp(B("pf"), B("pc"))
+    ts(B("c1"), B("pc"), 16.0, A.mult, 15.0, A.add)
+    ts(B("c2"), B("podd"), -2.0, A.mult, 1.0, A.add)
+    ts(B("c3"), B("pmi"), 16.0, A.mult, float(CAP), A.add)
+    ts(B("pidx"), B("pmi"), 1.0, A.add)
+    ts(B("widx"), B("pmi"), -1.0, A.mult, 31.0, A.add)
+    fill(B("x", (0, PAD)), 0.0)
+    fill(B("x", (PAD + H, TRX)), 0.0)
+    ts(B("dcol"), B("ef", (0, 16)), B("pm"), A.is_equal)
+    ts(B("zl"), B("ef", (0, 144)), B("pz"), A.is_equal, 32.0, A.mult)
+    ts(B("j2"), B("ef", (0, 16)), 16.0, A.mult, B("pm"), A.add)
+    ts(B("bo"), n128, B("pg"), A.is_equal)
+    for m in range(16):
+        ac(B("bm", m), B("bo"), AF.Copy, scale=B("dcol", (m, m + 1)))
+    ts(B("zw"), B("zl"), B("evc"), A.mult)
+    ts(B("z8"), B("ef", (0, 144)), B("c1"), A.is_equal)
+    ts(B("e8"), n128, B("pf"), A.is_equal)
+    tt(B("c2"), B("c2"), B("pf"), A.add)
+    cp(B("jb"), B("j2"))
+    ts(B("rj"), B("j2"), -1.0, A.mult, 511.0, A.add)
+    ts(B("trx"), B("j2"), float(TRX - PAD - Z), A.add, 16.0, A.mult)
+    for s in range(2):
+        ts(B("trp", (16 * s, 16 * s + 16)), B("j2"), float(TRP), A.add)
+    ts(B("trph"), B("j2"), float(TRP), A.add)
+    ts(B("j2"), B("j2"), 2.0, A.mult)
+    ts(B("nid"), B("id"), -1.0, A.mult)
+    ts(B("nbo"), B("bo"), -1.0, A.mult)
+    pick(B("ntri"), B("nbo"), [[1, 128]], A.is_gt, 0.0, 0, -1)
+    ts(B("sw"), e128, B("c2"), A.is_equal)
+    ts(B("oh", (0, 16)), B("ef", (0, 16)), B("pidx"), A.is_equal)
+    ts(B("oh", (16, 32)), B("ef", (16, 32)), B("widx"), A.is_equal)
+    ts(B("idk"), B("id"), -1024.0, A.mult)
+    ts(B("kp"), B("id"), 128.0, A.mult)
+    ts(B("kn"), B("id"), -128.0, A.mult)
+    tt(B("swd"), B("sw"), B("id"), A.subtract)
+    fill(B("thq"), MID)
+    fill(B("zz"), 0.0)
+    fill(B("cs"), 0.0)
+    fill(B("qz"), 0.0)
+    fill(B("dg", (0, CAP)), 0.0)
+    send("p", 0)
+    send("x", 0)
     parity(True)
-    qrep(QV0)
     cp(rows8("mo8"), rows8("moi"))
     for m in range(16):
         mm(B("b7", (0, 32)), rows8("z8", (15 - m, 143 - m)), rows8("mo8", (0, 16), (2 * m, 2 * m + 2)), m == 0, m == 15)
     mm(B("b4"), rows8("e8"), rows8("mo8"), True, True)
-    ac(B("moh"), B("b7", (0, 32)), AF.Copy)
-    cp(B("pt", (0, LP + V)), B("pti"))
-    send("p", 0)
-    send("x", 0)
-    ts(B("ci"), B("it"), 1.0, A.add)
+    qrep("s", QV0, 16)
+    qrep("v", 0, 4)
+    towns(0)
+    cp(B("moh"), B("b7", (0, 32)))
+    towns(1)
     tt(B("dmo"), B("moh", (0, 16), 1), B("moh", (0, 16), 0), A.subtract)
+    qrep("v", 4, 6)
+    towns(2)
+    qrep("v", 6, QV0)
+    towns(3)
+    ts(B("resn"), B("it"), 0.5, A.is_lt, 2 * BIG, A.mult)
+    gat(B("li"), B("pti", (LP, LP + V)), B("uu"))
+    cp(B("pt", (0, LP + V)), B("pti"))
+    ts(B("resx"), B("it"), 0.5, A.is_lt, -BIG - 2.0, A.mult)
+    ts(B("resn"), B("resn"), -BIG, A.add)
+    ts(B("th32"), B("pt", (LP - 1, LP)), 32.0, A.mult)
+    ts(B("resx"), B("resx"), 2.0, A.add)
+    ts(B("dm"), B("it", (0, 64)), B("pm"), A.is_equal)
+    ts(B("thb"), B("th32"), MID, A.add)
+    ts(B("thq", (0, 16)), B("jb"), 0.0, A.mult, B("th32"), A.add)
+    ts(B("resa"), B("it", (0, 64)), 0.5, A.is_gt)
+    ts(B("sg"), i128, B("pm"), A.is_equal)
+    ts(B("trib"), B("it"), B("pm"), A.is_ge, 1024.0, A.mult)
+    ts(B("um"), B("nt", (0, 64)), 256.0, A.mult, B("c3"), A.add)
+    tt(B("pcg"), B("um"), B("it", (0, 64)), A.add)
+    iota(B("plw", (CAP, 256)), [[0, 256 - CAP]], -PAD - Z)
+    iota(B("plw", (256, 512)), [[0, 256]])
+    iota(B("fw", (CAP, 512)), [[0, 512 - CAP]])
+    iota(B("gw", (CAP, 512)), [[0, 512 - CAP]])
+    iota(B("flw", (0, CAP)), [[0, CAP]])
+    iota(B("flw", (CAP, CAP + 1024)), [[0, 1024]], -2)
 
-    def late_constants():
-        ts(B("resn"), B("it"), 0.5, A.is_lt, 2 * BIG, A.mult)
-        ts(B("resx"), B("it"), 0.5, A.is_lt, -BIG - 2.0, A.mult)
-        ts(B("th32"), B("pt", (LP - 1, LP)), 32.0, A.mult)
-        ts(B("t16", (0, 1)), B("podd"), -2.0, A.mult, 1.0, A.add)
-        ts(B("resn"), B("resn"), -BIG, A.add)
-        ts(B("resx"), B("resx"), 2.0, A.add)
-        tt(B("t16", (0, 1)), B("t16", (0, 1)), B("pf"), A.add)
-        ts(B("thb"), B("th32"), MID, A.add)
-        fill(B("thq"), MID)
-        ts(B("sw"), e128, B("t16", (0, 1)), A.is_equal)
-        ts(B("thq", (0, 16)), B("jb"), 0.0, A.mult, B("th32"), A.add)
-        tt(B("swd"), B("sw"), B("id"), A.subtract)
-        ts(B("pidx"), B("pm"), 1.0, A.add)
-        ts(B("widx"), B("pm"), -1.0, A.mult, 31.0, A.add)
-        ts(B("nbo"), B("bo"), -1.0, A.mult)
-        fill(B("zz"), 0.0)
-        fill(B("cs"), 0.0)
-        op("g", lambda: g.affine_select(B("ntri")[0], B("nbo")[0], [[1, 128]], A.is_gt, 0.0, 0, -1), B("ntri"), B("nbo"))
-        iota(B("plw", (256, 512)), [[0, 256]])
-        iota(B("fw", (CAP, 512)), [[0, 512 - CAP]])
-        iota(B("gw", (CAP, 512)), [[0, 512 - CAP]])
-        iota(B("flw", (0, CAP)), [[0, CAP]])
-        iota(B("flw", (CAP, CAP + 1024)), [[0, 1024]], -2)
-
-    def later_constants():
-        ts(B("oh", (0, 16)), B("ef", (0, 16)), B("pidx"), A.is_equal)
-        ts(B("oh", (16, 32)), B("ef", (16, 32)), B("widx"), A.is_equal)
-        ts(B("dm"), B("it", (0, 64)), B("pm"), A.is_equal)
-        ts(B("resa"), B("it", (0, 64)), 0.5, A.is_gt)
-        ts(B("dcol"), B("ef", (0, 16)), B("pm"), A.is_equal)
-        ts(B("sg"), i128, B("pm"), A.is_equal)
-        ts(B("trib"), B("it"), B("pm"), A.is_ge, 1024.0, A.mult)
-        ts(B("t16", (0, 1)), B("pm"), 16.0, A.mult, float(CAP), A.add)
-        ts(B("id14"), B("id"), 1424.0, A.mult)
-        ts(B("um"), B("nt", (0, 64)), 256.0, A.mult, B("t16", (0, 1)), A.add)
-        ts(B("idk"), B("id"), -1024.0, A.mult)
-        tt(B("pcg"), B("um"), B("it", (0, 64)), A.add)
-        cp(B("trph"), B("trp", (0, 16)))
-
-    xwin = B("x", (PAD, TRX))
-    u0, u1 = B("uf", (0, 16)), B("uf", (16, 32))
-    k0, k1, k2 = B("b0", (0, 256)), B("b1", (0, 192)), B("b0", (256, 320))
-    best0, best1 = B("sc", (15, 256, 16)), B("sc", (527, 768, 16))
-    ok0, h = B("ok", (0, 16)), B("ok", (16, 32))
-
-    def towns_a():
-        cp(B("bi"), par)
-
-    def towns_b():
-        ts(B("bq"), B("bi"), 1, AND)
-
-    def towns_c():
-        tt(B("t16"), B("bq"), B("dmo"), A.mult)
-        tt(u0, B("bq"), B("j2"), A.add)
-
-    def towns_d():
-        tt(u1, B("t16"), B("moh", (0, 16), 0), A.add)
-        cp(B("uu"), B("uf"))
-
-    towns_a()
-    towns_b()
-    towns_c()
-    towns_d()
     for t in range(R_):
         end = t == R_ - 1
         xr, pr = "xr%d" % t, "pr%d" % t
@@ -417,32 +427,37 @@ def rank_program(g, core, T, topo):
 
         def raw(k):
             agat(B("d", (1024 * k, 1024 * k + 1024)), xwin, B("li", (64 * k, 64 * k + 64)))
+
+        def raw_q(k):
             for a in range(2):
                 r = (2 * k + a) % 8
-                mm(B("b%d" % (2 + a)), B("nid"), B("qrep", (512 * r, 512 * r + 512)), True, False)
-                mm(B("b%d" % (2 + a)), B("id"), B("d", (512 * (2 * k + a), 512 * (2 * k + a + 1))), False, True)
+                mm(B(RAW[k][a]), B("nid"), B("qrep", (512 * r, 512 * r + 512)), True, False)
+
+        def raw_x(k):
+            for a in range(2):
+                mm(B(RAW[k][a]), B("id"), B("d", (512 * (2 * k + a), 512 * (2 * k + a + 1))), False, True)
 
         def raw_abs(k):
             for a in range(2):
-                ac(B("ad", (4 * k + 2 * a, 4 * k + 2 * a + 2)), B("b%d" % (2 + a)), AF.Abs)
+                ac(B("ad", (4 * k + 2 * a, 4 * k + 2 * a + 2)), B(RAW[k][a]), AF.Abs)
 
         def reduce(k):
             s, c = k // 4, k % 4
             out = k2 if k == 7 else B("b%d" % s, (64 * c, 64 * c + 64))
-            mm(out, B("id"), B("ci", (0, 64)), True, False)
+            mm(out, B("id"), B("ci"), True, False)
             for m in range(16):
                 mm(out, lm(m), B("ad", (4 * k, 4 * k + 4), m), False, m == 15)
 
-        def entries(s):
-            r = (32 * s, 32 * s + 32)
-            tt(B("kc", r), B("sc", (512 * s + 15, 512 * s + 512, 16)), B("thq", r), A.min)
-            ts(B("ke", r), B("kc", r), 31, AND)
-            cp(B("eu", r), B("ke", r))
+        def records(ns):
+            for n in ns:
+                scat(B("x"), B("xoff", (2 * n, 2 * n + 1)), B("rn", (16 * n, 16 * n + 16)))
 
-        gat(B("li"), lists, B("uu"))
-        iota(B("pk", (0, CAP)), [[0, CAP]], 512)
-        iota(B("plw", (0, 256)), [[1, 256]], 1216 + CAP * t)
+        pick(B("pk", (0, CAP)), B("plw", (256, 256 + CAP)), [[0, CAP]], A.is_gt, 0.25, 0, 0)
+        iota(B("plw", (0, CAP)), [[1, CAP]], H - Z + CAP * t)
+        raw_q(0)
+        raw_q(4)
         raw(0)
+        raw_x(0)
         diff(1)
         absd(1)
         raw_abs(0)
@@ -452,43 +467,49 @@ def rank_program(g, core, T, topo):
         absd(2)
         raw(4)
         reduce(2)
+        raw_x(4)
         diff(3)
         absd(3)
         reduce(3)
-        if t == 0:
-            late_constants()
         diff(5)
         raw_abs(4)
         reduce(4)
         absd(5)
         ac(B("u1h"), u1, AF.Copy)
         reduce(5)
-        if t == 0:
-            later_constants()
         diff(6)
         absd(6)
-        reduce(6)
         scan(B("sc", (0, 256)), B("resn"), k0, A.max, A.min)
-        scan(B("sc", (256, 512)), B("resx"), k0, A.add, A.max)
+        reduce(6)
+        diff(7, (0,))
+        absd(7, (0,))
         ts(B("f0"), best0, B("th32"), A.is_ge)
         mm(B("b6", (48, 64)), B("swd"), B("u1h"), True, True)
         mm(B("b6", (64, 80)), B("sw"), B("f0"), True, True)
-        for hf in range(2):
-            diff(7, (hf,))
-            absd(7, (hf,))
+        diff(7, (1,))
+        absd(7, (1,))
+        scan(B("sc", (512, 768)), B("resx"), k0, A.add, A.max)
         reduce(7)
+        ac(B("mw"), B("b4"), AF.Copy)
+        ac(B("qf"), B("q"), AF.Copy, scale=1.0 / 2048)
+        agat(B("u2f"), B("mw"), B("uu", (16, 32)))
         if t == 0:
-            ac(B("mw"), B("b4"), AF.Copy, scale=1024.0)
-        agat(B("lif"), lists, B("uu"))
-        ac(B("lic"), B("lif"), AF.Identity, bias=-44.0, scale=1.0 / 32)
+            agat(B("lic"), lists, B("uu"), bias=-Z / 32, scale=1.0 / 32)
+        ac(ok0, B("f0"), AF.Identity, bias=1.0, scale=-1.0)
         ts(B("thl"), B("f0"), -MID, A.mult, B("thb"), A.add)
-        ts(B("thq", (32, 48)), B("f0"), B("th32"), A.mult)
-        scan(B("sc", (512, 704)), B("resn", (0, 192)), k1, A.max, A.min)
+        ts(B("thq", (16, 32)), B("f0"), B("th32"), A.mult)
+        tt(B("xk"), B("b6", (64, 80)), B("f0"), A.mult)
+        scan(B("sc", (256, 448)), B("resn", (0, 192)), k1, A.max, A.min)
+        tt(B("dl"), B("b6", (48, 64)), B("xk"), A.mult)
         scan(B("sc", (768, 960)), B("resx", (0, 192)), k1, A.add, A.max)
-        gat_tt(B("vv"), B("mw"), B("uu", (16, 32)), B("q"), A.add)
-        scan(B("sc", (704, 768)), B("resn", (0, 64)), k2, A.max, A.min)
-        tt(h, best1, B("thl"), A.is_lt)
+        tt(B("d1"), B("dl"), B("bq"), A.mult)
+        tt(B("d0"), B("dl"), B("d1"), A.subtract)
+        tt(B("moh", (0, 16), 1), B("moh", (0, 16), 1), B("d1"), A.add)
+        tt(B("moh", (0, 16), 0), B("moh", (0, 16), 0), B("d0"), A.add)
+        scan(B("sc", (448, 512)), B("resn", (0, 64)), k2, A.max, A.min)
         scan(B("sc", (960, 1024)), B("resx", (0, 64)), k2, A.add, A.max)
+        tt(h, best1, B("thl"), A.is_lt)
+        tt(B("kc"), B("sc", (15, 1024, 16)), B("thq"), A.min)
         scan(B("cs", (1, 17)), h, B("zz"), A.add, A.add)
         tt(B("hj"), h, B("rj"), A.mult)
         off = B("b6", (16, 32))
@@ -496,136 +517,135 @@ def rank_program(g, core, T, topo):
         mm(off, B("ntri"), h, False, False)
         mm(off, B("nbo"), B("cs", (0, 16)), False, False)
         mm(off, B("id"), B("hj"), False, True)
-        tt(B("kc"), B("sc", (15, 1024, 16)), B("thq"), A.min)
         ts(B("ke"), B("kc"), 31, AND)
-        cp(B("offu"), off)
+        tt(B("dmo"), B("moh", (0, 16), 1), B("moh", (0, 16), 0), A.subtract)
         cp(B("eu"), B("ke"))
-        scat(B("pk"), B("offu"), B("vv"))
-        ac(B("un"), h, AF.Identity, bias=1.0, scale=-1.0)
-        ac(ok0, B("f0"), AF.Identity, bias=1.0, scale=-1.0)
-        op("s", lambda: act.activation(B("plg")[0], B("plw")[0].indirect(B("offu")[0]), AF.Copy, scale=1.0 / 32), B("plg"), B("plw"), B("offu"))
-        ts(B("qi"), B("pk", (0, CAP)), 1023, AND)
-        ts(B("u2i"), B("pk", (0, CAP)), 10, SHR)
-        cp(B("qb"), B("qi"))
+        cp(B("offu"), off)
+        for m in range(16):
+            mm(B("b4", (0, 16), (2 * m, 2 * m + 2)), B("bm", m), B("moh"), True, True)
+        agat(B("plg"), B("plw"), B("offu"), scale=1.0 / 32)
+        gat_tt(B("ns"), B("oh"), B("eu", (0, 32)), B("lic"), A.mult)
+        agat(B("ohw"), B("oh"), B("eu", (32, 64)))
+        scat_add(B("pk"), B("offu"), B("u2f"), B("qf"))
+        vp, num, dd = B("b7", (256, 512)), B("b7", (0, 16)), B("b5", (0, 256))
+        mm(vp, B("id"), B("plg"), True, False)
+        for s in range(2):
+            mm(vp, B("bo"), B("ns", (256 * s, 256 * s + 256)), False, s == 1)
+        ac(B("vps"), vp, AF.Copy)
+        mm(dd, B("nid"), B("trib"), True, False)
+        for m in range(16):
+            mm(num, lm(m), B("vps", (m, 256, 16)), m == 0, m == 15)
+        mm(dd, B("nid"), B("vps"), False, False)
+        cp(B("u2i"), B("pk", (0, CAP)))
+        tt(B("zu"), B("trp"), B("ok"), A.mult)
+        tt(B("qs"), B("pk", (0, CAP)), B("u2i"), A.subtract)
         tt(B("um"), B("u2i"), B("dm"), A.mult)
         for i in range(GV, 16):
-            ac(B("qg", (i, 1024, 16)), B("qb"), AF.Copy)
-        gat_tt(B("ns", (0, 256)), B("oh"), B("eu", (0, 16)), B("lic", (0, 256)), A.mult)
+            ac(B("qg", (i, 1024, 16)), B("qs"), AF.Copy, scale=2048.0)
+        ac(B("numc"), num, AF.Copy, scale=1.0 / 512)
+        for m in range(16):
+            mm(B("b5", (m, 256, 16)), B("id"), B("numc"), False, m == 15)
+        tt(B("ub"), B("zu"), B("uf"), A.max)
         scan(B("us"), B("resa"), B("um"), A.mult, A.add)
-        gat_tt(B("ns", (256, 512)), B("oh"), B("eu", (32, 48)), B("lic", (256, 512)), A.mult)
+        ts(B("qg", (0, 1024, 16)), B("qs"), 2048.0, A.mult)
         cp(B("u2u"), B("us", (15, 64, 16)))
-        num = B("b7", (0, 16))
-        mm(num, B("id14"), h, True, False)
-        for s in range(2):
-            for m in range(16):
-                mm(num, lm(m), B("ns", (256 * s + m, 256 * s + 256, 16)), False, s == 1 and m == 15)
-        for i in range(GV):
-            cp(B("qg", (i, 1024, 16)), B("qb"))
+        for i in range(1, GV):
+            ts(B("qg", (i, 1024, 16)), B("qs"), 2048.0, A.mult)
         for kind in KINDS:
             arrived(kind, t)
         gat(B("lig"), B(pr, (LP, LP + V)), B("u2u"))
-        ac(B("dg", (0, CAP)), B("qb"), AF.Copy, scale=-1.0)
-        ac(B("numc"), num, AF.Identity, bias=-44.5, scale=1.0 / 32)
-        dd = B("b5", (0, 256))
-        mm(dd, B("nid"), B("trib"), True, False)
-        mm(dd, B("nid"), B("plg"), False, False)
-        for s in range(2):
-            mm(dd, B("nbo"), B("ns", (256 * s, 256 * s + 256)), False, False)
-        for m in range(16):
-            mm(B("b5", (m, 256, 16)), B("id"), B("numc"), False, m == 15)
-        cp(B("numu"), num)
-        for hf in range(2):
-            r = (CAP + 512 * hf, CAP + 512 * hf + 512)
-            gat_tt(B("dg", r), B(xr, (0, H + CAP * t)), B("lig", (32 * hf, 32 * hf + 32)), B("qg", (512 * hf, 512 * hf + 512)), A.subtract)
-            ac(B("adg", (2 * hf, 2 * hf + 2)), B("dg", r), AF.Abs, scale=64.0)
-            if hf == 0:
-                ac(B("da"), dd, AF.Abs, scale=float(2 ** 17))
+        ts(B("numu"), num, 1.0 / 16, A.mult, float(PAD + Z), A.add)
+        xg, g0, g1 = B(xr, (0, H + CAP * t)), B("dg", (CAP, CAP + 512)), B("dg", (CAP + 512, CAP + 1024))
+        mm(B("b3"), B("nid"), B("qg", (512, 1024)), True, False)
+        agat(g1, xg, B("lig", (32, 64)))
+        mm(B("b3"), B("id"), g1, False, True)
+        gat_tt(g0, xg, B("lig", (0, 32)), B("qg", (0, 512)), A.subtract)
+        ac(B("adg", (0, 2)), g0, AF.Abs, scale=64.0)
+        ac(B("adg", (2, 4)), B("b3"), AF.Abs, scale=64.0)
+        gat_tt(B("sh"), B("x", (0, TRX)), B("numu"), B("q"), A.add)
+        ts(B("th2k"), B(pr, (LP - 1, LP)), 2048.0, A.mult)
+        ts(B("dg", (0, CAP // 2)), B("qs", (0, CAP // 2)), -2048.0, A.mult)
+        ts(B("thp"), B("jb", (0, 4)), B("th2k"), A.add)
+        ts(B("qz", (0, CAP // 2)), B("qs", (0, CAP // 2)), 2048.0, A.mult)
+        ac(B("da"), dd, AF.Abs, scale=float(2 ** 21))
+        ac(B("rnh"), B("sh"), AF.Identity, bias=1279.75, scale=0.5)
+        ac(B("rn"), B("rnh"), AF.Identity, bias=-1280.0)
         gk = B("b0", (320, 384))
         mm(gk, B("id"), B("pcg"), True, False)
         for m in range(16):
             mm(gk, lm(m), B("adg", (0, 4), m), False, m == 15)
+        mm(B("b3"), B("id"), B("lic"), True, False)
+        mm(B("b3"), B("kn"), B("ohw"), False, True)
+        mm(B("b2"), B("kp"), B("ohw"), True, False)
         for s in range(2):
-            dv = B("b2", (256 * s, 256 * s + 256))
-            mm(dv, B("nid"), B("lic", (256 * s, 256 * s + 256)), True, False)
-            mm(dv, B("id"), B("plg"), False, False)
-            for a in range(2):
-                mm(dv, B("bo"), B("ns", (256 * a, 256 * a + 256)), False, a == 1)
-        gat_tt(B("sh"), B("x", (0, TRX)), B("numu"), B("q"), A.add)
-        ac(B("th2k"), B(pr, (LP - 1, LP)), AF.Copy, scale=2048.0)
-        ac(B("rnh"), B("sh"), AF.Identity, bias=1279.75, scale=0.5)
-        ac(B("thp"), B("jb", (0, 4)), AF.Identity, bias=B("th2k"))
-        ac(B("rn"), B("rnh"), AF.Identity, bias=-1280.0)
+            mm(B("b2", (256 * s, 256 * s + 256)), B("id"), B("vps"), False, s == 1)
         scan(B("am"), B("resn"), B("da"), A.max, A.min)
-        tt(B("xk"), B("b6", (64, 80)), B("f0"), A.mult)
         tt(B("a2"), B("am", (15, 256, 16)), h, A.mult)
-        tt(B("dl"), B("b6", (48, 64)), B("xk"), A.mult)
         tt(B("xt"), B("trx"), B("a2"), A.subtract)
-        tt(B("d1"), B("dl"), B("bq"), A.mult)
         tt(B("xo"), B("xt"), num, A.max)
-        tt(B("d0"), B("dl"), B("d1"), A.subtract)
-        cp(B("xoff", (0, 32, 2)), B("xo"))
-        tt(B("moh", (0, 16), 1), B("moh", (0, 16), 1), B("d1"), A.add)
+        ts(B("xoff", (0, 32, 2)), B("xo"), 1.0 / 16, A.mult, float(PAD + Z), A.add)
+        records(range(15, 11, -1))
         scan(B("sg2"), B("resn", (0, 64)), gk, A.max, A.min)
-        tt(B("moh", (0, 16), 0), B("moh", (0, 16), 0), B("d0"), A.add)
+        records([11])
         tt(B("gkc"), B("sg2", (15, 64, 16)), B("thp"), A.min)
-        tt(B("zu"), B("trp"), B("ok"), A.mult)
+        records([10])
         ts(B("gpos"), B("gkc"), 2047, AND)
-        tt(B("dmo"), B("moh", (0, 16), 1), B("moh", (0, 16), 0), A.subtract)
+        records([9])
         cp(B("posu"), B("gpos"))
-        tt(B("ub"), B("zu"), B("uf"), A.max)
-        gat_tt(B("gw", (0, CAP)), B("dg"), B("posu"), B("qb"), A.add)
+        records([8])
+        gat_tt(B("gw", (0, CAP)), B("dg"), B("posu"), B("qz"), A.add)
         agat(B("fw", (0, CAP)), B("flw"), B("posu"))
         agat(B("c"), B("fw"), B("offu"))
+        ac(B("t1"), B("b3"), AF.Relu, bias=float(Z), scale=32.0)
+        ac(B("t2"), B("b2"), AF.Relu, bias=float(Z - 4096), scale=32.0)
+        if end:
+            ac(B("ym2"), B("b4"), AF.Copy)
+            dma("y", T.ym[:], T.z_ym2[0:128:16, :], (B("ym2"),), ())
         tr = B("b6", (96, 112))
         mm(tr, B("id"), B("trph"), True, False)
         mm(tr, B("idk"), h, False, False)
         for m in range(16):
             mm(tr, lm(m), B("c", (m, 256, 16)), False, m == 15)
         gcol = B("x", (PAD + H + CAP * t, PAD + H + CAP * t + CAP))
-        ac(B("dvs"), B("b2"), AF.Copy, scale=32.0)
+        records([7])
         if not end:
             gat_tt(B("s1"), B("gw"), B("offu"), B("sh"), A.add)
+            records([6])
             ts(B("s2"), B("s1"), 255, AND)
+            records([5])
             cp(B("q"), B("s2"))
             parity(False)
-        for n in range(15, -1, -1):
-            scat(B("x"), B("xoff", (2 * n, 2 * n + 1)), B("rn", (16 * n, 16 * n + 16)))
-        if not end:
-            send("x", t + 1)
-            qrep(QV)
-        ac(gcol, B("gw", (0, CAP)), AF.Copy)
-        if not end:
-            send("c", t + 1)
+            records([4])
+            qrep("s", QV + QG, 16)
+            records(range(3, 0, -1))
             ts(B("got"), tr, 0.0, A.is_lt)
             mm(par, B("sg"), B("got"), False, True)
+            records([0])
+            send("x", t + 1)
+            qrep("g", QV, QV + QG)
         else:
-            dma("y", T.yx[:], B("x", (PAD, TRX))[0], (B("x", (PAD, TRX)),), ())
-        if t == 0:
-            for m in range(16):
-                ac(B("bm", m), B("bo"), AF.Copy, scale=B("dcol", (m, m + 1)))
-        for m in range(16):
-            mm(B("b4", (0, 16), (2 * m, 2 * m + 2)), B("bm", m), B("moh"), True, True)
-        if not end:
-            ac(B("mw"), B("b4"), AF.Copy, scale=1024.0)
-        else:
-            ac(B("ym2"), B("b4"), AF.Copy)
-            dma("y", T.ym[:], T.z_ym2[0:128:16, :], (B("ym2"),), ())
+            records(range(6, -1, -1))
         for s in range(2):
             tt(B("po", (16 * s, 16 * s + 16)), B("ub", (16 * s, 16 * s + 16)), tr, A.max)
-        for s in (1, 0):
-            gat_tt(B("wd", (256 * s, 256 * s + 256)), B("oh"), B("eu", (32 * s + 16, 32 * s + 32)), B("dvs", (256 * s, 256 * s + 256)), A.mult)
-            if s:
-                cp(B("poff"), B("po"))
+        cp(gcol, B("gw", (0, CAP)))
+        if end:
+            dma("y", T.yx[:], B("x", (PAD, TRX))[0], (B("x", (PAD, TRX)),), ())
+        cp(B("poff"), B("po"))
         if not end:
-            towns_a()
-        scat_add(B("pt", (LP, LP + V + 256)), B("poff", (16, 32)), B("lif", (256, 512)), B("wd", (256, 512)))
+            send("c", t + 1)
+        scat_add(B("pt", (LP, LP + V + 256)), B("poff", (16, 32)), B("t1", (256, 512)), B("t2", (256, 512)))
         if not end:
-            towns_b()
-            towns_c()
-        scat_add(B("pt", (LP, LP + V + 256)), B("poff", (0, 16)), B("lif", (0, 256)), B("wd", (0, 256)))
+            towns(0)
+        scat_add(B("pt", (LP, LP + V + 256)), B("poff", (0, 16)), B("t1", (0, 256)), B("t2", (0, 256)))
         if not end:
             send("p", t + 1)
-            towns_d()
+            towns(1)
+            qrep("v", 0, QV // 2)
+            towns(2)
+            towns(3)
+            qrep("v", QV // 2, QV)
+            gat(B("li"), lists, B("uu"))
+            agat(B("lic"), lists, B("uu"), bias=-Z / 32, scale=1.0 / 32)
     dma("s", T.yp[:], lists[0], (lists,), ())
     for s, v in total.items():
         g.wait_ge(T.sem[s], v)

@@ -10,9 +10,8 @@ BIG = float(2 ** 30)
 MID = float(2 ** 20)
 Z = 1408
 RAW = {0: ("b2", "b3"), 4: ("b5", "b7")}
-QV, QG = 2, 0
-QV0 = 8
-GV = 5
+QV, QV0 = 2, 4
+NR = 5
 
 BUF, AT = {}, {}
 SCRATCH = {}
@@ -33,25 +32,28 @@ def _pack(dtype, **kw):
     SCRATCH["t_" + dtype] = ("sbuf", [128, at], dtype)
 
 
-_add("sbuf", "int32", pti=LP + V, pr0=LP + V, moi=V, s1=256, s2=256)
+_add("sbuf", "int32", pti=LP + V, pr0=LP + V, moi=V, s1=256, s2=256, sh=256, rn=256)
 _pack("int32", pc=1, pmi=1, pgi=1, podd=1, bi=16, bq=16, kc=64, ke=64, u2i=64, gkc=4, gpos=4)
 _add("sbuf", "uint16", li=512)
-_pack("uint16", uu=32, offu=16, numu=16, xoff=32, poff=32, u2u=4, posu=4, lig=64, eu=64)
-_add("sbuf", "bfloat16", x=TRX + 256, q=256, qrep=4096, d=8192, ad=[32, 16, 16], bm=[16, 128], zl=144, zw=144, ci=64, resn=256,
-     resx=256, nt=256, qg=1024, dg=CAP + 1024, flw=CAP + 1024, adg=[4, 16, 16], xr0=H, xr1=H + CAP, xr2=H + 2 * CAP, fw=512, gw=512,
-     rn=256, ohw=512)
-_pack("bfloat16", id=128, nid=128, bo=128, nbo=128, ntri=128, idk=128, kp=128, kn=128, sw=128, swd=128, sg=128, one=144, ef=256,
-      it=256, dm=64, trib=256, resa=64, c=256, da=256, am=256, jb=16, zz=16, ok=32, f0=16, cs=32, xk=16, qs=64, qz=64, got=16, oh=32)
+_pack("uint16", uu=32, offu=16, numu=16, xoff=32, poff=32, u2u=4, posu=4, lig=64, eu=64, expl=16)
+_add("sbuf", "bfloat16", x=TRX + 16, q=256, qrep=3072, d=8192, dr=[32, 256], ad=[32, 16, 16], bm=[16, 128], zl=144, zw=144, zn=144,
+     z2=144, ci=64, resn=256, resx=256, nt=128, dg=CAP + 1024, flw=CAP + 1024, adg=[4, 16, 16], xr0=H + 16, xr1=H + CAP,
+     xr2=H + 2 * CAP, fw=512, gw=512, ohw=512, nil=512)
+_pack("bfloat16", id=128, nid=128, bo=128, nbo=128, ntri=128, idk=128, idp=128, idq=128, kp=128, kn=128, sw=128, swd=128, sg=128,
+      one=128, ef=144, it=256, dm=64, trib=256, resa=64, c=256, da=256, am=256, jb=16, zz=16, h=16, f0=16, cs=32, xk=16, qs=64,
+      got=16, oh=32)
 _add("sbuf", "float16", moh=[16, 2], mo8=[16, 32], e8=128, z8=144, pcg=64)
-_pack("float16", lic=512, ns=512, plg=256, vps=256, rnh=256, u1h=16, rj=16, hj=16, numc=16, trph=16)
-_add("sbuf", "float32", pt=LP + V + 256, pr1=LP + V, pr2=LP + V, mw=V, pf=1, sc=1024, sg2=64, ym2=V, plw=512, t1=512,
-     t2=512, sh=256, pk=512, u2f=256, qf=256)
-_pack("float32", pm=1, pg=1, pz=1, pidx=1, widx=1, evc=1, th32=1, thb=1, th2k=1, c1=1, c2=1, c3=1, dcol=16, j2=16, trx=16, trp=32,
-      dmo=16, uf=32, t16=16, dl=16, d1=16, d0=16, thl=16, thq=64, thp=4, a2=16, xt=16, xo=16, um=64, us=64, zu=32, ub=32, po=32)
+_pack("float16", lic=512, ns=512, plg=256, vps=256, uf=32, dmo=16, dl=16, d1=16, rj=16, hj=16, nex=256, trph=16, trpm=16)
+_add("sbuf", "float32", pt=LP + V + 256, pr1=LP + V, pr2=LP + V, mw=V, pf=1, sc=1024, sg2=64, ym2=V, plw=512, t1=512, t2=512,
+     pk=512, u2f=256, qf=256)
+_pack("float32", pm=1, pg=1, pz=1, pidx=1, widx=1, evc=1, th32=1, thb=1, th2k=1, c1=1, c2=1, c3=1, trx=1, trc=1, j2=16, t16=16,
+      tn=16, numc=16, thl=16, thq=32, thp=4, xo=16, um=64, us=64, ub=32, po=32)
 _add("psum", "float32", b0=512, b1=512, b2=512, b3=512, b4=[16, 32], b5=512, b6=512, b7=512)
-KINDS = "xcp"
+KINDS = ("pxyz", "xycp", "xycp")
+THIRD = 880
+NCORES = 256
 SEMAPHORES = (["sv", "sa", "st", "sg"] + ["dma%d" % i for i in range(16)]
-              + [a + k + str(t) for a in ("in", "lo") for k in KINDS for t in range(R_)])
+              + [a + k + str(t) for a in ("in", "lo") for t in range(R_) for k in KINDS[t]])
 
 
 def _mask(es):
@@ -61,24 +63,51 @@ def _mask(es):
     return m
 
 
-def _relays(T, topo, r, t):
-    def far(a):
-        return not topo.may_write(T.cores[a], T.cores[(a - 1 - t) % N])
+def _ways(T, topo, r, t):
     src, dst = T.cores[r], T.cores[(r - 1 - t) % N]
-    if not far(r):
-        return []
-    busy = {topo.die(T.cores[a]) for a in range(N) if a != r and T.cores[a] in topo.cores_of(src) and far(a)}
-    return [c for c in topo.cores_of(src) if topo.may_write(c, dst) and topo.die(c) not in busy]
+    if dst in topo.cores_of(src):
+        return [[dst]]
+
+    def mate(c):
+        return [m for m in range(NCORES) if topo.mates(c, m)][0]
+
+    def port(c, die):
+        return [k for k in topo.cores_of(c) if topo.die(k) == die and topo.may_write(k, mate(c))][0]
+    near, far = port(src, topo.die(src)), port(mate(dst), topo.die(src))
+    if topo.may_write(src, dst):
+        return [[dst], [near, far, dst]]
+    idle = [topo.die(T.cores[a]) for a in range(N)
+            if a != r and T.cores[a] in topo.cores_of(src) and T.cores[(a - 1 - t) % N] in topo.cores_of(src)]
+    return [[near, dst], [far, dst]] + [[port(src, d), dst] for d in idle]
+
+
+PLAN = {}
 
 
 def _pieces(T, topo, r, t, kind):
-    hops = _relays(T, topo, r, t) or [None]
-    old = H + CAP * max(t - 1, 0)
-    if kind == "c":
-        return [(hops[0], old, old + CAP)] if t else []
-    lo, hi = (0, old) if kind == "x" else (LP - 4, LP + V)
-    n = (hi - lo) // len(hops)
-    return [(c, lo + n * k, lo + n * k + n) for k, c in enumerate(hops)]
+    if (r, t, kind) not in PLAN:
+        src, ways = T.cores[r], _ways(T, topo, r, t)
+        old = H + CAP * max(t - 1, 0)
+        chip = topo.cores_of(src)
+        out = [topo.engines(src, w[0]) for w in ways if w[0] not in chip]
+        if kind != "x":
+            ways = [w for w in ways if len(w) < 3]
+        if kind == "c":
+            ways, lo, n = ways[:1], old, CAP
+        elif kind == "p":
+            n = -(-(V + 1) // len(ways))
+            lo = LP + V - n * len(ways)
+        elif t == 0:
+            k = "xyz".index(kind)
+            ways, lo, n = [sorted(ways, key=lambda w: w[0] in chip)[k % len(ways)]], k * THIRD, THIRD
+        else:
+            lo, n = old // 2 * (kind == "y"), old // 2 // len(ways)
+        on = [w for w in ways if w[0] in chip]
+        left = [e for e in topo.engines(src, on[0][0]) if e not in sum(out, [])] if on else []
+        PLAN[(r, t, kind)] = [
+            (w, out[0] if w not in on else left[on.index(w) * len(left) // len(on):(on.index(w) + 1) * len(left) // len(on)],
+             lo + n * k, lo + n * k + n) for k, w in enumerate(ways)]
+    return PLAN[(r, t, kind)]
 
 
 def _copy(kind, t):
@@ -88,17 +117,16 @@ def _copy(kind, t):
 def _hand_on(g, core, T, topo):
     sent = []
     for t in range(R_):
-        for kind in (KINDS if t else "px"):
+        for kind in KINDS[t]:
             for r in range(N):
-                ps = _pieces(T, topo, r, t, kind)
-                for c, lo, hi in ps:
-                    if c == core:
-                        dst = T.cores[(r - 1 - t) % N]
-                        g.wait_ge(T.sem["in%s%d" % (kind, t)], len(topo.engines(T.cores[r], core)) // len(ps))
-                        rid, pid = topo.addr(dst, core)
+                for way, es, lo, hi in _pieces(T, topo, r, t, kind):
+                    if core in way:
+                        k = way.index(core)
+                        g.wait_ge(T.sem["in%s%d" % (kind, t)], len(topo.engines(way[k - 1], core) if k else es))
+                        rid, pid = topo.addr(way[k + 1], core)
                         ap = T["z_" + _copy(kind, t)][:, lo:hi]
-                        g.remote_dma(ap, ap, T.sem["in%s%d" % (kind, t)], T.sem["lo%s%d" % (kind, t)], pid, rid, topo.mask(core, dst))
-                        sent.append(("lo%s%d" % (kind, t), len(topo.engines(core, dst))))
+                        g.remote_dma(ap, ap, T.sem["in%s%d" % (kind, t)], T.sem["lo%s%d" % (kind, t)], pid, rid, topo.mask(core, way[k + 1]))
+                        sent.append(("lo%s%d" % (kind, t), len(topo.engines(core, way[k + 1]))))
     for sem, n in sent:
         g.wait_ge(T.sem[sem], n)
 
@@ -188,23 +216,20 @@ def rank_program(g, core, T, topo):
         r = (rank + 1 + t) % N
         sem, name = "in%s%d" % (kind, t), _copy(kind, t)
         ps = _pieces(T, topo, r, t, kind)
-        n = sum(len(topo.engines(T.cores[r] if c is None else c, core)) for c, lo, hi in ps)
+        n = sum(len(topo.engines(way[-2], core) if len(way) > 1 else es) for way, es, lo, hi in ps)
         if n:
             total[sem] = n
             clk[(sem, n)] = {}
-            hist.setdefault(name, []).append((B(name, (ps[0][1], ps[-1][2]))[2], True, sem, n, sem))
+            hist.setdefault(name, []).append((B(name, (ps[0][2], ps[-1][3]))[2], True, sem, n, sem))
 
     def send(kind, t):
         ps = _pieces(T, topo, rank, t, kind)
         name, at = ("pt" if t else "pti", 0) if kind == "p" else ("x", PAD)
-        src = B(name, (at + ps[0][1], at + ps[-1][2]))
+        src = B(name, (at + ps[0][2], at + ps[-1][3]))
         wait("g", deps("g", (src,), ()))
         trs, n = [], 0
-        for k, (c, lo, hi) in enumerate(ps):
-            dst = T.cores[(rank - 1 - t) % N] if c is None else c
-            es = topo.engines(core, dst)
-            es = es[k * len(es) // len(ps):(k + 1) * len(es) // len(ps)]
-            rid, pid = topo.addr(dst, core)
+        for way, es, lo, hi in ps:
+            rid, pid = topo.addr(way[0], core)
             trs.append(RemoteDMATransfer(dst_ids=[DstId(rid=rid, pnc=pid)], dma_engine_mask=_mask(es),
                                          remote_sem=T.sem["in%s%d" % (kind, t)],
                                          src=B(name, (at + lo, at + hi))[0], dst=T["z_" + _copy(kind, t)][:, lo:hi]))
@@ -261,6 +286,10 @@ def rank_program(g, core, T, topo):
     def mm(out, l, r, start, stop):
         op("t", lambda: pe.matmul(out[0], l[0], r[0], start, stop), out, l, r)
 
+    def mms(out, *terms):
+        for i, (l, r) in enumerate(terms):
+            mm(out, B(l), r, i == 0, i == len(terms) - 1)
+
     def iota(out, pattern, base=0, mult=0):
         if BUF[out[1]][2] == "int32":
             op("g", lambda: g.iota(out[0], pattern, base, mult), out)
@@ -279,23 +308,28 @@ def rank_program(g, core, T, topo):
 
     lists = B("pt", (LP, LP + V))
     AND, SHR = A.bitwise_and, A.arith_shift_right
-    e128, i128, n128 = B("ef", (0, 128)), B("it", (0, 128)), B("nt", (0, 128))
+    e128, i128 = B("ef", (0, 128)), B("it", (0, 128))
     par = B("b1", (256, 272))
     xwin = B("x", (PAD, TRX))
     u0, u1 = B("uf", (0, 16)), B("uf", (16, 32))
-    k0, k1, k2 = B("b0", (0, 256)), B("b1", (0, 192)), B("b0", (256, 320))
+    m0, m1 = B("moh", (0, 16), 0), B("moh", (0, 16), 1)
+    k0, k1 = B("b0", (0, 256)), B("b1", (0, 256))
     best0, best1 = B("sc", (15, 256, 16)), B("sc", (271, 512, 16))
-    ok0, h = B("ok", (0, 16)), B("ok", (16, 32))
+    h = B("h")
 
     def qrep(q, lo, hi):
         for i in range(lo, hi):
-            out = B("qrep", (i, 4096, 16))
             if q == "v":
-                cp(out, B("q"))
-            elif q == "s":
-                ac(out, B("q"), AF.Copy)
+                cp(B("qrep", (i, 3072, 16)), B("q", (64, 256)))
             else:
-                pick(out, B("q"), [[0, 256]], A.is_ge, 0.0, 0, 0)
+                ac(B("qrep", (i, 3072, 16)), B("q", (64, 256)), AF.Copy)
+
+    def zero(bank):
+        mm(B(bank), B("nil", (0, 128)), B("nil"), True, False)
+
+    def minus(bank, l, qs):
+        for i in range(16):
+            mm(B(bank, (i, 512, 16)), l, qs, False, False)
 
     def parity(last):
         for m in range(16):
@@ -309,342 +343,355 @@ def rank_program(g, core, T, topo):
         elif step == 2:
             tt(B("t16"), B("bq"), B("dmo"), A.mult)
             tt(u0, B("bq"), B("j2"), A.add)
+        elif step == 3:
+            tt(u1, B("t16"), m0, A.add)
         else:
-            tt(u1, B("t16"), B("moh", (0, 16), 0), A.add)
             cp(B("uu"), B("uf"))
 
     dma("y", B("q")[0], T.qs[:], (), (B("q"),))
-    dma("s", T.z_moi[0:8, :], T.mo[:], (), (B("moi"),))
+    dma("s", B("pti", (LP - 1, LP))[0], T.th[:], (), (B("pti", (LP - 1, LP)),))
     dma("y", B("pti", (LP, LP + V))[0], T.towns[:], (), (B("pti", (LP, LP + V)),))
-    fill(B("pti", (0, LP)), 0)
-    dma("s", B("pti", (LP - 1, LP))[0], T.th[:], (), (B("pti", (0, LP)),))
-    dma("y", B("x", (PAD, PAD + H))[0], T.x[:], (), (B("x", (PAD, PAD + H)),))
+    dma("s", T.z_moi[0:8, :], T.mo[:], (), (B("moi"),))
+    for lo in range(0, H, THIRD):
+        part = B("x", (PAD + lo, PAD + min(lo + THIRD, H)))
+        dma("y", part[0], T.x[:, lo:min(lo + THIRD, H)], (), (part,))
     iota(B("pc"), [[1, 1]], 0, 1)
-    iota(B("ef"), [[1, 256]])
+    iota(B("ef"), [[1, 144]])
     fill(B("one"), 1.0)
-    iota(B("nt", (0, 128)), [[1, 8], [0, 16]])
-    pick(B("id"), B("one", (0, 128)), [[-1, 128]], A.is_equal, 0.0, 0, 1)
+    pick(B("id"), B("one"), [[-1, 128]], A.is_equal, 0.0, 0, 1)
+    iota(B("nt"), [[1, 8], [0, 16]])
     iota(B("it"), [[0, 16], [1, 16]])
     iota(B("ci"), [[0, 4], [1, 16]], 1)
     ts(B("pmi"), B("pc"), 15, AND)
     ts(B("pgi"), B("pc"), 4, SHR)
     ts(B("podd"), B("pc"), 1, AND)
     cp(B("pm"), B("pmi"))
-    cp(B("pg"), B("pgi"))
     ts(B("pz"), B("pgi"), 16.0, A.mult, 15.0, A.add)
     ts(B("evc"), B("podd"), -1.0 / 32, A.mult, 1.0 / 32, A.add)
+    cp(B("pg"), B("pgi"))
+    ts(B("zl"), B("ef"), B("pz"), A.is_equal, 32.0, A.mult)
+    ts(B("j2"), B("ef", (0, 16)), 16.0, A.mult, B("pm"), A.add)
     cp(B("pf"), B("pc"))
+    ts(B("zw"), B("zl"), B("evc"), A.mult)
+    cp(B("jb"), B("j2"))
+    ts(B("j2"), B("j2"), 2.0, A.mult)
+    ac(B("nid"), B("id"), AF.Copy, scale=-1.0)
+    ac(B("zn"), B("zl"), AF.Copy, scale=-1.0)
+    ac(B("z2"), B("zl"), AF.Copy, scale=2.0)
+    ac(B("rj"), B("jb"), AF.Identity, bias=511.0, scale=-1.0)
+    ac(B("trx"), B("pm"), AF.Identity, bias=16.0 * (TRX - PAD - Z), scale=16.0)
+    ac(B("trc"), B("pm"), AF.Identity, bias=float(TRX))
+    ac(B("trph"), B("jb"), AF.Identity, bias=float(TRP))
+    ac(B("trpm"), B("jb"), AF.Identity, bias=float(TRP - 1024))
+    ac(B("idk"), B("id"), AF.Copy, scale=-1024.0)
     ts(B("c1"), B("pc"), 16.0, A.mult, 15.0, A.add)
     ts(B("c2"), B("podd"), -2.0, A.mult, 1.0, A.add)
     ts(B("c3"), B("pmi"), 16.0, A.mult, float(CAP), A.add)
     ts(B("pidx"), B("pmi"), 1.0, A.add)
     ts(B("widx"), B("pmi"), -1.0, A.mult, 31.0, A.add)
+    ts(B("z8"), B("ef"), B("c1"), A.is_equal)
+    tt(B("c2"), B("c2"), B("pf"), A.add)
+    ts(B("bo"), B("nt"), B("pg"), A.is_equal)
+    ac(B("nbo"), B("bo"), AF.Copy, scale=-1.0)
+    ts(B("e8"), B("nt"), B("pf"), A.is_equal)
     fill(B("x", (0, PAD)), 0.0)
     fill(B("x", (PAD + H, TRX)), 0.0)
-    ts(B("dcol"), B("ef", (0, 16)), B("pm"), A.is_equal)
-    ts(B("zl"), B("ef", (0, 144)), B("pz"), A.is_equal, 32.0, A.mult)
-    ts(B("j2"), B("ef", (0, 16)), 16.0, A.mult, B("pm"), A.add)
-    ts(B("bo"), n128, B("pg"), A.is_equal)
-    for m in range(16):
-        ac(B("bm", m), B("bo"), AF.Copy, scale=B("dcol", (m, m + 1)))
-    ts(B("zw"), B("zl"), B("evc"), A.mult)
-    ts(B("z8"), B("ef", (0, 144)), B("c1"), A.is_equal)
-    ts(B("e8"), n128, B("pf"), A.is_equal)
-    tt(B("c2"), B("c2"), B("pf"), A.add)
-    cp(B("jb"), B("j2"))
-    ts(B("rj"), B("j2"), -1.0, A.mult, 511.0, A.add)
-    ts(B("trx"), B("j2"), float(TRX - PAD - Z), A.add, 16.0, A.mult)
-    for s in range(2):
-        ts(B("trp", (16 * s, 16 * s + 16)), B("j2"), float(TRP), A.add)
-    ts(B("trph"), B("j2"), float(TRP), A.add)
-    ts(B("j2"), B("j2"), 2.0, A.mult)
-    ts(B("nid"), B("id"), -1.0, A.mult)
-    ts(B("nbo"), B("bo"), -1.0, A.mult)
-    pick(B("ntri"), B("nbo"), [[1, 128]], A.is_gt, 0.0, 0, -1)
+    fill(B("nil"), 0.0)
     ts(B("sw"), e128, B("c2"), A.is_equal)
     ts(B("oh", (0, 16)), B("ef", (0, 16)), B("pidx"), A.is_equal)
     ts(B("oh", (16, 32)), B("ef", (16, 32)), B("widx"), A.is_equal)
-    ts(B("idk"), B("id"), -1024.0, A.mult)
-    ts(B("kp"), B("id"), 128.0, A.mult)
-    ts(B("kn"), B("id"), -128.0, A.mult)
-    tt(B("swd"), B("sw"), B("id"), A.subtract)
-    fill(B("thq"), MID)
+    cp(B("expl"), B("ef", (0, 16)))
     fill(B("zz"), 0.0)
     fill(B("cs"), 0.0)
-    fill(B("qz"), 0.0)
-    fill(B("dg", (0, CAP)), 0.0)
-    send("p", 0)
-    send("x", 0)
+    iota(B("da"), [[0, 256]], 2)
+    pick(B("resn"), B("nil", (0, 256)), [[0, 16], [1, 16]], A.is_gt, BIG, 0, 0)
+    for kind in KINDS[0]:
+        send(kind, 0)
+    pick(B("resx"), B("da"), [[0, 16], [1, 16]], A.is_gt, -BIG, 0, 0)
+    pick(B("ntri"), B("nbo"), [[1, 128]], A.is_gt, 0.0, 0, -1)
     parity(True)
+    qrep("s", QV0, 16)
+    fill(B("dg", (0, CAP)), 0.0)
+    qrep("v", 0, QV0)
     cp(rows8("mo8"), rows8("moi"))
     for m in range(16):
         mm(B("b7", (0, 32)), rows8("z8", (15 - m, 143 - m)), rows8("mo8", (0, 16), (2 * m, 2 * m + 2)), m == 0, m == 15)
     mm(B("b4"), rows8("e8"), rows8("mo8"), True, True)
-    qrep("s", QV0, 16)
-    qrep("v", 0, 4)
     towns(0)
-    cp(B("moh"), B("b7", (0, 32)))
+    tt(B("swd"), B("sw"), B("id"), A.subtract)
     towns(1)
-    tt(B("dmo"), B("moh", (0, 16), 1), B("moh", (0, 16), 0), A.subtract)
-    qrep("v", 4, 6)
-    towns(2)
-    qrep("v", 6, QV0)
-    towns(3)
-    ts(B("resn"), B("it"), 0.5, A.is_lt, 2 * BIG, A.mult)
-    gat(B("li"), B("pti", (LP, LP + V)), B("uu"))
-    cp(B("pt", (0, LP + V)), B("pti"))
-    ts(B("resx"), B("it"), 0.5, A.is_lt, -BIG - 2.0, A.mult)
-    ts(B("resn"), B("resn"), -BIG, A.add)
-    ts(B("th32"), B("pt", (LP - 1, LP)), 32.0, A.mult)
-    ts(B("resx"), B("resx"), 2.0, A.add)
+    cp(B("moh"), B("b7", (0, 32)))
+    ts(B("th32"), B("pti", (LP - 1, LP)), 32.0, A.mult)
     ts(B("dm"), B("it", (0, 64)), B("pm"), A.is_equal)
+    tt(B("dmo"), m1, m0, A.subtract)
     ts(B("thb"), B("th32"), MID, A.add)
     ts(B("thq", (0, 16)), B("jb"), 0.0, A.mult, B("th32"), A.add)
-    ts(B("resa"), B("it", (0, 64)), 0.5, A.is_gt)
+    towns(2)
+    towns(3)
     ts(B("sg"), i128, B("pm"), A.is_equal)
-    ts(B("trib"), B("it"), B("pm"), A.is_ge, 1024.0, A.mult)
+    towns(4)
     ts(B("um"), B("nt", (0, 64)), 256.0, A.mult, B("c3"), A.add)
+    gat(B("li"), B("pti", (LP, LP + V)), B("uu"))
+    cp(B("pt", (LP - 1, LP + V)), B("pti", (LP - 1, LP + V)))
+    ts(B("trib"), B("it"), B("pm"), A.is_ge, 1024.0, A.mult)
     tt(B("pcg"), B("um"), B("it", (0, 64)), A.add)
-    iota(B("plw", (CAP, 256)), [[0, 256 - CAP]], -PAD - Z)
-    iota(B("plw", (256, 512)), [[0, 256]])
-    iota(B("fw", (CAP, 512)), [[0, 512 - CAP]])
-    iota(B("gw", (CAP, 512)), [[0, 512 - CAP]])
-    iota(B("flw", (0, CAP)), [[0, CAP]])
-    iota(B("flw", (CAP, CAP + 1024)), [[0, 1024]], -2)
+    ac(B("plw", (256, 512)), B("nil", (0, 256)), AF.Copy)
+    ac(B("plw", (CAP, 256)), B("nil", (CAP, 256)), AF.Identity, bias=-float(PAD + Z))
+    ac(B("pt", (0, LP - 1)), B("nil", (0, LP - 1)), AF.Copy)
+
+    def mothers():
+        for m in range(16):
+            mm(B("b4", (0, 16), (2 * m, 2 * m + 2)), B("bm", m), B("moh"), True, True)
 
     for t in range(R_):
         end = t == R_ - 1
         xr, pr = "xr%d" % t, "pr%d" % t
 
-        def diff(k, parts=(0, 1)):
-            lo, hi = 2 * k + parts[0], 2 * k + parts[-1] + 1
-            r = lo % 8
-            gat_tt(B("d", (512 * lo, 512 * hi)), xwin, B("li", (32 * lo, 32 * hi)), B("qrep", (512 * r, 512 * (r + hi - lo))), A.subtract)
+        def diff(k, half=None):
+            lo, n = (64 * k, 64) if half is None else (64 * k + 32 * half, 32)
+            r = 16 * (lo % 256 - 64)
+            gat_tt(B("d", (16 * lo, 16 * (lo + n))), xwin, B("li", (lo, lo + n)), B("qrep", (r, r + 16 * n)), A.subtract)
 
-        def absd(k, parts=(0, 1)):
-            lo, hi = 2 * k + parts[0], 2 * k + parts[-1] + 1
-            ac(B("ad", (2 * lo, 2 * hi)), B("d", (512 * lo, 512 * hi)), AF.Abs)
+        def absd(k, half=None):
+            lo, n = (64 * k, 64) if half is None else (64 * k + 32 * half, 32)
+            ac(B("ad", (lo // 16, (lo + n) // 16)), B("d", (16 * lo, 16 * (lo + n))), AF.Abs)
+
+        def rows(k, parts=(0, 1)):
+            for n in range(4 * k + 2 * parts[0], 4 * k + 2 * parts[-1] + 2):
+                r = 256 * (n % 16 - 4)
+                gat_tt(B("dr", n), xwin, B("li", (16 * n, 16 * n + 16)), B("qrep", (r, r + 256)), A.subtract)
+
+        def relu(k, parts=(0, 1)):
+            r = (4 * k + 2 * parts[0], 4 * k + 2 * parts[-1] + 2)
+            ts(B("ad", r), B("dr", r), 0.0, A.max)
 
         def raw(k):
             agat(B("d", (1024 * k, 1024 * k + 1024)), xwin, B("li", (64 * k, 64 * k + 64)))
 
         def raw_q(k):
-            for a in range(2):
+            for a, bank in enumerate(RAW[k]):
                 r = (2 * k + a) % 8
-                mm(B(RAW[k][a]), B("nid"), B("qrep", (512 * r, 512 * r + 512)), True, False)
+                if r < 2:
+                    zero(bank)
+                    minus(bank, B("nid"), B("q", (32 * r, 32 * r + 32)))
+                else:
+                    mm(B(bank), B("nid"), B("qrep", (512 * r - 1024, 512 * r - 512)), True, False)
 
         def raw_x(k):
-            for a in range(2):
-                mm(B(RAW[k][a]), B("id"), B("d", (512 * (2 * k + a), 512 * (2 * k + a + 1))), False, True)
+            for a, bank in enumerate(RAW[k]):
+                mm(B(bank), B("id"), B("d", (1024 * k + 512 * a, 1024 * k + 512 * a + 512)), False, True)
 
         def raw_abs(k):
-            for a in range(2):
-                ac(B("ad", (4 * k + 2 * a, 4 * k + 2 * a + 2)), B(RAW[k][a]), AF.Abs)
+            for a, bank in enumerate(RAW[k]):
+                ac(B("ad", (4 * k + 2 * a, 4 * k + 2 * a + 2)), B(bank), AF.Abs)
 
-        def reduce(k):
-            s, c = k // 4, k % 4
-            out = k2 if k == 7 else B("b%d" % s, (64 * c, 64 * c + 64))
-            mm(out, B("id"), B("ci"), True, False)
+        def reduce(k, part=None):
+            out = B("b%d" % (k // 4), (64 * (k % 4), 64 * (k % 4) + 64))
+            if part != 1:
+                mm(out, B("id"), B("ci"), True, False)
             for m in range(16):
-                mm(out, lm(m), B("ad", (4 * k, 4 * k + 4), m), False, m == 15)
+                src = B("dr", (4 * k, 4 * k + 4), (16 * m, 16 * m + 16)) if part == 0 else B("ad", (4 * k, 4 * k + 4), m)
+                mm(out, lm(m, {None: "zl", 0: "zn", 1: "z2"}[part]), src, False, part != 0 and m == 15)
 
-        def records(ns):
-            for n in ns:
+        left = list(range(15, -1, -1))
+
+        def records(count=1):
+            for n in [left.pop(0) for _ in range(min(count, len(left)))]:
                 scat(B("x"), B("xoff", (2 * n, 2 * n + 1)), B("rn", (16 * n, 16 * n + 16)))
 
         pick(B("pk", (0, CAP)), B("plw", (256, 256 + CAP)), [[0, CAP]], A.is_gt, 0.25, 0, 0)
         iota(B("plw", (0, CAP)), [[1, CAP]], H - Z + CAP * t)
+        if t == 0:
+            pick(B("resa"), B("one", (0, 64)), [[0, 4], [1, 16]], A.is_gt, 0.0, 0, 0)
+            iota(B("flw", (0, CAP)), [[0, CAP]])
+            iota(B("flw", (CAP, CAP + 1024)), [[0, 1024]], -2)
+            iota(B("fw", (CAP, 512)), [[0, 512 - CAP]])
+            iota(B("gw", (CAP, 512)), [[0, 512 - CAP]])
+            for m in range(16):
+                pick(B("bm", m), B("one"), [[-16, 8], [0, 16]], A.is_equal, 0.0, -m, 1)
         raw_q(0)
         raw_q(4)
         raw(0)
         raw_x(0)
-        diff(1)
-        absd(1)
-        raw_abs(0)
-        reduce(1)
-        reduce(0)
-        diff(2)
-        absd(2)
+        rows(7)
+        reduce(7, 0)
         raw(4)
-        reduce(2)
+        relu(7)
+        reduce(7, 1)
         raw_x(4)
-        diff(3)
-        absd(3)
-        reduce(3)
-        diff(5)
+        diff(1)
+        raw_abs(0)
+        reduce(0)
+        absd(1)
+        reduce(1)
+        diff(2)
         raw_abs(4)
         reduce(4)
-        absd(5)
-        ac(B("u1h"), u1, AF.Copy)
-        reduce(5)
-        diff(6)
-        absd(6)
+        for k in (2, 3, 5):
+            if k > 2:
+                diff(k)
+            absd(k)
+            reduce(k)
+        for half in range(2):
+            diff(6, half)
+            absd(6, half)
         scan(B("sc", (0, 256)), B("resn"), k0, A.max, A.min)
-        reduce(6)
-        diff(7, (0,))
-        absd(7, (0,))
-        ts(B("f0"), best0, B("th32"), A.is_ge)
-        mm(B("b6", (48, 64)), B("swd"), B("u1h"), True, True)
-        mm(B("b6", (64, 80)), B("sw"), B("f0"), True, True)
-        diff(7, (1,))
-        absd(7, (1,))
         scan(B("sc", (512, 768)), B("resx"), k0, A.add, A.max)
-        reduce(7)
+        ts(B("f0"), best0, B("th32"), A.is_ge)
+        mm(B("b6", (48, 64)), B("swd"), u1, True, True)
+        mm(B("b6", (64, 80)), B("sw"), B("f0"), True, True)
+        reduce(6)
+        ts(B("thl"), B("f0"), -MID, A.mult, B("thb"), A.add)
         ac(B("mw"), B("b4"), AF.Copy)
         ac(B("qf"), B("q"), AF.Copy, scale=1.0 / 2048)
         agat(B("u2f"), B("mw"), B("uu", (16, 32)))
         if t == 0:
             agat(B("lic"), lists, B("uu"), bias=-Z / 32, scale=1.0 / 32)
-        ac(ok0, B("f0"), AF.Identity, bias=1.0, scale=-1.0)
-        ts(B("thl"), B("f0"), -MID, A.mult, B("thb"), A.add)
+            for name, c in (("idp", 1024.0), ("idq", -2048.0), ("kp", 128.0), ("kn", -128.0)):
+                ac(B(name), B("id"), AF.Copy, scale=c)
         ts(B("thq", (16, 32)), B("f0"), B("th32"), A.mult)
         tt(B("xk"), B("b6", (64, 80)), B("f0"), A.mult)
-        scan(B("sc", (256, 448)), B("resn", (0, 192)), k1, A.max, A.min)
         tt(B("dl"), B("b6", (48, 64)), B("xk"), A.mult)
-        scan(B("sc", (768, 960)), B("resx", (0, 192)), k1, A.add, A.max)
         tt(B("d1"), B("dl"), B("bq"), A.mult)
-        tt(B("d0"), B("dl"), B("d1"), A.subtract)
-        tt(B("moh", (0, 16), 1), B("moh", (0, 16), 1), B("d1"), A.add)
-        tt(B("moh", (0, 16), 0), B("moh", (0, 16), 0), B("d0"), A.add)
-        scan(B("sc", (448, 512)), B("resn", (0, 64)), k2, A.max, A.min)
-        scan(B("sc", (960, 1024)), B("resx", (0, 64)), k2, A.add, A.max)
+        mms(B("b7", (128, 160, 2)), ("id", m0), ("id", B("dl")), ("nid", B("d1")))
+        mms(B("b7", (129, 160, 2)), ("id", m1), ("id", B("d1")))
+        mms(B("b7", (160, 176)), ("id", B("dmo")), ("id", B("d1")), ("id", B("d1")), ("nid", B("dl")))
+        ac(B("moh"), B("b7", (128, 160)), AF.Copy)
+        ac(B("dmo"), B("b7", (160, 176)), AF.Copy)
+        scan(B("sc", (256, 512)), B("resn"), k1, A.max, A.min)
         tt(h, best1, B("thl"), A.is_lt)
-        tt(B("kc"), B("sc", (15, 1024, 16)), B("thq"), A.min)
+        tt(B("kc", (0, 32)), B("sc", (15, 512, 16)), B("thq"), A.min)
         scan(B("cs", (1, 17)), h, B("zz"), A.add, A.add)
         tt(B("hj"), h, B("rj"), A.mult)
         off = B("b6", (16, 32))
-        mm(off, B("id"), B("jb"), True, False)
-        mm(off, B("ntri"), h, False, False)
-        mm(off, B("nbo"), B("cs", (0, 16)), False, False)
-        mm(off, B("id"), B("hj"), False, True)
-        ts(B("ke"), B("kc"), 31, AND)
-        tt(B("dmo"), B("moh", (0, 16), 1), B("moh", (0, 16), 0), A.subtract)
-        cp(B("eu"), B("ke"))
+        mms(off, ("id", B("jb")), ("ntri", h), ("nbo", B("cs", (0, 16))), ("id", B("hj")))
+        mms(B("b5", (256, 272)), ("id", B("trph")), ("idk", B("f0")))
+        mms(B("b5", (272, 288)), ("id", B("trpm")), ("idp", h))
+        for bank in ("b3", "b2"):
+            zero(bank)
+        ts(B("ke", (0, 32)), B("kc", (0, 32)), 31, AND)
+        scan(B("sc", (768, 1024)), B("resx"), k1, A.add, A.max)
+        cp(B("eu", (0, 32)), B("ke", (0, 32)))
         cp(B("offu"), off)
-        for m in range(16):
-            mm(B("b4", (0, 16), (2 * m, 2 * m + 2)), B("bm", m), B("moh"), True, True)
         agat(B("plg"), B("plw"), B("offu"), scale=1.0 / 32)
+        cp(B("kc", (32, 64)), B("sc", (527, 1024, 16)))
         gat_tt(B("ns"), B("oh"), B("eu", (0, 32)), B("lic"), A.mult)
-        agat(B("ohw"), B("oh"), B("eu", (32, 64)))
+        ts(B("ke", (32, 64)), B("kc", (32, 64)), 31, AND)
+        tt(B("ub"), B("uf"), B("b5", (256, 288)), A.max)
+        cp(B("eu", (32, 64)), B("ke", (32, 64)))
         scat_add(B("pk"), B("offu"), B("u2f"), B("qf"))
         vp, num, dd = B("b7", (256, 512)), B("b7", (0, 16)), B("b5", (0, 256))
-        mm(vp, B("id"), B("plg"), True, False)
-        for s in range(2):
-            mm(vp, B("bo"), B("ns", (256 * s, 256 * s + 256)), False, s == 1)
+        mms(vp, ("id", B("plg")), ("bo", B("ns", (0, 256))), ("bo", B("ns", (256, 512))))
         ac(B("vps"), vp, AF.Copy)
-        mm(dd, B("nid"), B("trib"), True, False)
+        agat(B("ohw"), B("oh"), B("eu", (32, 64)))
         for m in range(16):
             mm(num, lm(m), B("vps", (m, 256, 16)), m == 0, m == 15)
-        mm(dd, B("nid"), B("vps"), False, False)
-        cp(B("u2i"), B("pk", (0, CAP)))
-        tt(B("zu"), B("trp"), B("ok"), A.mult)
-        tt(B("qs"), B("pk", (0, CAP)), B("u2i"), A.subtract)
-        tt(B("um"), B("u2i"), B("dm"), A.mult)
-        for i in range(GV, 16):
-            ac(B("qg", (i, 1024, 16)), B("qs"), AF.Copy, scale=2048.0)
         ac(B("numc"), num, AF.Copy, scale=1.0 / 512)
-        for m in range(16):
-            mm(B("b5", (m, 256, 16)), B("id"), B("numc"), False, m == 15)
-        tt(B("ub"), B("zu"), B("uf"), A.max)
+        ac(B("tn"), num, AF.Identity, bias=B("trx"), scale=-1.0)
+        agat(B("nex"), B("numc"), B("expl"))
+        cp(B("u2i"), B("pk", (0, CAP)))
+        tt(B("um"), B("u2i"), B("dm"), A.mult)
+        tt(B("qs"), B("pk", (0, CAP)), B("u2i"), A.subtract)
         scan(B("us"), B("resa"), B("um"), A.mult, A.add)
-        ts(B("qg", (0, 1024, 16)), B("qs"), 2048.0, A.mult)
-        cp(B("u2u"), B("us", (15, 64, 16)))
-        for i in range(1, GV):
-            ts(B("qg", (i, 1024, 16)), B("qs"), 2048.0, A.mult)
-        for kind in KINDS:
+        for kind in KINDS[t]:
             arrived(kind, t)
-        gat(B("lig"), B(pr, (LP, LP + V)), B("u2u"))
         ts(B("numu"), num, 1.0 / 16, A.mult, float(PAD + Z), A.add)
-        xg, g0, g1 = B(xr, (0, H + CAP * t)), B("dg", (CAP, CAP + 512)), B("dg", (CAP + 512, CAP + 1024))
-        mm(B("b3"), B("nid"), B("qg", (512, 1024)), True, False)
-        agat(g1, xg, B("lig", (32, 64)))
-        mm(B("b3"), B("id"), g1, False, True)
-        gat_tt(g0, xg, B("lig", (0, 32)), B("qg", (0, 512)), A.subtract)
-        ac(B("adg", (0, 2)), g0, AF.Abs, scale=64.0)
-        ac(B("adg", (2, 4)), B("b3"), AF.Abs, scale=64.0)
-        gat_tt(B("sh"), B("x", (0, TRX)), B("numu"), B("q"), A.add)
+        cp(B("u2u"), B("us", (15, 64, 16)))
+        mm(dd, B("nid"), B("trib"), True, False)
+        mm(dd, B("nid"), B("vps"), False, False)
+        minus("b3", B("idq"), B("qs", (32, 64)))
+        mm(dd, B("id"), B("nex"), False, True)
+        minus("b2", B("idq"), B("qs", (0, 32)))
         ts(B("th2k"), B(pr, (LP - 1, LP)), 2048.0, A.mult)
-        ts(B("dg", (0, CAP // 2)), B("qs", (0, CAP // 2)), -2048.0, A.mult)
+        gat(B("lig"), B(pr, (LP, LP + V)), B("u2u"))
         ts(B("thp"), B("jb", (0, 4)), B("th2k"), A.add)
-        ts(B("qz", (0, CAP // 2)), B("qs", (0, CAP // 2)), 2048.0, A.mult)
+        xg, g0, g1 = B(xr, (0, H + CAP * t)), B("dg", (CAP, CAP + 512)), B("dg", (CAP + 512, CAP + 1024))
+        agat(g1, xg, B("lig", (32, 64)))
+        gat(g0, xg, B("lig", (0, 32)))
+        mm(B("b3"), B("id"), g1, False, True)
+        mm(B("b2"), B("id"), g0, False, True)
         ac(B("da"), dd, AF.Abs, scale=float(2 ** 21))
-        ac(B("rnh"), B("sh"), AF.Identity, bias=1279.75, scale=0.5)
-        ac(B("rn"), B("rnh"), AF.Identity, bias=-1280.0)
-        gk = B("b0", (320, 384))
+        ac(B("adg", (2, 4)), B("b3"), AF.Abs, scale=64.0)
+        ac(B("adg", (0, 2)), B("b2"), AF.Abs, scale=64.0)
+        mms(B("b1"), ("id", B("lic")), ("kn", B("ohw")))
+        ac(B("t1"), B("b1"), AF.Relu, bias=float(Z), scale=32.0)
+        gk = B("b6", (256, 320))
         mm(gk, B("id"), B("pcg"), True, False)
         for m in range(16):
             mm(gk, lm(m), B("adg", (0, 4), m), False, m == 15)
-        mm(B("b3"), B("id"), B("lic"), True, False)
-        mm(B("b3"), B("kn"), B("ohw"), False, True)
-        mm(B("b2"), B("kp"), B("ohw"), True, False)
+        mm(B("b0"), B("kp"), B("ohw"), True, False)
         for s in range(2):
-            mm(B("b2", (256 * s, 256 * s + 256)), B("id"), B("vps"), False, s == 1)
+            mm(B("b0", (256 * s, 256 * s + 256)), B("id"), B("vps"), False, s == 1)
+        mothers()
+        gat_tt(B("sh"), B("x", (0, TRX)), B("numu"), B("q"), A.add)
         scan(B("am"), B("resn"), B("da"), A.max, A.min)
-        tt(B("a2"), B("am", (15, 256, 16)), h, A.mult)
-        tt(B("xt"), B("trx"), B("a2"), A.subtract)
-        tt(B("xo"), B("xt"), num, A.max)
-        ts(B("xoff", (0, 32, 2)), B("xo"), 1.0 / 16, A.mult, float(PAD + Z), A.add)
-        records(range(15, 11, -1))
+        ts(B("rn"), B("sh"), 1, SHR)
+        tt(B("xo"), B("am", (15, 256, 16)), B("tn"), A.min)
+        ts(B("xoff", (0, 32, 2)), B("xo"), -1.0 / 16, A.mult, B("trc"), A.add)
+        records(NR)
         scan(B("sg2"), B("resn", (0, 64)), gk, A.max, A.min)
-        records([11])
+        records()
         tt(B("gkc"), B("sg2", (15, 64, 16)), B("thp"), A.min)
-        records([10])
+        records()
         ts(B("gpos"), B("gkc"), 2047, AND)
-        records([9])
+        records()
         cp(B("posu"), B("gpos"))
-        records([8])
-        gat_tt(B("gw", (0, CAP)), B("dg"), B("posu"), B("qz"), A.add)
+        records()
+        gat(B("gw", (0, CAP)), B("dg"), B("posu"))
         agat(B("fw", (0, CAP)), B("flw"), B("posu"))
         agat(B("c"), B("fw"), B("offu"))
-        ac(B("t1"), B("b3"), AF.Relu, bias=float(Z), scale=32.0)
-        ac(B("t2"), B("b2"), AF.Relu, bias=float(Z - 4096), scale=32.0)
-        if end:
-            ac(B("ym2"), B("b4"), AF.Copy)
-            dma("y", T.ym[:], T.z_ym2[0:128:16, :], (B("ym2"),), ())
+        ac(B("t2"), B("b0"), AF.Relu, bias=float(Z - 4096), scale=32.0)
         tr = B("b6", (96, 112))
         mm(tr, B("id"), B("trph"), True, False)
         mm(tr, B("idk"), h, False, False)
         for m in range(16):
             mm(tr, lm(m), B("c", (m, 256, 16)), False, m == 15)
         gcol = B("x", (PAD + H + CAP * t, PAD + H + CAP * t + CAP))
-        records([7])
+        records()
         if not end:
             gat_tt(B("s1"), B("gw"), B("offu"), B("sh"), A.add)
-            records([6])
+            records()
             ts(B("s2"), B("s1"), 255, AND)
-            records([5])
+            records()
             cp(B("q"), B("s2"))
             parity(False)
-            records([4])
-            qrep("s", QV + QG, 16)
-            records(range(3, 0, -1))
+            qrep("s", QV, 16)
+            records()
             ts(B("got"), tr, 0.0, A.is_lt)
             mm(par, B("sg"), B("got"), False, True)
-            records([0])
-            send("x", t + 1)
-            qrep("g", QV, QV + QG)
+            records()
         else:
-            records(range(6, -1, -1))
+            ac(B("ym2"), B("b4"), AF.Copy)
+            dma("y", T.ym[:], T.z_ym2[0:128:16, :], (B("ym2"),), ())
+            records(len(left) - 3)
         for s in range(2):
             tt(B("po", (16 * s, 16 * s + 16)), B("ub", (16 * s, 16 * s + 16)), tr, A.max)
-        cp(gcol, B("gw", (0, CAP)))
-        if end:
-            dma("y", T.yx[:], B("x", (PAD, TRX))[0], (B("x", (PAD, TRX)),), ())
+            records()
         cp(B("poff"), B("po"))
-        if not end:
+        records(16)
+        if end:
+            dma("y", T.yx[:, 0:H + 2 * CAP], B("x", (PAD, PAD + H + 2 * CAP))[0], (B("x", (PAD, PAD + H + 2 * CAP)),), ())
+            ac(gcol, B("gw", (0, CAP)), AF.Copy)
+            dma("y", T.yx[:, H + 2 * CAP:W], gcol[0], (gcol,), ())
+        else:
+            send("x", t + 1)
+            send("y", t + 1)
+            iota(B("x", (0, PAD)), [[0, PAD]])
+            towns(0)
+            cp(gcol, B("gw", (0, CAP)))
             send("c", t + 1)
+            towns(1)
         scat_add(B("pt", (LP, LP + V + 256)), B("poff", (16, 32)), B("t1", (256, 512)), B("t2", (256, 512)))
         if not end:
-            towns(0)
+            towns(2)
+            towns(3)
         scat_add(B("pt", (LP, LP + V + 256)), B("poff", (0, 16)), B("t1", (0, 256)), B("t2", (0, 256)))
         if not end:
             send("p", t + 1)
-            towns(1)
-            qrep("v", 0, QV // 2)
-            towns(2)
-            towns(3)
-            qrep("v", QV // 2, QV)
+            towns(4)
+            qrep("v", 0, 1)
             gat(B("li"), lists, B("uu"))
+            qrep("v", 1, QV)
             agat(B("lic"), lists, B("uu"), bias=-Z / 32, scale=1.0 / 32)
     dma("s", T.yp[:], lists[0], (lists,), ())
     for s, v in total.items():

@@ -10,8 +10,7 @@ BIG = float(2 ** 30)
 MID = float(2 ** 20)
 Z = 1408
 RAW = {0: ("b2", "b3"), 4: ("b5", "b7")}
-QV, QV0 = 2, 4
-NR = 5
+QV, QG, QV0 = 0, 3, 3
 
 BUF, AT = {}, {}
 SCRATCH = {}
@@ -35,21 +34,21 @@ def _pack(dtype, **kw):
 _add("sbuf", "int32", pti=LP + V, pr0=LP + V, moi=V, s1=256, s2=256, sh=256, rn=256)
 _pack("int32", pc=1, pmi=1, pgi=1, podd=1, bi=16, bq=16, kc=64, ke=64, u2i=64, gkc=4, gpos=4)
 _add("sbuf", "uint16", li=512)
-_pack("uint16", uu=32, offu=16, numu=16, xoff=32, poff=32, u2u=4, posu=4, lig=64, eu=64, expl=16)
-_add("sbuf", "bfloat16", x=TRX + 16, q=256, qrep=3072, d=8192, dr=[32, 256], ad=[32, 16, 16], bm=[16, 128], zl=144, zw=144, zn=144,
+_pack("uint16", uu=32, offu=16, numu=16, xoff=32, poff=32, u2u=4, posu=4, lig=64, eu=64, expl=16, exp2=32)
+_add("sbuf", "bfloat16", x=TRX + 32, q=256, qrep=3072, d=8192, dr=[32, 256], ad=[32, 16, 16], bm=[16, 128], zl=144, zw=144, zn=144,
      z2=144, ci=64, resn=256, resx=256, nt=128, dg=CAP + 1024, flw=CAP + 1024, adg=[4, 16, 16], xr0=H + 16, xr1=H + CAP,
-     xr2=H + 2 * CAP, fw=512, gw=512, ohw=512, nil=512)
-_pack("bfloat16", id=128, nid=128, bo=128, nbo=128, ntri=128, idk=128, idp=128, idq=128, kp=128, kn=128, sw=128, swd=128, sg=128,
-      one=128, ef=144, it=256, dm=64, trib=256, resa=64, c=256, da=256, am=256, jb=16, zz=16, h=16, f0=16, cs=32, xk=16, qs=64,
+     xr2=H + 2 * CAP, fw=512, gw=512, ohw=512, nil=512, res2=512, da=512, am=512)
+_pack("bfloat16", id=128, nid=128, bo=128, nbo=128, ntri=128, idk=128, idp=128, idq=128, kp=128, kn=128, sw=128, sg=128,
+      one=128, ef=144, it=256, dm=64, trib=256, resa=64, c=256, jb=16, zz=16, h=16, f0=16, cs=32, xk=16, qs=64,
       got=16, oh=32)
 _add("sbuf", "float16", moh=[16, 2], mo8=[16, 32], e8=128, z8=144, pcg=64)
-_pack("float16", lic=512, ns=512, plg=256, vps=256, uf=32, dmo=16, dl=16, d1=16, rj=16, hj=16, nex=256, trph=16, trpm=16)
+_pack("float16", lic=512, ns=512, plg=256, vps=256, uf=32, dmo=16, dl=16, d1=16, rj=16, hj=16, nex=512, trph=16, trpm=16)
 _add("sbuf", "float32", pt=LP + V + 256, pr1=LP + V, pr2=LP + V, mw=V, pf=1, sc=1024, sg2=64, ym2=V, plw=512, t1=512, t2=512,
      pk=512, u2f=256, qf=256)
-_pack("float32", pm=1, pg=1, pz=1, pidx=1, widx=1, evc=1, th32=1, thb=1, th2k=1, c1=1, c2=1, c3=1, trx=1, trc=1, j2=16, t16=16,
+_pack("float32", pm=1, pg=1, pz=1, pidx=1, widx=1, evc=1, th32=1, thb=1, th2k=1, c1=1, c2=1, c3=1, trx=1, trc=1, trx1=1, trc1=1, j2=16, t16=16,
       tn=16, numc=16, thl=16, thq=32, thp=4, xo=16, um=64, us=64, ub=32, po=32)
 _add("psum", "float32", b0=512, b1=512, b2=512, b3=512, b4=[16, 32], b5=512, b6=512, b7=512)
-KINDS = ("pxyz", "xycp", "xycp")
+KINDS = ("pxyz", "xypc", "xypc")
 THIRD = 880
 NCORES = 256
 SEMAPHORES = (["sv", "sa", "st", "sg"] + ["dma%d" % i for i in range(16)]
@@ -104,6 +103,8 @@ def _pieces(T, topo, r, t, kind):
             lo, n = old // 2 * (kind == "y"), old // 2 // len(ways)
         on = [w for w in ways if w[0] in chip]
         left = [e for e in topo.engines(src, on[0][0]) if e not in sum(out, [])] if on else []
+        if kind == "z" and out:
+            left = out[0]
         PLAN[(r, t, kind)] = [
             (w, out[0] if w not in on else left[on.index(w) * len(left) // len(on):(on.index(w) + 1) * len(left) // len(on)],
              lo + n * k, lo + n * k + n) for k, w in enumerate(ways)]
@@ -321,6 +322,8 @@ def rank_program(g, core, T, topo):
         for i in range(lo, hi):
             if q == "v":
                 cp(B("qrep", (i, 3072, 16)), B("q", (64, 256)))
+            elif q == "g":
+                pick(B("qrep", (i, 3072, 16)), B("q", (64, 256)), [[0, 192]], A.is_ge, 0.0, 0, 0)
             else:
                 ac(B("qrep", (i, 3072, 16)), B("q", (64, 256)), AF.Copy)
 
@@ -333,7 +336,7 @@ def rank_program(g, core, T, topo):
 
     def parity(last):
         for m in range(16):
-            mm(par, lm(m, "zw"), B("q", (m, 256, 16)), m == 0, last and m == 15)
+            mm(par, lm(m, "zw"), B("q", (m, 256, 16)), last and m == 0, m == 15)
 
     def towns(step):
         if step == 0:
@@ -348,13 +351,15 @@ def rank_program(g, core, T, topo):
         else:
             cp(B("uu"), B("uf"))
 
-    dma("y", B("q")[0], T.qs[:], (), (B("q"),))
-    dma("s", B("pti", (LP - 1, LP))[0], T.th[:], (), (B("pti", (LP - 1, LP)),))
-    dma("y", B("pti", (LP, LP + V))[0], T.towns[:], (), (B("pti", (LP, LP + V)),))
+    def first_lists():
+        for lo, hi in ((0, 4), (16, 32), (4, 16)):
+            gat(B("li", (16 * lo, 16 * hi)), lists, B("uu", (lo, hi)))
+
     dma("s", T.z_moi[0:8, :], T.mo[:], (), (B("moi"),))
-    for lo in range(0, H, THIRD):
-        part = B("x", (PAD + lo, PAD + min(lo + THIRD, H)))
-        dma("y", part[0], T.x[:, lo:min(lo + THIRD, H)], (), (part,))
+    dma("y", B("pti", (LP, LP + V))[0], T.towns[:], (), (B("pti", (LP, LP + V)),))
+    dma("s", B("pti", (LP - 1, LP))[0], T.th[:], (), (B("pti", (LP - 1, LP)),))
+    dma("y", B("q")[0], T.qs[:], (), (B("q"),))
+    dma("y", B("x", (PAD, PAD + H))[0], T.x[:], (), (B("x", (PAD, PAD + H)),))
     iota(B("pc"), [[1, 1]], 0, 1)
     iota(B("ef"), [[1, 144]])
     fill(B("one"), 1.0)
@@ -400,44 +405,51 @@ def rank_program(g, core, T, topo):
     ts(B("sw"), e128, B("c2"), A.is_equal)
     ts(B("oh", (0, 16)), B("ef", (0, 16)), B("pidx"), A.is_equal)
     ts(B("oh", (16, 32)), B("ef", (16, 32)), B("widx"), A.is_equal)
-    cp(B("expl"), B("ef", (0, 16)))
+    for out in (B("expl"), B("exp2", (0, 32, 2)), B("exp2", (1, 32, 2))):
+        cp(out, B("ef", (0, 16)))
     fill(B("zz"), 0.0)
     fill(B("cs"), 0.0)
-    iota(B("da"), [[0, 256]], 2)
+    iota(B("da", (0, 256)), [[0, 256]], 2)
+    send("p", 0)
     pick(B("resn"), B("nil", (0, 256)), [[0, 16], [1, 16]], A.is_gt, BIG, 0, 0)
-    for kind in KINDS[0]:
+    qrep("g", QV0, QV0 + QG)
+    for kind in KINDS[0][1:]:
         send(kind, 0)
-    pick(B("resx"), B("da"), [[0, 16], [1, 16]], A.is_gt, -BIG, 0, 0)
+    pick(B("resx"), B("da", (0, 256)), [[0, 16], [1, 16]], A.is_gt, -BIG, 0, 0)
     pick(B("ntri"), B("nbo"), [[1, 128]], A.is_gt, 0.0, 0, -1)
-    parity(True)
-    qrep("s", QV0, 16)
-    fill(B("dg", (0, CAP)), 0.0)
-    qrep("v", 0, QV0)
+    ac(B("plw", (256, 512)), B("nil", (0, 256)), AF.Copy)
+    ac(B("plw", (CAP, 256)), B("nil", (CAP, 256)), AF.Identity, bias=-float(PAD + Z))
+    ac(B("pt", (0, LP - 1)), B("nil", (0, LP - 1)), AF.Copy)
+    ac(B("trx1"), B("trx"), AF.Identity, bias=256.0)
+    ac(B("trc1"), B("trc"), AF.Identity, bias=16.0)
+    for name, c in (("idp", 1024.0), ("idq", -2048.0), ("kp", 128.0), ("kn", -128.0)):
+        ac(B(name), B("id"), AF.Copy, scale=c)
+    qrep("s", QV0 + QG, 16)
     cp(rows8("mo8"), rows8("moi"))
     for m in range(16):
         mm(B("b7", (0, 32)), rows8("z8", (15 - m, 143 - m)), rows8("mo8", (0, 16), (2 * m, 2 * m + 2)), m == 0, m == 15)
+    parity(True)
     mm(B("b4"), rows8("e8"), rows8("mo8"), True, True)
-    towns(0)
-    tt(B("swd"), B("sw"), B("id"), A.subtract)
-    towns(1)
+    fill(B("dg", (0, CAP)), 0.0)
+    ts(B("um"), B("nt", (0, 64)), 256.0, A.mult, B("c3"), A.add)
+    ts(B("trib"), B("it"), B("pm"), A.is_ge, 1024.0, A.mult)
+    tt(B("pcg"), B("um"), B("it", (0, 64)), A.add)
+    cp(B("pt", (LP - 1, LP + V)), B("pti", (LP - 1, LP + V)))
     cp(B("moh"), B("b7", (0, 32)))
     ts(B("th32"), B("pti", (LP - 1, LP)), 32.0, A.mult)
     ts(B("dm"), B("it", (0, 64)), B("pm"), A.is_equal)
     tt(B("dmo"), m1, m0, A.subtract)
-    ts(B("thb"), B("th32"), MID, A.add)
-    ts(B("thq", (0, 16)), B("jb"), 0.0, A.mult, B("th32"), A.add)
+    qrep("v", 0, QV0 - 2)
+    towns(0)
+    ts(B("sg"), i128, B("pm"), A.is_equal)
+    towns(1)
+    qrep("v", QV0 - 2, QV0 - 1)
     towns(2)
     towns(3)
-    ts(B("sg"), i128, B("pm"), A.is_equal)
+    qrep("v", QV0 - 1, QV0)
     towns(4)
-    ts(B("um"), B("nt", (0, 64)), 256.0, A.mult, B("c3"), A.add)
-    gat(B("li"), B("pti", (LP, LP + V)), B("uu"))
-    cp(B("pt", (LP - 1, LP + V)), B("pti", (LP - 1, LP + V)))
-    ts(B("trib"), B("it"), B("pm"), A.is_ge, 1024.0, A.mult)
-    tt(B("pcg"), B("um"), B("it", (0, 64)), A.add)
-    ac(B("plw", (256, 512)), B("nil", (0, 256)), AF.Copy)
-    ac(B("plw", (CAP, 256)), B("nil", (CAP, 256)), AF.Identity, bias=-float(PAD + Z))
-    ac(B("pt", (0, LP - 1)), B("nil", (0, LP - 1)), AF.Copy)
+    ts(B("thb"), B("th32"), MID, A.add)
+    first_lists()
 
     def mothers():
         for m in range(16):
@@ -493,11 +505,12 @@ def rank_program(g, core, T, topo):
                 src = B("dr", (4 * k, 4 * k + 4), (16 * m, 16 * m + 16)) if part == 0 else B("ad", (4 * k, 4 * k + 4), m)
                 mm(out, lm(m, {None: "zl", 0: "zn", 1: "z2"}[part]), src, False, part != 0 and m == 15)
 
-        left = list(range(15, -1, -1))
+        wide = 2 if end else 1
+        left = list(range(16 // wide - 1, -1, -1))
 
         def records(count=1):
             for n in [left.pop(0) for _ in range(min(count, len(left)))]:
-                scat(B("x"), B("xoff", (2 * n, 2 * n + 1)), B("rn", (16 * n, 16 * n + 16)))
+                scat(B("x"), B("xoff", (2 * n, 2 * n + wide)), B("rn", (16 * wide * n, 16 * wide * (n + 1))))
 
         pick(B("pk", (0, CAP)), B("plw", (256, 256 + CAP)), [[0, CAP]], A.is_gt, 0.25, 0, 0)
         iota(B("plw", (0, CAP)), [[1, CAP]], H - Z + CAP * t)
@@ -511,15 +524,18 @@ def rank_program(g, core, T, topo):
                 pick(B("bm", m), B("one"), [[-16, 8], [0, 16]], A.is_equal, 0.0, -m, 1)
         raw_q(0)
         raw_q(4)
+        if t == 1:
+            pick(B("res2"), B("nil"), [[0, 16], [1, 32]], A.is_gt, BIG, 0, 0)
+            mothers()
         raw(0)
         raw_x(0)
         rows(7)
         reduce(7, 0)
         raw(4)
+        diff(1)
+        raw_x(4)
         relu(7)
         reduce(7, 1)
-        raw_x(4)
-        diff(1)
         raw_abs(0)
         reduce(0)
         absd(1)
@@ -530,6 +546,8 @@ def rank_program(g, core, T, topo):
         for k in (2, 3, 5):
             if k > 2:
                 diff(k)
+            if k == 5:
+                agat(B("lic", (0, 256)), lists, B("uu", (0, 16)), bias=-Z / 32, scale=1.0 / 32)
             absd(k)
             reduce(k)
         for half in range(2):
@@ -538,97 +556,113 @@ def rank_program(g, core, T, topo):
         scan(B("sc", (0, 256)), B("resn"), k0, A.max, A.min)
         scan(B("sc", (512, 768)), B("resx"), k0, A.add, A.max)
         ts(B("f0"), best0, B("th32"), A.is_ge)
-        mm(B("b6", (48, 64)), B("swd"), u1, True, True)
+        ts(B("kc", (0, 16)), best0, B("th32"), A.min)
+        mms(B("b6", (48, 64)), ("sw", u1), ("nid", u1))
         mm(B("b6", (64, 80)), B("sw"), B("f0"), True, True)
         reduce(6)
         ts(B("thl"), B("f0"), -MID, A.mult, B("thb"), A.add)
-        ac(B("mw"), B("b4"), AF.Copy)
+        agat(B("lic", (256, 512)), lists, B("uu", (16, 32)), bias=-Z / 32, scale=1.0 / 32)
+        if not end:
+            ac(B("mw"), B("b4"), AF.Copy)
         ac(B("qf"), B("q"), AF.Copy, scale=1.0 / 2048)
         agat(B("u2f"), B("mw"), B("uu", (16, 32)))
-        if t == 0:
-            agat(B("lic"), lists, B("uu"), bias=-Z / 32, scale=1.0 / 32)
-            for name, c in (("idp", 1024.0), ("idq", -2048.0), ("kp", 128.0), ("kn", -128.0)):
-                ac(B(name), B("id"), AF.Copy, scale=c)
+        ts(B("ke", (0, 16)), B("kc", (0, 16)), 31, AND)
         ts(B("thq", (16, 32)), B("f0"), B("th32"), A.mult)
+        cp(B("eu", (0, 16)), B("ke", (0, 16)))
         tt(B("xk"), B("b6", (64, 80)), B("f0"), A.mult)
-        tt(B("dl"), B("b6", (48, 64)), B("xk"), A.mult)
-        tt(B("d1"), B("dl"), B("bq"), A.mult)
-        mms(B("b7", (128, 160, 2)), ("id", m0), ("id", B("dl")), ("nid", B("d1")))
-        mms(B("b7", (129, 160, 2)), ("id", m1), ("id", B("d1")))
-        mms(B("b7", (160, 176)), ("id", B("dmo")), ("id", B("d1")), ("id", B("d1")), ("nid", B("dl")))
-        ac(B("moh"), B("b7", (128, 160)), AF.Copy)
-        ac(B("dmo"), B("b7", (160, 176)), AF.Copy)
+        gat_tt(B("ns", (0, 256)), B("oh"), B("eu", (0, 16)), B("lic", (0, 256)), A.mult)
         scan(B("sc", (256, 512)), B("resn"), k1, A.max, A.min)
+        tt(B("dl"), B("b6", (48, 64)), B("xk"), A.mult)
         tt(h, best1, B("thl"), A.is_lt)
-        tt(B("kc", (0, 32)), B("sc", (15, 512, 16)), B("thq"), A.min)
+        tt(B("kc", (16, 32)), best1, B("thq", (16, 32)), A.min)
         scan(B("cs", (1, 17)), h, B("zz"), A.add, A.add)
         tt(B("hj"), h, B("rj"), A.mult)
+        ts(B("ke", (16, 32)), B("kc", (16, 32)), 31, AND)
+        tt(B("d1"), B("dl"), B("bq"), A.mult)
         off = B("b6", (16, 32))
         mms(off, ("id", B("jb")), ("ntri", h), ("nbo", B("cs", (0, 16))), ("id", B("hj")))
         mms(B("b5", (256, 272)), ("id", B("trph")), ("idk", B("f0")))
         mms(B("b5", (272, 288)), ("id", B("trpm")), ("idp", h))
-        for bank in ("b3", "b2"):
-            zero(bank)
-        ts(B("ke", (0, 32)), B("kc", (0, 32)), 31, AND)
-        scan(B("sc", (768, 1024)), B("resx"), k1, A.add, A.max)
-        cp(B("eu", (0, 32)), B("ke", (0, 32)))
+        mms(B("b0", (128, 160, 2)), ("id", m0), ("id", B("dl")), ("nid", B("d1")))
+        mms(B("b0", (129, 160, 2)), ("id", m1), ("id", B("d1")))
+        mms(B("b0", (160, 176)), ("id", B("dmo")), ("id", B("d1")), ("id", B("d1")), ("nid", B("dl")))
+        cp(B("eu", (16, 32)), B("ke", (16, 32)))
         cp(B("offu"), off)
         agat(B("plg"), B("plw"), B("offu"), scale=1.0 / 32)
-        cp(B("kc", (32, 64)), B("sc", (527, 1024, 16)))
-        gat_tt(B("ns"), B("oh"), B("eu", (0, 32)), B("lic"), A.mult)
-        ts(B("ke", (32, 64)), B("kc", (32, 64)), 31, AND)
-        tt(B("ub"), B("uf"), B("b5", (256, 288)), A.max)
-        cp(B("eu", (32, 64)), B("ke", (32, 64)))
+        gat_tt(B("ns", (256, 512)), B("oh"), B("eu", (16, 32)), B("lic", (256, 512)), A.mult)
         scat_add(B("pk"), B("offu"), B("u2f"), B("qf"))
-        vp, num, dd = B("b7", (256, 512)), B("b7", (0, 16)), B("b5", (0, 256))
-        mms(vp, ("id", B("plg")), ("bo", B("ns", (0, 256))), ("bo", B("ns", (256, 512))))
+        vp, num, dd = B("b7", (256, 512)), B("b7", (0, 16)), B("b4") if end else B("b5", (0, 256))
+        mms(vp, ("bo", B("ns", (0, 256))), ("bo", B("ns", (256, 512))), ("id", B("plg")))
+        for bank in ("b3", "b2"):
+            zero(bank)
         ac(B("vps"), vp, AF.Copy)
-        agat(B("ohw"), B("oh"), B("eu", (32, 64)))
+        ac(B("moh"), B("b0", (128, 160)), AF.Copy)
+        ac(B("dmo"), B("b0", (160, 176)), AF.Copy)
         for m in range(16):
             mm(num, lm(m), B("vps", (m, 256, 16)), m == 0, m == 15)
         ac(B("numc"), num, AF.Copy, scale=1.0 / 512)
-        ac(B("tn"), num, AF.Identity, bias=B("trx"), scale=-1.0)
-        agat(B("nex"), B("numc"), B("expl"))
+        for a, col in enumerate(("trx", "trx1")[:wide]):
+            ac(B("tn", (a, 16, wide)), B("b7", (a, 16, wide)), AF.Identity, bias=B(col), scale=-1.0)
+        nex, da, am = (B(n, (0, 256 * wide)) for n in ("nex", "da", "am"))
+        agat(nex, B("numc"), B("exp2" if end else "expl"))
+        for kind in KINDS[t]:
+            arrived(kind, t)
+        tt(B("ub"), B("uf"), B("b5", (256, 288)), A.max)
         cp(B("u2i"), B("pk", (0, CAP)))
         tt(B("um"), B("u2i"), B("dm"), A.mult)
         tt(B("qs"), B("pk", (0, CAP)), B("u2i"), A.subtract)
         scan(B("us"), B("resa"), B("um"), A.mult, A.add)
-        for kind in KINDS[t]:
-            arrived(kind, t)
-        ts(B("numu"), num, 1.0 / 16, A.mult, float(PAD + Z), A.add)
         cp(B("u2u"), B("us", (15, 64, 16)))
-        mm(dd, B("nid"), B("trib"), True, False)
-        mm(dd, B("nid"), B("vps"), False, False)
+        if end:
+            mm(dd, B("nil", (0, 128)), B("nil"), True, False)
+            mm(B("b4", (0, 16, 2), (16, 32)), B("idk"), B("one"), False, False)
+            for a in range(2):
+                mm(B("b4", (a, 16, 2), (16 * a, 16 * a + 16)), B("nid"), B("trib", (0, 128)), False, False)
+                mm(B("b4", (a, 16, 2)), B("nid"), B("vps"), False, False)
+        else:
+            mm(dd, B("nid"), B("trib"), True, False)
+            mm(dd, B("nid"), B("vps"), False, False)
         minus("b3", B("idq"), B("qs", (32, 64)))
-        mm(dd, B("id"), B("nex"), False, True)
+        mm(dd, B("id"), nex, False, True)
         minus("b2", B("idq"), B("qs", (0, 32)))
-        ts(B("th2k"), B(pr, (LP - 1, LP)), 2048.0, A.mult)
         gat(B("lig"), B(pr, (LP, LP + V)), B("u2u"))
-        ts(B("thp"), B("jb", (0, 4)), B("th2k"), A.add)
         xg, g0, g1 = B(xr, (0, H + CAP * t)), B("dg", (CAP, CAP + 512)), B("dg", (CAP + 512, CAP + 1024))
         agat(g1, xg, B("lig", (32, 64)))
+        scan(B("sc", (768, 1024)), B("resx"), k1, A.add, A.max)
+        ts(B("numu"), num, 1.0 / 16, A.mult, float(PAD + Z), A.add)
         gat(g0, xg, B("lig", (0, 32)))
         mm(B("b3"), B("id"), g1, False, True)
         mm(B("b2"), B("id"), g0, False, True)
-        ac(B("da"), dd, AF.Abs, scale=float(2 ** 21))
+        ac(da, dd, AF.Abs, scale=float(2 ** 21))
+        if t:
+            mothers()
         ac(B("adg", (2, 4)), B("b3"), AF.Abs, scale=64.0)
         ac(B("adg", (0, 2)), B("b2"), AF.Abs, scale=64.0)
-        mms(B("b1"), ("id", B("lic")), ("kn", B("ohw")))
-        ac(B("t1"), B("b1"), AF.Relu, bias=float(Z), scale=32.0)
+        if t and not end:
+            ac(B("mw"), B("b4"), AF.Copy)
         gk = B("b6", (256, 320))
         mm(gk, B("id"), B("pcg"), True, False)
         for m in range(16):
             mm(gk, lm(m), B("adg", (0, 4), m), False, m == 15)
+        gat_tt(B("sh"), B("x", (0, TRX)), B("numu"), B("q"), A.add)
+        scan(am, B("res2" if end else "resn"), da, A.max, A.min)
+        cp(B("kc", (32, 64)), B("sc", (527, 1024, 16)))
+        tt(B("xo"), B("am", (16 * wide - 1, 256 * wide, 16 * wide)), B("tn"), A.min)
+        ts(B("ke", (32, 64)), B("kc", (32, 64)), 31, AND)
+        ts(B("rn"), B("sh"), 1, SHR)
+        for a, col in enumerate(("trc", "trc1")[:wide]):
+            ts(B("xoff", (a, 32 // wide, 2)), B("xo", (a, 16, wide)), -1.0 / 16, A.mult, B(col), A.add)
+        cp(B("eu", (32, 64)), B("ke", (32, 64)))
+        records()
+        ts(B("th2k"), B(pr, (LP - 1, LP)), 2048.0, A.mult)
+        records()
+        ts(B("thp"), B("jb", (0, 4)), B("th2k"), A.add)
+        records(0 if end else 2)
+        agat(B("ohw"), B("oh"), B("eu", (32, 64)))
+        mms(B("b1"), ("id", B("lic")), ("kn", B("ohw")))
         mm(B("b0"), B("kp"), B("ohw"), True, False)
         for s in range(2):
             mm(B("b0", (256 * s, 256 * s + 256)), B("id"), B("vps"), False, s == 1)
-        mothers()
-        gat_tt(B("sh"), B("x", (0, TRX)), B("numu"), B("q"), A.add)
-        scan(B("am"), B("resn"), B("da"), A.max, A.min)
-        ts(B("rn"), B("sh"), 1, SHR)
-        tt(B("xo"), B("am", (15, 256, 16)), B("tn"), A.min)
-        ts(B("xoff", (0, 32, 2)), B("xo"), -1.0 / 16, A.mult, B("trc"), A.add)
-        records(NR)
         scan(B("sg2"), B("resn", (0, 64)), gk, A.max, A.min)
         records()
         tt(B("gkc"), B("sg2", (15, 64, 16)), B("thp"), A.min)
@@ -640,6 +674,7 @@ def rank_program(g, core, T, topo):
         gat(B("gw", (0, CAP)), B("dg"), B("posu"))
         agat(B("fw", (0, CAP)), B("flw"), B("posu"))
         agat(B("c"), B("fw"), B("offu"))
+        ac(B("t1"), B("b1"), AF.Relu, bias=float(Z), scale=32.0)
         ac(B("t2"), B("b0"), AF.Relu, bias=float(Z - 4096), scale=32.0)
         tr = B("b6", (96, 112))
         mm(tr, B("id"), B("trph"), True, False)
@@ -647,52 +682,49 @@ def rank_program(g, core, T, topo):
         for m in range(16):
             mm(tr, lm(m), B("c", (m, 256, 16)), False, m == 15)
         gcol = B("x", (PAD + H + CAP * t, PAD + H + CAP * t + CAP))
-        records()
+        records(16 if end else 1)
         if not end:
             gat_tt(B("s1"), B("gw"), B("offu"), B("sh"), A.add)
             records()
             ts(B("s2"), B("s1"), 255, AND)
             records()
             cp(B("q"), B("s2"))
-            parity(False)
-            qrep("s", QV, 16)
             records()
             ts(B("got"), tr, 0.0, A.is_lt)
-            mm(par, B("sg"), B("got"), False, True)
-            records()
+            mm(par, B("sg"), B("got"), True, False)
+            parity(False)
+            qrep("s", QV + QG, 16)
+            qrep("g", QV, QV + QG)
         else:
+            cp(gcol, B("gw", (0, CAP)))
+            dma("y", T.yx[:], B("x", (PAD, TRX))[0], (B("x", (PAD, TRX)),), ())
             ac(B("ym2"), B("b4"), AF.Copy)
             dma("y", T.ym[:], T.z_ym2[0:128:16, :], (B("ym2"),), ())
-            records(len(left) - 3)
-        for s in range(2):
-            tt(B("po", (16 * s, 16 * s + 16)), B("ub", (16 * s, 16 * s + 16)), tr, A.max)
+        for s in (1, 0):
             records()
+            tt(B("po", (16 * s, 16 * s + 16)), B("ub", (16 * s, 16 * s + 16)), tr, A.max)
+        records()
         cp(B("poff"), B("po"))
         records(16)
-        if end:
-            dma("y", T.yx[:, 0:H + 2 * CAP], B("x", (PAD, PAD + H + 2 * CAP))[0], (B("x", (PAD, PAD + H + 2 * CAP)),), ())
-            ac(gcol, B("gw", (0, CAP)), AF.Copy)
-            dma("y", T.yx[:, H + 2 * CAP:W], gcol[0], (gcol,), ())
-        else:
+        if not end:
             send("x", t + 1)
             send("y", t + 1)
-            iota(B("x", (0, PAD)), [[0, PAD]])
-            towns(0)
-            cp(gcol, B("gw", (0, CAP)))
-            send("c", t + 1)
-            towns(1)
         scat_add(B("pt", (LP, LP + V + 256)), B("poff", (16, 32)), B("t1", (256, 512)), B("t2", (256, 512)))
         if not end:
-            towns(2)
-            towns(3)
+            towns(0)
+            cp(gcol, B("gw", (0, CAP)))
+            towns(1)
         scat_add(B("pt", (LP, LP + V + 256)), B("poff", (0, 16)), B("t1", (0, 256)), B("t2", (0, 256)))
         if not end:
             send("p", t + 1)
-            towns(4)
-            qrep("v", 0, 1)
-            gat(B("li"), lists, B("uu"))
-            qrep("v", 1, QV)
-            agat(B("lic"), lists, B("uu"), bias=-Z / 32, scale=1.0 / 32)
+            send("c", t + 1)
+            iota(B("x", (0, PAD)), [[0, PAD]])
+            towns(2)
+            towns(3)
+            qrep("v", 0, QV)
+            cp(B("uu", (0, 16)), u0)
+            cp(B("uu", (16, 32)), u1)
+            first_lists()
     dma("s", T.yp[:], lists[0], (lists,), ())
     for s, v in total.items():
         g.wait_ge(T.sem[s], v)

import numpy as np
from concourse.bass import DstId, RemoteDMATransfer
from concourse.mybir import AluOpType as A, ActivationFunctionType as AF

R_, H, V, K, CAP, N = 3, 2624, 512, 256, 64, 8
PAD, W = 16, 2816
TRX, TRP = PAD + W, V
LP = 8
BIG = float(2 ** 30)
MID = float(2 ** 20)
Z = 1408
RAW = {0: ("b2", "b3"), 4: ("b5", "b7")}
QV, QG, QV0 = 0, 3, 3

BUF, AT = {}, {}
SCRATCH = {}


def _add(where, dtype, **kw):
    for k, v in kw.items():
        BUF[k] = (where, [128] + (v if isinstance(v, list) else [v]), dtype)
        SCRATCH["z_" + k] = BUF[k]


def _pack(dtype, **kw):
    at = 0
    for k, v in kw.items():
        BUF[k] = ("sbuf", [128, v], dtype)
        AT[k] = ("t_" + dtype, at, v)
        at += (v + 15) // 16 * 16
    SCRATCH["t_" + dtype] = ("sbuf", [128, at], dtype)


_add("sbuf", "int32", pti=LP + V, pr0=LP + V, moi=V, s1=256, s2=256, sh=256, rn=256)
_pack("int32", pc=1, pmi=1, pgi=1, podd=1, bi=16, bq=16, kc=64, ke=64, u2i=64, gkc=4, gpos=4)
_add("sbuf", "uint16", li=512)
_pack("uint16", uu=32, offu=16, numu=16, xoff=32, poff=32, u2u=4, posu=4, lig=64, eu=64, expl=16, exp2=32)
_add("sbuf", "bfloat16", x=TRX + 32, q=256, qrep=3072, d=8192, dr=[32, 256], ad=[32, 16, 16], bm=[16, 128], zl=144, zw=144, zn=144,
     z2=144, ci=64, resn=256, resx=256, nt=128, dg=CAP + 1024, flw=CAP + 1024, adg=[4, 16, 16], xr0=H + 16, xr1=H + CAP,
     xr2=H + 2 * CAP, fw=512, gw=512, ohw=512, nil=512, res2=512, da=512, am=512)
_pack("bfloat16", id=128, nid=128, bo=128, nbo=128, ntri=128, idk=128, idp=128, idq=128, kp=128, kn=128, sw=128, sg=128,
      one=128, ef=144, it=256, dm=64, trib=256, resa=64, c=256, jb=16, zz=16, h=16, f0=16, cs=32, xk=16, qs=64,
      got=16, oh=32)
_add("sbuf", "float16", moh=[16, 2], mo8=[16, 32], e8=128, z8=144, pcg=64)
_pack("float16", lic=512, ns=512, plg=256, vps=256, uf=32, dmo=16, dl=16, d1=16, rj=16, hj=16, nex=512, trph=16, trpm=16)
_add("sbuf", "float32", pt=LP + V + 256, pr1=LP + V, pr2=LP + V, mw=V, pf=1, sc=1024, sg2=64, ym2=V, plw=512, t1=512, t2=512,
     pk=512, u2f=256, qf=256)
_pack("float32", pm=1, pg=1, pz=1, pidx=1, widx=1, evc=1, th32=1, thb=1, th2k=1, c1=1, c2=1, c3=1, trx=1, trc=1, trx1=1, trc1=1, j2=16, t16=16,
      tn=16, numc=16, thl=16, thq=32, thp=4, xo=16, um=64, us=64, ub=32, po=32)
_add("psum", "float32", b0=512, b1=512, b2=512, b3=512, b4=[16, 32], b5=512, b6=512, b7=512)
KINDS = ("pxyz", "xypc", "xypc")
THIRD = 880
NCORES = 256
SEMAPHORES = (["sv", "sa", "st", "sg"] + ["dma%d" % i for i in range(16)]
              + [a + k + str(t) for a in ("in", "lo") for t in range(R_) for k in KINDS[t]])


def _mask(es):
    m = 0
    for e in es:
        m |= 1 << e
    return m


def _ways(T, topo, r, t):
    src, dst = T.cores[r], T.cores[(r - 1 - t) % N]
    if dst in topo.cores_of(src):
        return [[dst]]

    def mate(c):
        return [m for m in range(NCORES) if topo.mates(c, m)][0]

    def port(c, die):
        return [k for k in topo.cores_of(c) if topo.die(k) == die and topo.may_write(k, mate(c))][0]
    near, far = port(src, topo.die(src)), port(mate(dst), topo.die(src))
    if topo.may_write(src, dst):
        return [[dst], [near, far, dst]]
    idle = [topo.die(T.cores[a]) for a in range(N)
            if a != r and T.cores[a] in topo.cores_of(src) and T.cores[(a - 1 - t) % N] in topo.cores_of(src)]
    return [[near, dst], [far, dst]] + [[port(src, d), dst] for d in idle]


PLAN = {}


def _pieces(T, topo, r, t, kind):
    if (r, t, kind) not in PLAN:
        src, ways = T.cores[r], _ways(T, topo, r, t)
        old = H + CAP * max(t - 1, 0)
        chip = topo.cores_of(src)
        out = [topo.engines(src, w[0]) for w in ways if w[0] not in chip]
        if kind != "x":
            ways = [w for w in ways if len(w) < 3]
        if kind == "c":
            ways, lo, n = ways[:1], old, CAP
        elif kind == "p":
            n = -(-(V + 1) // len(ways))
            lo = LP + V - n * len(ways)
        elif t == 0:
            k = "xyz".index(kind)
            ways, lo, n = [sorted(ways, key=lambda w: w[0] in chip)[k % len(ways)]], k * THIRD, THIRD
        else:
            lo, n = old // 2 * (kind == "y"), old // 2 // len(ways)
        on = [w for w in ways if w[0] in chip]
        left = [e for e in topo.engines(src, on[0][0]) if e not in sum(out, [])] if on else []
        if kind == "z" and out:
            left = out[0]
        PLAN[(r, t, kind)] = [
            (w, out[0] if w not in on else left[on.index(w) * len(left) // len(on):(on.index(w) + 1) * len(left) // len(on)],
             lo + n * k, lo + n * k + n) for k, w in enumerate(ways)]
    return PLAN[(r, t, kind)]


def _copy(kind, t):
    return "%s%d" % ("pr" if kind == "p" else "xr", t)


def _hand_on(g, core, T, topo):
    sent = []
    for t in range(R_):
        for kind in KINDS[t]:
            for r in range(N):
                for way, es, lo, hi in _pieces(T, topo, r, t, kind):
                    if core in way:
                        k = way.index(core)
                        g.wait_ge(T.sem["in%s%d" % (kind, t)], len(topo.engines(way[k - 1], core) if k else es))
                        rid, pid = topo.addr(way[k + 1], core)
                        ap = T["z_" + _copy(kind, t)][:, lo:hi]
                        g.remote_dma(ap, ap, T.sem["in%s%d" % (kind, t)], T.sem["lo%s%d" % (kind, t)], pid, rid, topo.mask(core, way[k + 1]))
                        sent.append(("lo%s%d" % (kind, t), len(topo.engines(core, way[k + 1]))))
    for sem, n in sent:
        g.wait_ge(T.sem[sem], n)


def rank_program(g, core, T, topo):
    rank = T.rank_of(core)
    if rank is None:
        _hand_on(g, core, T, topo)
        return

    Q = {"v": g.vector, "s": g.scalar, "t": g.tensor, "g": g, "y": g.sync}
    SEM = {"v": "sv", "s": "sa", "t": "st", "g": "sg"}
    total, hist, clk, known, cache = {}, {}, {}, {k: {} for k in "vstgy"}, {}
    ndma = [0]

    def B(name, *idx):
        key = (name, idx)
        if key not in cache:
            full = (slice(None),) + tuple(slice(*i) if isinstance(i, tuple) else i for i in idx)
            m = np.zeros(BUF[name][1][1:], bool)
            m[tuple(full[1:])] = True
            if name in AT:
                phys, at, w = AT[name]
                lo, hi, st = (tuple(idx[0]) + (1,))[:3] if idx else (0, w, 1)
                ap = T[phys][:, at + lo:at + hi:st] if st > 1 else T[phys][:, at + lo:at + hi]
            else:
                ap = T["z_" + name][full]
            cache[key] = (ap, name, int.from_bytes(np.packbits(m.ravel(), bitorder="little").tobytes(), "little"))
        return cache[key]

    def deps(q, reads, writes):
        need = {}

        def want(rec):
            need[rec[2]] = max(need.get(rec[2], 0), rec[3])
        for wr, lst in ((False, reads), (True, writes)):
            for ap, name, m in lst:
                ps = BUF[name][0] == "psum"
                for rec in hist.get(name, ()):
                    same = rec[4] == q
                    if ps and not same:
                        want(rec)
                    elif rec[0] & m:
                        if rec[1] and not (ps and q == "t" and same):
                            want(rec)
                        elif wr and not rec[1] and not same:
                            want(rec)
        return need

    def wait(q, need):
        kn = known[q]
        todo = {s: v for s, v in need.items() if kn.get(s, 0) < v}
        for s, v in todo.items():
            if any(o != s and clk[(o, w)].get(s, 0) >= v for o, w in todo.items()):
                continue
            if kn.get(s, 0) >= v:
                continue
            Q[q].wait_ge(T.sem[s], v)
            for k2, v2 in clk[(s, v)].items():
                kn[k2] = max(kn.get(k2, 0), v2)
            kn[s] = max(kn.get(s, 0), v)

    def record(q, reads, writes, sem, val, who=None):
        clk[(sem, val)] = dict(known[q])
        who = who or q
        for ap, name, m in writes:
            hist[name] = [r for r in hist.get(name, []) if r[0] & ~m] + [(m, True, sem, val, who)]
        for ap, name, m in reads:
            hist[name] = [r for r in hist.get(name, []) if r[1] or r[4] != who or r[0] & ~m] + [(m, False, sem, val, who)]

    def op(q, fn, out, *ins):
        wait(q, deps(q, ins, (out,)))
        sem = SEM[q]
        total[sem] = total.get(sem, 0) + 1
        fn().then_inc(T.sem[sem], 1)
        record(q, ins, (out,), sem, total[sem])

    def dma(q, out, in_, reads, writes):
        wait(q, deps(q, reads, writes))
        sem = "dma%d" % ndma[0]
        ndma[0] += 1
        total[sem] = 16
        Q[q].dma_start(out, in_).then_inc(T.sem[sem], 16)
        record(q, reads, writes, sem, 16, sem)

    def arrived(kind, t):
        r = (rank + 1 + t) % N
        sem, name = "in%s%d" % (kind, t), _copy(kind, t)
        ps = _pieces(T, topo, r, t, kind)
        n = sum(len(topo.engines(way[-2], core) if len(way) > 1 else es) for way, es, lo, hi in ps)
        if n:
            total[sem] = n
            clk[(sem, n)] = {}
            hist.setdefault(name, []).append((B(name, (ps[0][2], ps[-1][3]))[2], True, sem, n, sem))

    def send(kind, t):
        ps = _pieces(T, topo, rank, t, kind)
        name, at = ("pt" if t else "pti", 0) if kind == "p" else ("x", PAD)
        src = B(name, (at + ps[0][2], at + ps[-1][3]))
        wait("g", deps("g", (src,), ()))
        trs, n = [], 0
        for way, es, lo, hi in ps:
            rid, pid = topo.addr(way[0], core)
            trs.append(RemoteDMATransfer(dst_ids=[DstId(rid=rid, pnc=pid)], dma_engine_mask=_mask(es),
                                         remote_sem=T.sem["in%s%d" % (kind, t)],
                                         src=B(name, (at + lo, at + hi))[0], dst=T["z_" + _copy(kind, t)][:, lo:hi]))
            n += len(es)
        sem = "lo%s%d" % (kind, t)
        g.remote_dma_fused(trs, local_sem=T.sem[sem])
        total[sem] = n
        record("g", (src,), (), sem, n, sem)

    vec, act, pe = g.vector, g.scalar, g.tensor

    def cp(out, in_):
        op("v", lambda: vec.tensor_copy(out[0], in_[0]), out, in_)

    def tt(out, a, b, o):
        op("v", lambda: vec.tensor_tensor(out[0], a[0], b[0], o), out, a, b)

    def ts(out, a, s1, o1, s2=None, o2=None):
        cols = [s for s in (s1, s2) if isinstance(s, tuple)]
        x1 = s1[0] if isinstance(s1, tuple) else s1
        x2 = s2[0] if isinstance(s2, tuple) else s2
        if o2 is None:
            op("v", lambda: vec.tensor_scalar(out[0], a[0], x1, None, o1), out, a, *cols)
        else:
            op("v", lambda: vec.tensor_scalar(out[0], a[0], x1, x2, o1, o2), out, a, *cols)

    def scan(out, d0, d1, o1, o2):
        op("v", lambda: vec.tensor_tensor_scan(out[0], d0[0], d1[0], 0.0, o1, o2), out, d0, d1)

    def gat(out, win, off):
        op("v", lambda: vec.tensor_copy(out[0], win[0].indirect(off[0])), out, win, off)

    def gat_tt(out, win, off, b, o):
        op("v", lambda: vec.tensor_tensor(out[0], win[0].indirect(off[0]), b[0], o), out, win, off, b)

    def scat(win, off, in_):
        op("v", lambda: vec.tensor_copy(win[0].indirect(off[0]), in_[0]), win, off, in_)

    def scat_add(win, off, a, b):
        op("v", lambda: vec.tensor_tensor(win[0].indirect(off[0]), a[0], b[0], A.add), win, off, a, b)

    def fill(out, c):
        op("v", lambda: vec.memset(out[0], c), out)

    def ac(out, in_, f, bias=0.0, scale=1.0):
        cols = [s for s in (bias, scale) if isinstance(s, tuple)]
        b = bias[0] if isinstance(bias, tuple) else bias
        s = scale[0] if isinstance(scale, tuple) else scale
        op("s", lambda: act.activation(out[0], in_[0], f, bias=b, scale=s), out, in_, *cols)

    def agat(out, win, off, bias=0.0, scale=1.0):
        op("s", lambda: act.activation(out[0], win[0].indirect(off[0]), AF.Identity, bias=bias, scale=scale), out, win, off)

    def mm(out, l, r, start, stop):
        op("t", lambda: pe.matmul(out[0], l[0], r[0], start, stop), out, l, r)

    def mms(out, *terms):
        for i, (l, r) in enumerate(terms):
            mm(out, B(l), r, i == 0, i == len(terms) - 1)

    def iota(out, pattern, base=0, mult=0):
        if BUF[out[1]][2] == "int32":
            op("g", lambda: g.iota(out[0], pattern, base, mult), out)
        else:
            op("g", lambda: g.iota(out[0], pattern, base, mult, allow_small_or_imprecise_dtypes=True), out)

    def pick(out, in_, pattern, cmp, fill_, base, mult):
        op("g", lambda: g.affine_select(out[0], in_[0], pattern, cmp, fill_, base, mult), out, in_)

    def rows8(b, *idx):
        full = (slice(0, 8),) + tuple(slice(*i) for i in idx)
        return (T["z_" + b][full], b, B(b, *idx)[2])

    def lm(m, name="zl"):
        return B(name, (15 - m, 143 - m))

    lists = B("pt", (LP, LP + V))
    AND, SHR = A.bitwise_and, A.arith_shift_right
    e128, i128 = B("ef", (0, 128)), B("it", (0, 128))
    par = B("b1", (256, 272))
    xwin = B("x", (PAD, TRX))
    u0, u1 = B("uf", (0, 16)), B("uf", (16, 32))
    m0, m1 = B("moh", (0, 16), 0), B("moh", (0, 16), 1)
    k0, k1 = B("b0", (0, 256)), B("b1", (0, 256))
    best0, best1 = B("sc", (15, 256, 16)), B("sc", (271, 512, 16))
    h = B("h")

    def qrep(q, lo, hi):
        for i in range(lo, hi):
            if q == "v":
                cp(B("qrep", (i, 3072, 16)), B("q", (64, 256)))
            elif q == "g":
                pick(B("qrep", (i, 3072, 16)), B("q", (64, 256)), [[0, 192]], A.is_ge, 0.0, 0, 0)
            else:
                ac(B("qrep", (i, 3072, 16)), B("q", (64, 256)), AF.Copy)

    def zero(bank):
        mm(B(bank), B("nil", (0, 128)), B("nil"), True, False)

    def minus(bank, l, qs):
        for i in range(16):
            mm(B(bank, (i, 512, 16)), l, qs, False, False)

    def parity(last):
        for m in range(16):
            mm(par, lm(m, "zw"), B("q", (m, 256, 16)), last and m == 0, m == 15)

    def towns(step):
        if step == 0:
            cp(B("bi"), par)
        elif step == 1:
            ts(B("bq"), B("bi"), 1, AND)
        elif step == 2:
            tt(B("t16"), B("bq"), B("dmo"), A.mult)
            tt(u0, B("bq"), B("j2"), A.add)
        elif step == 3:
            tt(u1, B("t16"), m0, A.add)
        else:
            cp(B("uu"), B("uf"))

    def first_lists():
        for lo, hi in ((0, 4), (16, 32), (4, 16)):
            gat(B("li", (16 * lo, 16 * hi)), lists, B("uu", (lo, hi)))

    dma("s", T.z_moi[0:8, :], T.mo[:], (), (B("moi"),))
    dma("y", B("pti", (LP, LP + V))[0], T.towns[:], (), (B("pti", (LP, LP + V)),))
    dma("s", B("pti", (LP - 1, LP))[0], T.th[:], (), (B("pti", (LP - 1, LP)),))
    dma("y", B("q")[0], T.qs[:], (), (B("q"),))
    dma("y", B("x", (PAD, PAD + H))[0], T.x[:], (), (B("x", (PAD, PAD + H)),))
    iota(B("pc"), [[1, 1]], 0, 1)
    iota(B("ef"), [[1, 144]])
    fill(B("one"), 1.0)
    pick(B("id"), B("one"), [[-1, 128]], A.is_equal, 0.0, 0, 1)
    iota(B("nt"), [[1, 8], [0, 16]])
    iota(B("it"), [[0, 16], [1, 16]])
    iota(B("ci"), [[0, 4], [1, 16]], 1)
    ts(B("pmi"), B("pc"), 15, AND)
    ts(B("pgi"), B("pc"), 4, SHR)
    ts(B("podd"), B("pc"), 1, AND)
    cp(B("pm"), B("pmi"))
    ts(B("pz"), B("pgi"), 16.0, A.mult, 15.0, A.add)
    ts(B("evc"), B("podd"), -1.0 / 32, A.mult, 1.0 / 32, A.add)
    cp(B("pg"), B("pgi"))
    ts(B("zl"), B("ef"), B("pz"), A.is_equal, 32.0, A.mult)
    ts(B("j2"), B("ef", (0, 16)), 16.0, A.mult, B("pm"), A.add)
    cp(B("pf"), B("pc"))
    ts(B("zw"), B("zl"), B("evc"), A.mult)
    cp(B("jb"), B("j2"))
    ts(B("j2"), B("j2"), 2.0, A.mult)
    ac(B("nid"), B("id"), AF.Copy, scale=-1.0)
    ac(B("zn"), B("zl"), AF.Copy, scale=-1.0)
    ac(B("z2"), B("zl"), AF.Copy, scale=2.0)
    ac(B("rj"), B("jb"), AF.Identity, bias=511.0, scale=-1.0)
    ac(B("trx"), B("pm"), AF.Identity, bias=16.0 * (TRX - PAD - Z), scale=16.0)
    ac(B("trc"), B("pm"), AF.Identity, bias=float(TRX))
    ac(B("trph"), B("jb"), AF.Identity, bias=float(TRP))
    ac(B("trpm"), B("jb"), AF.Identity, bias=float(TRP - 1024))
    ac(B("idk"), B("id"), AF.Copy, scale=-1024.0)
    ts(B("c1"), B("pc"), 16.0, A.mult, 15.0, A.add)
    ts(B("c2"), B("podd"), -2.0, A.mult, 1.0, A.add)
    ts(B("c3"), B("pmi"), 16.0, A.mult, float(CAP), A.add)
    ts(B("pidx"), B("pmi"), 1.0, A.add)
    ts(B("widx"), B("pmi"), -1.0, A.mult, 31.0, A.add)
    ts(B("z8"), B("ef"), B("c1"), A.is_equal)
    tt(B("c2"), B("c2"), B("pf"), A.add)
    ts(B("bo"), B("nt"), B("pg"), A.is_equal)
    ac(B("nbo"), B("bo"), AF.Copy, scale=-1.0)
    ts(B("e8"), B("nt"), B("pf"), A.is_equal)
    fill(B("x", (0, PAD)), 0.0)
    fill(B("x", (PAD + H, TRX)), 0.0)
    fill(B("nil"), 0.0)
    ts(B("sw"), e128, B("c2"), A.is_equal)
    ts(B("oh", (0, 16)), B("ef", (0, 16)), B("pidx"), A.is_equal)
    ts(B("oh", (16, 32)), B("ef", (16, 32)), B("widx"), A.is_equal)
    for out in (B("expl"), B("exp2", (0, 32, 2)), B("exp2", (1, 32, 2))):
        cp(out, B("ef", (0, 16)))
    fill(B("zz"), 0.0)
    fill(B("cs"), 0.0)
    iota(B("da", (0, 256)), [[0, 256]], 2)
    send("p", 0)
    pick(B("resn"), B("nil", (0, 256)), [[0, 16], [1, 16]], A.is_gt, BIG, 0, 0)
    qrep("g", QV0, QV0 + QG)
    for kind in KINDS[0][1:]:
        send(kind, 0)
    pick(B("resx"), B("da", (0, 256)), [[0, 16], [1, 16]], A.is_gt, -BIG, 0, 0)
    pick(B("ntri"), B("nbo"), [[1, 128]], A.is_gt, 0.0, 0, -1)
    ac(B("plw", (256, 512)), B("nil", (0, 256)), AF.Copy)
    ac(B("plw", (CAP, 256)), B("nil", (CAP, 256)), AF.Identity, bias=-float(PAD + Z))
    ac(B("pt", (0, LP - 1)), B("nil", (0, LP - 1)), AF.Copy)
    ac(B("trx1"), B("trx"), AF.Identity, bias=256.0)
    ac(B("trc1"), B("trc"), AF.Identity, bias=16.0)
    for name, c in (("idp", 1024.0), ("idq", -2048.0), ("kp", 128.0), ("kn", -128.0)):
        ac(B(name), B("id"), AF.Copy, scale=c)
    qrep("s", QV0 + QG, 16)
    cp(rows8("mo8"), rows8("moi"))
    for m in range(16):
        mm(B("b7", (0, 32)), rows8("z8", (15 - m, 143 - m)), rows8("mo8", (0, 16), (2 * m, 2 * m + 2)), m == 0, m == 15)
    parity(True)
    mm(B("b4"), rows8("e8"), rows8("mo8"), True, True)
    fill(B("dg", (0, CAP)), 0.0)
    ts(B("um"), B("nt", (0, 64)), 256.0, A.mult, B("c3"), A.add)
    ts(B("trib"), B("it"), B("pm"), A.is_ge, 1024.0, A.mult)
    tt(B("pcg"), B("um"), B("it", (0, 64)), A.add)
    cp(B("pt", (LP - 1, LP + V)), B("pti", (LP - 1, LP + V)))
    cp(B("moh"), B("b7", (0, 32)))
    ts(B("th32"), B("pti", (LP - 1, LP)), 32.0, A.mult)
    ts(B("dm"), B("it", (0, 64)), B("pm"), A.is_equal)
    tt(B("dmo"), m1, m0, A.subtract)
    qrep("v", 0, QV0 - 2)
    towns(0)
    ts(B("sg"), i128, B("pm"), A.is_equal)
    towns(1)
    qrep("v", QV0 - 2, QV0 - 1)
    towns(2)
    towns(3)
    qrep("v", QV0 - 1, QV0)
    towns(4)
    ts(B("thb"), B("th32"), MID, A.add)
    first_lists()

    def mothers():
        for m in range(16):
            mm(B("b4", (0, 16), (2 * m, 2 * m + 2)), B("bm", m), B("moh"), True, True)

    for t in range(R_):
        end = t == R_ - 1
        xr, pr = "xr%d" % t, "pr%d" % t

        def diff(k, half=None):
            lo, n = (64 * k, 64) if half is None else (64 * k + 32 * half, 32)
            r = 16 * (lo % 256 - 64)
            gat_tt(B("d", (16 * lo, 16 * (lo + n))), xwin, B("li", (lo, lo + n)), B("qrep", (r, r + 16 * n)), A.subtract)

        def absd(k, half=None):
            lo, n = (64 * k, 64) if half is None else (64 * k + 32 * half, 32)
            ac(B("ad", (lo // 16, (lo + n) // 16)), B("d", (16 * lo, 16 * (lo + n))), AF.Abs)

        def rows(k, parts=(0, 1)):
            for n in range(4 * k + 2 * parts[0], 4 * k + 2 * parts[-1] + 2):
                r = 256 * (n % 16 - 4)
                gat_tt(B("dr", n), xwin, B("li", (16 * n, 16 * n + 16)), B("qrep", (r, r + 256)), A.subtract)

        def relu(k, parts=(0, 1)):
            r = (4 * k + 2 * parts[0], 4 * k + 2 * parts[-1] + 2)
            ts(B("ad", r), B("dr", r), 0.0, A.max)

        def raw(k):
            agat(B("d", (1024 * k, 1024 * k + 1024)), xwin, B("li", (64 * k, 64 * k + 64)))

        def raw_q(k):
            for a, bank in enumerate(RAW[k]):
                r = (2 * k + a) % 8
                if r < 2:
                    zero(bank)
                    minus(bank, B("nid"), B("q", (32 * r, 32 * r + 32)))
                else:
                    mm(B(bank), B("nid"), B("qrep", (512 * r - 1024, 512 * r - 512)), True, False)

        def raw_x(k):
            for a, bank in enumerate(RAW[k]):
                mm(B(bank), B("id"), B("d", (1024 * k + 512 * a, 1024 * k + 512 * a + 512)), False, True)

        def raw_abs(k):
            for a, bank in enumerate(RAW[k]):
                ac(B("ad", (4 * k + 2 * a, 4 * k + 2 * a + 2)), B(bank), AF.Abs)

        def reduce(k, part=None):
            out = B("b%d" % (k // 4), (64 * (k % 4), 64 * (k % 4) + 64))
            if part != 1:
                mm(out, B("id"), B("ci"), True, False)
            for m in range(16):
                src = B("dr", (4 * k, 4 * k + 4), (16 * m, 16 * m + 16)) if part == 0 else B("ad", (4 * k, 4 * k + 4), m)
                mm(out, lm(m, {None: "zl", 0: "zn", 1: "z2"}[part]), src, False, part != 0 and m == 15)

        wide = 2 if end else 1
        left = list(range(16 // wide - 1, -1, -1))

        def records(count=1):
            for n in [left.pop(0) for _ in range(min(count, len(left)))]:
                scat(B("x"), B("xoff", (2 * n, 2 * n + wide)), B("rn", (16 * wide * n, 16 * wide * (n + 1))))

        pick(B("pk", (0, CAP)), B("plw", (256, 256 + CAP)), [[0, CAP]], A.is_gt, 0.25, 0, 0)
        iota(B("plw", (0, CAP)), [[1, CAP]], H - Z + CAP * t)
        if t == 0:
            pick(B("resa"), B("one", (0, 64)), [[0, 4], [1, 16]], A.is_gt, 0.0, 0, 0)
            iota(B("flw", (0, CAP)), [[0, CAP]])
            iota(B("flw", (CAP, CAP + 1024)), [[0, 1024]], -2)
            iota(B("fw", (CAP, 512)), [[0, 512 - CAP]])
            iota(B("gw", (CAP, 512)), [[0, 512 - CAP]])
            for m in range(16):
                pick(B("bm", m), B("one"), [[-16, 8], [0, 16]], A.is_equal, 0.0, -m, 1)
        raw_q(0)
        raw_q(4)
        if t == 1:
            pick(B("res2"), B("nil"), [[0, 16], [1, 32]], A.is_gt, BIG, 0, 0)
            mothers()
        raw(0)
        raw_x(0)
        rows(7)
        reduce(7, 0)
        raw(4)
        diff(1)
        raw_x(4)
        relu(7)
        reduce(7, 1)
        raw_abs(0)
        reduce(0)
        absd(1)
        reduce(1)
        diff(2)
        raw_abs(4)
        reduce(4)
        for k in (2, 3, 5):
            if k > 2:
                diff(k)
            if k == 5:
                agat(B("lic", (0, 256)), lists, B("uu", (0, 16)), bias=-Z / 32, scale=1.0 / 32)
            absd(k)
            reduce(k)
        for half in range(2):
            diff(6, half)
            absd(6, half)
        scan(B("sc", (0, 256)), B("resn"), k0, A.max, A.min)
        scan(B("sc", (512, 768)), B("resx"), k0, A.add, A.max)
        ts(B("f0"), best0, B("th32"), A.is_ge)
        ts(B("kc", (0, 16)), best0, B("th32"), A.min)
        mms(B("b6", (48, 64)), ("sw", u1), ("nid", u1))
        mm(B("b6", (64, 80)), B("sw"), B("f0"), True, True)
        reduce(6)
        ts(B("thl"), B("f0"), -MID, A.mult, B("thb"), A.add)
        agat(B("lic", (256, 512)), lists, B("uu", (16, 32)), bias=-Z / 32, scale=1.0 / 32)
        if not end:
            ac(B("mw"), B("b4"), AF.Copy)
        ac(B("qf"), B("q"), AF.Copy, scale=1.0 / 2048)
        agat(B("u2f"), B("mw"), B("uu", (16, 32)))
        ts(B("ke", (0, 16)), B("kc", (0, 16)), 31, AND)
        ts(B("thq", (16, 32)), B("f0"), B("th32"), A.mult)
        cp(B("eu", (0, 16)), B("ke", (0, 16)))
        tt(B("xk"), B("b6", (64, 80)), B("f0"), A.mult)
        gat_tt(B("ns", (0, 256)), B("oh"), B("eu", (0, 16)), B("lic", (0, 256)), A.mult)
        scan(B("sc", (256, 512)), B("resn"), k1, A.max, A.min)
        tt(B("dl"), B("b6", (48, 64)), B("xk"), A.mult)
        tt(h, best1, B("thl"), A.is_lt)
        tt(B("kc", (16, 32)), best1, B("thq", (16, 32)), A.min)
        scan(B("cs", (1, 17)), h, B("zz"), A.add, A.add)
        tt(B("hj"), h, B("rj"), A.mult)
        ts(B("ke", (16, 32)), B("kc", (16, 32)), 31, AND)
        tt(B("d1"), B("dl"), B("bq"), A.mult)
        off = B("b6", (16, 32))
        mms(off, ("id", B("jb")), ("ntri", h), ("nbo", B("cs", (0, 16))), ("id", B("hj")))
        mms(B("b5", (256, 272)), ("id", B("trph")), ("idk", B("f0")))
        mms(B("b5", (272, 288)), ("id", B("trpm")), ("idp", h))
        mms(B("b0", (128, 160, 2)), ("id", m0), ("id", B("dl")), ("nid", B("d1")))
        mms(B("b0", (129, 160, 2)), ("id", m1), ("id", B("d1")))
        mms(B("b0", (160, 176)), ("id", B("dmo")), ("id", B("d1")), ("id", B("d1")), ("nid", B("dl")))
        cp(B("eu", (16, 32)), B("ke", (16, 32)))
        cp(B("offu"), off)
        agat(B("plg"), B("plw"), B("offu"), scale=1.0 / 32)
        gat_tt(B("ns", (256, 512)), B("oh"), B("eu", (16, 32)), B("lic", (256, 512)), A.mult)
        scat_add(B("pk"), B("offu"), B("u2f"), B("qf"))
        vp, num, dd = B("b7", (256, 512)), B("b7", (0, 16)), B("b4") if end else B("b5", (0, 256))
        mms(vp, ("bo", B("ns", (0, 256))), ("bo", B("ns", (256, 512))), ("id", B("plg")))
        for bank in ("b3", "b2"):
            zero(bank)
        ac(B("vps"), vp, AF.Copy)
        ac(B("moh"), B("b0", (128, 160)), AF.Copy)
        ac(B("dmo"), B("b0", (160, 176)), AF.Copy)
        for m in range(16):
            mm(num, lm(m), B("vps", (m, 256, 16)), m == 0, m == 15)
        ac(B("numc"), num, AF.Copy, scale=1.0 / 512)
        for a, col in enumerate(("trx", "trx1")[:wide]):
            ac(B("tn", (a, 16, wide)), B("b7", (a, 16, wide)), AF.Identity, bias=B(col), scale=-1.0)
        nex, da, am = (B(n, (0, 256 * wide)) for n in ("nex", "da", "am"))
        agat(nex, B("numc"), B("exp2" if end else "expl"))
        for kind in KINDS[t]:
            arrived(kind, t)
        tt(B("ub"), B("uf"), B("b5", (256, 288)), A.max)
        cp(B("u2i"), B("pk", (0, CAP)))
        tt(B("um"), B("u2i"), B("dm"), A.mult)
        tt(B("qs"), B("pk", (0, CAP)), B("u2i"), A.subtract)
        scan(B("us"), B("resa"), B("um"), A.mult, A.add)
        cp(B("u2u"), B("us", (15, 64, 16)))
        if end:
            mm(dd, B("nil", (0, 128)), B("nil"), True, False)
            mm(B("b4", (0, 16, 2), (16, 32)), B("idk"), B("one"), False, False)
            for a in range(2):
                mm(B("b4", (a, 16, 2), (16 * a, 16 * a + 16)), B("nid"), B("trib", (0, 128)), False, False)
                mm(B("b4", (a, 16, 2)), B("nid"), B("vps"), False, False)
        else:
            mm(dd, B("nid"), B("trib"), True, False)
            mm(dd, B("nid"), B("vps"), False, False)
        minus("b3", B("idq"), B("qs", (32, 64)))
        mm(dd, B("id"), nex, False, True)
        minus("b2", B("idq"), B("qs", (0, 32)))
        gat(B("lig"), B(pr, (LP, LP + V)), B("u2u"))
        xg, g0, g1 = B(xr, (0, H + CAP * t)), B("dg", (CAP, CAP + 512)), B("dg", (CAP + 512, CAP + 1024))
        agat(g1, xg, B("lig", (32, 64)))
        scan(B("sc", (768, 1024)), B("resx"), k1, A.add, A.max)
        ts(B("numu"), num, 1.0 / 16, A.mult, float(PAD + Z), A.add)
        gat(g0, xg, B("lig", (0, 32)))
        mm(B("b3"), B("id"), g1, False, True)
        mm(B("b2"), B("id"), g0, False, True)
        ac(da, dd, AF.Abs, scale=float(2 ** 21))
        if t:
            mothers()
        ac(B("adg", (2, 4)), B("b3"), AF.Abs, scale=64.0)
        ac(B("adg", (0, 2)), B("b2"), AF.Abs, scale=64.0)
        if t and not end:
            ac(B("mw"), B("b4"), AF.Copy)
        gk = B("b6", (256, 320))
        mm(gk, B("id"), B("pcg"), True, False)
        for m in range(16):
            mm(gk, lm(m), B("adg", (0, 4), m), False, m == 15)
        gat_tt(B("sh"), B("x", (0, TRX)), B("numu"), B("q"), A.add)
        scan(am, B("res2" if end else "resn"), da, A.max, A.min)
        cp(B("kc", (32, 64)), B("sc", (527, 1024, 16)))
        tt(B("xo"), B("am", (16 * wide - 1, 256 * wide, 16 * wide)), B("tn"), A.min)
        ts(B("ke", (32, 64)), B("kc", (32, 64)), 31, AND)
        ts(B("rn"), B("sh"), 1, SHR)
        for a, col in enumerate(("trc", "trc1")[:wide]):
            ts(B("xoff", (a, 32 // wide, 2)), B("xo", (a, 16, wide)), -1.0 / 16, A.mult, B(col), A.add)
        cp(B("eu", (32, 64)), B("ke", (32, 64)))
        records()
        ts(B("th2k"), B(pr, (LP - 1, LP)), 2048.0, A.mult)
        records()
        ts(B("thp"), B("jb", (0, 4)), B("th2k"), A.add)
        records(0 if end else 2)
        agat(B("ohw"), B("oh"), B("eu", (32, 64)))
        mms(B("b1"), ("id", B("lic")), ("kn", B("ohw")))
        mm(B("b0"), B("kp"), B("ohw"), True, False)
        for s in range(2):
            mm(B("b0", (256 * s, 256 * s + 256)), B("id"), B("vps"), False, s == 1)
        scan(B("sg2"), B("resn", (0, 64)), gk, A.max, A.min)
        records()
        tt(B("gkc"), B("sg2", (15, 64, 16)), B("thp"), A.min)
        records()
        ts(B("gpos"), B("gkc"), 2047, AND)
        records()
        cp(B("posu"), B("gpos"))
        records()
        gat(B("gw", (0, CAP)), B("dg"), B("posu"))
        agat(B("fw", (0, CAP)), B("flw"), B("posu"))
        agat(B("c"), B("fw"), B("offu"))
        ac(B("t1"), B("b1"), AF.Relu, bias=float(Z), scale=32.0)
        ac(B("t2"), B("b0"), AF.Relu, bias=float(Z - 4096), scale=32.0)
        tr = B("b6", (96, 112))
        mm(tr, B("id"), B("trph"), True, False)
        mm(tr, B("idk"), h, False, False)
        for m in range(16):
            mm(tr, lm(m), B("c", (m, 256, 16)), False, m == 15)
        gcol = B("x", (PAD + H + CAP * t, PAD + H + CAP * t + CAP))
        records(16 if end else 1)
        if not end:
            gat_tt(B("s1"), B("gw"), B("offu"), B("sh"), A.add)
            records()
            ts(B("s2"), B("s1"), 255, AND)
            records()
            cp(B("q"), B("s2"))
            records()
            ts(B("got"), tr, 0.0, A.is_lt)
            mm(par, B("sg"), B("got"), True, False)
            parity(False)
            qrep("s", QV + QG, 16)
            qrep("g", QV, QV + QG)
        else:
            cp(gcol, B("gw", (0, CAP)))
            dma("y", T.yx[:], B("x", (PAD, TRX))[0], (B("x", (PAD, TRX)),), ())
            ac(B("ym2"), B("b4"), AF.Copy)
            dma("y", T.ym[:], T.z_ym2[0:128:16, :], (B("ym2"),), ())
        for s in (1, 0):
            records()
            tt(B("po", (16 * s, 16 * s + 16)), B("ub", (16 * s, 16 * s + 16)), tr, A.max)
        records()
        cp(B("poff"), B("po"))
        records(16)
        if not end:
            send("x", t + 1)
            send("y", t + 1)
        scat_add(B("pt", (LP, LP + V + 256)), B("poff", (16, 32)), B("t1", (256, 512)), B("t2", (256, 512)))
        if not end:
            towns(0)
            cp(gcol, B("gw", (0, CAP)))
            towns(1)
        scat_add(B("pt", (LP, LP + V + 256)), B("poff", (0, 16)), B("t1", (0, 256)), B("t2", (0, 256)))
        if not end:
            send("p", t + 1)
            send("c", t + 1)
            iota(B("x", (0, PAD)), [[0, PAD]])
            towns(2)
            towns(3)
            qrep("v", 0, QV)
            cp(B("uu", (0, 16)), u0)
            cp(B("uu", (16, 32)), u1)
            first_lists()
    dma("s", T.yp[:], lists[0], (lists,), ())
    for s, v in total.items():
        g.wait_ge(T.sem[s], v)
